import numpy as np
import ml_dtypes


def mxq(x, axis, fmt="e4m3"):
    dtype, down = {"e4m3": (ml_dtypes.float8_e4m3fn, 7), "e5m2": (ml_dtypes.float8_e5m2, 14)}[fmt]
    v = np.moveaxis(np.asarray(x, np.float32).astype(ml_dtypes.bfloat16).astype(np.float64), axis, -1)
    blocks = v.reshape(v.shape[:-1] + (-1, 32))
    amax = np.abs(blocks).max(-1, keepdims=True)
    byte = np.maximum(np.where(amax > 0, np.frexp(amax)[1] - 1 + 127, 0) - down, 1)
    scale = np.exp2(byte - 127.0)
    codes = (blocks / scale).astype(np.float32).astype(dtype).astype(np.float64)
    return np.moveaxis((codes * scale).reshape(v.shape), -1, axis)


WIDE = False


def mx_kscale(k):
    if not WIDE:
        return np.ones(k)
    levels = np.array([18, -18])
    if k % 512:
        return np.exp2(np.random.permutation(np.resize(levels, k // 32))).repeat(32)
    a = np.empty((k // 512, 16))
    for p in range(k // 512):
        a[p, :8] = np.random.permutation(np.resize(levels, 8))
        for g in range(8):
            far = levels[np.abs(levels - a[p, g]) >= 10]
            a[p, g + 8] = far[np.random.randint(len(far))]
    return np.exp2(a.ravel()).repeat(32)


def f64(x):
    return np.asarray(x).astype(np.float64)


def striped(idx):
    return np.tile(np.asarray(idx).reshape(-1, 16).T, (8, 1)).astype(np.uint16)


def unstriped(offs):
    return offs[:16].T.reshape(-1).astype(np.int64)

def planes(y):
    n, m = y.shape
    v = y.astype(np.float32).astype(ml_dtypes.bfloat16).astype(np.float64).reshape(n // 32, 32, m)
    top = np.abs(v).max(1)
    byte = np.clip(np.where(top > 0, np.frexp(top)[1] - 1 + 127 - 7, 1), 1, 254)
    codes = (v * np.exp2(127.0 - byte)[:, None, :]).reshape(n, m).astype(np.float32).astype(ml_dtypes.float8_e4m3fn).view(np.uint8)
    words = codes.reshape(n // 512, 128, 4, m).transpose(0, 1, 3, 2)
    return np.ascontiguousarray(words), np.ascontiguousarray(byte.astype(np.uint8).reshape(n // 512, 16, m))


B, N, T, D, DV, R = 1, 512, 2048, 512, 512, 512


def setup_inputs():
    n = np.random.standard_normal
    idx = np.random.permutation(T)[:B * N]
    s = mx_kscale(D)[:, None]
    z = mx_kscale(R)[:, None]
    v = mx_kscale(DV)[:, None]
    q = n((B, D, R))
    do = n((B, DV, R))
    return {
        "qT": (q * s).astype(np.float32),
        "kT": (n((D, T)) * (1.00 / np.sqrt(D)) / s).astype(np.float32),
        "vT": (n((DV, T)) / np.sqrt(DV) / v).astype(np.float32),
        "doT": (do * v).astype(np.float32),
        "rw": (np.random.uniform(0.5, 1.5, (B, R, 1)) * 1.0 / np.sqrt(R) * z).astype(np.float32),
        "qm": (q.transpose(0, 2, 1) / z).astype(np.float32),
        "offs": striped(idx),
    }


def reference(qT, kT, vT, doT, rw, qm, offs):
    idx = unstriped(offs)
    pick = lambda x: x[:, idx].reshape(x.shape[0], B, N).transpose(1, 0, 2)
    a = mxq(f64(qT), 1, "e4m3").transpose(0, 2, 1) @ mxq(pick(f64(kT)), 1, "e4m3")
    p = 1.0 / (1.0 + np.exp(-a))
    dp = mxq(f64(doT), 1, "e5m2").transpose(0, 2, 1) @ mxq(pick(f64(vT)), 1, "e4m3")
    ds = f64(rw) * dp * p * (1.0 - p)
    dk = mxq(f64(qm), 1, "e4m3").transpose(0, 2, 1) @ mxq(ds, 1, "e5m2")
    gk = np.zeros((D, T))
    gk[:, idx] = dk.transpose(1, 0, 2).reshape(D, B * N)
    out_0 = gk
    return (out_0,) + planes(out_0)

@@ -1,0 +1,201 @@
+from contextlib import ExitStack
+
+import concourse.mybir as mybir
+
+N, T, D, R = 512, 2048, 512, 512
+P = 128
+PACK = 4
+FLOPS = 3 * 2 * R * D * N
+
+F32 = mybir.dt.float32
+BF16 = mybir.dt.bfloat16
+I32 = mybir.dt.int32
+U32 = mybir.dt.uint32
+U16 = mybir.dt.uint16
+U8 = mybir.dt.uint8
+E4M3 = mybir.dt.float8_e4m3fn_x4
+E5M2 = mybir.dt.float8_e5m2_x4
+ALU = mybir.AluOpType
+ACT = mybir.ActivationFunctionType
+
+CHUNKS = (256, 512, 512, 256, 256, 256)
+VECTOR_WEAVES = 4
+DS_VECTOR_SLOTS = 384
+
+
+def tile_attend_gat_pl_sig_k_kernel(tc, qT, kT, vT, doT, rw, qm, offs, out_0, out_1, out_2):
+    nc = tc.nc
+
+    with ExitStack() as ctx:
+        sb = ctx.enter_context(tc.tile_pool(name="sb", bufs=1))
+        psum = ctx.enter_context(tc.psum_pool(name="psum", bufs=PACK))
+
+        def rows_of(x):
+            return x.rearrange("(p t) c -> p t c", t=PACK)
+
+        def load(name, src):
+            t = sb.tile(list(src.shape), F32, name=name, align_bytes=64)
+            nc.sync.dma_start(out=t[:], in_=src)
+            return t
+
+        def mx_tiles(name, width):
+            codes = sb.tile([P, width], U32, name=name + "_codes", align_bytes=64)
+            scales = sb.tile([P, width], U8, name=name + "_scales", align_bytes=64)
+            return codes, scales
+
+        def quantize(mx, fmt, c0, c1, grouped):
+            nc.vector.quantize_mx(out=mx[0][:, c0:c1].bitcast(fmt), scales=mx[1][:, c0:c1], in_=grouped)
+
+        def product(out, lhs, lhs_fmt, j, rhs, rhs_fmt):
+            cols = slice(j * P, (j + 1) * P)
+            nc.tensor.matmul_mx(
+                out=out[:],
+                lhsT=lhs[0][:, cols].bitcast(lhs_fmt),
+                lhsT_scale=lhs[1][:, cols],
+                rhs=rhs[0][:].bitcast(rhs_fmt),
+                rhs_scale=rhs[1][:],
+                start=True,
+                stop=True,
+            )
+
+        def deal(dealt, raw, t0=0, j0=0, j1=PACK):
+            nc.scalar.copy(
+                out=dealt[:, j0:j1, :, t0 : t0 + raw.shape[1]].rearrange("p j s t -> p s t j"),
+                in_=raw[:].rearrange("p t (s j) -> p s t j", j=PACK)[:, :, :, j0:j1],
+            )
+
+        def flat(dealt, j):
+            return dealt[:, j, :, :].rearrange("p s t -> p (s t)")
+
+        offsets = sb.tile([P, N // 16], U16, name="offsets")
+        nc.sync.dma_start(offsets[:], offs)
+        q_raw = load("q_raw", rows_of(qT[0]))
+        gate = load("gate", rw[0].rearrange("(s j) o -> s (j o)", j=PACK))
+        k_pool = [load("k_pool%d" % t, rows_of(kT)[:, t, :]) for t in range(PACK)]
+        v_pool = [load("v_pool%d" % t, rows_of(vT)[:, t, :]) for t in range(PACK - 1)]
+        do_raw = [load("do_raw0", rows_of(doT[0])[:, 0:2, :])]
+        v_pool.append(load("v_pool3", rows_of(vT)[:, PACK - 1, :]))
+        do_raw.append(load("do_raw1", rows_of(doT[0])[:, 2:4, :]))
+        qm_raw = load("qm_raw", rows_of(qm[0]))
+
+        windows = [sb.tile([P, T], F32, name="window%d" % j, align_bytes=64) for j in range(PACK)]
+        for w in windows:
+            nc.vector.memset(w[:], 0.0)
+
+        neg_gate = sb.tile([P, PACK], F32, name="neg_gate")
+        nc.vector.tensor_scalar(out=neg_gate[:], in0=gate[:], scalar1=-1.0, scalar2=None, op0=ALU.mult)
+
+        q_dealt = sb.tile([P, PACK, P, PACK], BF16, name="q_dealt", align_bytes=64)
+        deal(q_dealt, q_raw)
+        q_mx = mx_tiles("q", R)
+        quantize(q_mx, E4M3, 0, R, q_dealt[:].rearrange("p j s t -> p (j s t)"))
+
+        k_grouped = sb.tile([P, N, PACK], BF16, name="k_grouped", align_bytes=64)
+        for t in range(PACK):
+            nc.vector.tensor_copy(out=k_grouped[:, :, t], in_=k_pool[t][:].indirect(offsets[:]))
+        k_mx = mx_tiles("k", N)
+        quantize(k_mx, E4M3, 0, N, k_grouped[:].rearrange("p n t -> p (n t)"))
+
+        probs = []
+        for j in range(PACK):
+            score = psum.tile([P, N], F32, name="score", tag="first_last")
+            product(score, q_mx, E4M3, j, k_mx, E4M3)
+            prob = sb.tile([P, N], F32, name="prob%d" % j, align_bytes=64)
+            nc.scalar.activation(out=prob[:], in_=score[:], func=ACT.Sigmoid)
+            probs.append(prob)
+
+        def neg_slope(j):
+            s = sb.tile([P, N], F32, name="slope%d" % j, align_bytes=64)
+            nc.vector.scalar_tensor_tensor(
+                out=s[:], in0=probs[j][:], scalar=1.0, in1=probs[j][:], op0=ALU.subtract, op1=ALU.mult
+            )
+            return s
+
+        v_grouped = sb.tile([P, N, PACK], BF16, name="v_grouped", align_bytes=64)
+        slopes = []
+        for t in range(PACK):
+            nc.vector.tensor_copy(out=v_grouped[:, :, t], in_=v_pool[t][:].indirect(offsets[:]))
+            for j in ((0,), (1,), (2, 3), ())[t]:
+                slopes.append(neg_slope(j))
+        v_mx = mx_tiles("v", N)
+        quantize(v_mx, E4M3, 0, N, v_grouped[:].rearrange("p n t -> p (n t)"))
+
+        do_dealt = sb.tile([P, PACK, P, PACK], BF16, name="do_dealt", align_bytes=64)
+        deal(do_dealt, do_raw[0], 0)
+        deal(do_dealt, do_raw[1], 2, 0, 2)
+        deal(do_dealt, do_raw[1], 2, 2, 4)
+        do_mx = mx_tiles("do", R)
+        ds = sb.tile([P, PACK, N], BF16, name="ds", align_bytes=64)
+        dps = []
+        for j in range(PACK):
+            quantize(do_mx, E5M2, j * P, (j + 1) * P, flat(do_dealt, j))
+            dp = psum.tile([P, N], F32, name="dp", tag="dp")
+            product(dp, do_mx, E5M2, j, v_mx, E4M3)
+            dps.append(dp)
+        for j in range(PACK):
+            nc.vector.scalar_tensor_tensor(
+                out=ds[:, j, :], in0=dps[j][:], scalar=neg_gate[:, j : j + 1], in1=slopes[j][:], op0=ALU.mult, op1=ALU.mult
+            )
+
+        qm_dealt = sb.tile([P, PACK, P, PACK], BF16, name="qm_dealt", align_bytes=64)
+        qm_mx = mx_tiles("qm", D)
+        deal(qm_dealt, qm_raw)
+
+        ds_grouped = sb.tile([P, N, PACK], BF16, name="ds_grouped", align_bytes=64)
+        for copy, c0, c1 in ((nc.vector.tensor_copy, 0, DS_VECTOR_SLOTS), (nc.scalar.copy, DS_VECTOR_SLOTS, N)):
+            copy(
+                out=ds_grouped[:, c0:c1, :].rearrange("p (c i) t -> p c t i", i=4),
+                in_=ds[:, :, c0:c1].rearrange("p t (c i) -> p c t i", i=4),
+            )
+        quantize(qm_mx, E4M3, 0, P, flat(qm_dealt, 0))
+        ds_mx = mx_tiles("ds", N)
+        quantize(ds_mx, E5M2, 0, N, ds_grouped[:].rearrange("p n t -> p (n t)"))
+        for j in range(1, PACK):
+            quantize(qm_mx, E4M3, j * P, (j + 1) * P, flat(qm_dealt, j))
+
+        starts = [sum(CHUNKS[:c]) for c in range(len(CHUNKS))]
+        pairs = [sb.tile([P, 2, w, 2], BF16, name="pairs%d" % c, align_bytes=64) for c, w in enumerate(CHUNKS)]
+
+        def pair_up(copy, j, c):
+            copy(out=pairs[c][:, j // 2, :, j % 2], in_=windows[j][:, starts[c] : starts[c] + CHUNKS[c]])
+
+        dks = []
+        for j in range(PACK):
+            acc = psum.tile([P, N], F32, name="acc", tag="first_last")
+            product(acc, qm_mx, E4M3, j, ds_mx, E5M2)
+            dk = sb.tile([P, N], F32, name="dk%d" % j, align_bytes=64)
+            nc.scalar.copy(out=dk[:], in_=acc[:])
+            dks.append(dk)
+        for j in range(PACK):
+            nc.vector.tensor_copy(out=windows[j][:].indirect(offsets[:]), in_=dks[j][:])
+            nc.sync.dma_start(out=rows_of(out_0)[:, j, :], in_=windows[j][:])
+            for c in range(len(CHUNKS)):
+                if j < 2 or c > 0:
+                    pair_up(nc.scalar.copy, j, c)
+        for j in (2, 3):
+            pair_up(nc.vector.tensor_copy, j, 0)
+
+        out_mx = mx_tiles("out", T)
+        words_out = out_1[0].rearrange("p t l -> p (t l)").bitcast(I32)
+        grouped = [sb.tile([P, w * PACK], BF16, name="out_grouped%d" % c, align_bytes=64) for c, w in enumerate(CHUNKS)]
+
+        def weave(c):
+            copy = nc.vector.tensor_copy if c < VECTOR_WEAVES else nc.scalar.copy
+            copy(
+                out=grouped[c][:].bitcast(F32).rearrange("p (n u) -> p n u", u=2),
+                in_=pairs[c][:].rearrange("p u n e -> p (u n e)").bitcast(F32).rearrange("p (u n) -> p n u", u=2),
+            )
+
+        weave(0)
+        for c, w in enumerate(CHUNKS):
+            if c + 1 < len(CHUNKS):
+                weave(c + 1)
+            c0, c1 = starts[c], starts[c] + w
+            quantize(out_mx, E4M3, c0, c1, grouped[c][:])
+            nc.sync.dma_start(out=words_out[:, c0:c1], in_=out_mx[0][:, c0:c1].bitcast(I32))
+        for quad in range(4):
+            queue = nc.scalar if quad % 2 else nc.sync
+            queue.dma_start(
+                out=out_2[0, 4 * quad : 4 * quad + 4, :].bitcast(I32),
+                in_=out_mx[1][32 * quad : 32 * quad + 4, :].bitcast(I32),
+            )

@@ -20,7 +20,6 @@ ACT = mybir.ActivationFunctionType
 
 CHUNKS = (256, 512, 512, 256, 256, 256)
 VECTOR_WEAVES = 4
-DS_VECTOR_SLOTS = 384
 
 
 def tile_attend_gat_pl_sig_k_kernel(tc, qT, kT, vT, doT, rw, qm, offs, out_0, out_1, out_2):
@@ -60,17 +59,18 @@ def tile_attend_gat_pl_sig_k_kernel(tc, qT, kT, vT, doT, rw, qm, offs, out_0, ou
 
         def deal(dealt, raw, t0=0, j0=0, j1=PACK):
             nc.scalar.copy(
-                out=dealt[:, j0:j1, :, t0 : t0 + raw.shape[1]].rearrange("p j s t -> p s t j"),
-                in_=raw[:].rearrange("p t (s j) -> p s t j", j=PACK)[:, :, :, j0:j1],
+                out=dealt[:, j0:j1, :, t0 : t0 + raw.shape[1]].rearrange("p j s t -> p s j t"),
+                in_=raw[:].rearrange("p t (s j) -> p s j t", j=PACK)[:, :, j0:j1, :],
             )
 
         def flat(dealt, j):
             return dealt[:, j, :, :].rearrange("p s t -> p (s t)")
 
+        q_raw = load("q_raw", rows_of(qT[0]))
         offsets = sb.tile([P, N // 16], U16, name="offsets")
         nc.sync.dma_start(offsets[:], offs)
-        q_raw = load("q_raw", rows_of(qT[0]))
-        gate = load("gate", rw[0].rearrange("(s j) o -> s (j o)", j=PACK))
+        gate = sb.tile([P, PACK], F32, name="gate")
+        nc.scalar.dma_start(out=gate[:], in_=rw[0].rearrange("(s j) o -> s (j o)", j=PACK))
         k_pool = [load("k_pool%d" % t, rows_of(kT)[:, t, :]) for t in range(PACK)]
         v_pool = [load("v_pool%d" % t, rows_of(vT)[:, t, :]) for t in range(PACK - 1)]
         do_raw = [load("do_raw0", rows_of(doT[0])[:, 0:2, :])]
@@ -112,16 +112,21 @@ def tile_attend_gat_pl_sig_k_kernel(tc, qT, kT, vT, doT, rw, qm, offs, out_0, ou
             return s
 
         v_grouped = sb.tile([P, N, PACK], BF16, name="v_grouped", align_bytes=64)
+        v_first = sb.tile([P, 2, N], BF16, name="v_first", align_bytes=64)
         slopes = []
         for t in range(PACK):
-            nc.vector.tensor_copy(out=v_grouped[:, :, t], in_=v_pool[t][:].indirect(offsets[:]))
+            dst = v_first[:, t, :] if t < 2 else v_grouped[:, :, t]
+            nc.vector.tensor_copy(out=dst, in_=v_pool[t][:].indirect(offsets[:]))
+            if t == 1:
+                nc.scalar.copy(out=v_grouped[:, :, 0:2], in_=v_first[:].rearrange("p t n -> p n t"))
             for j in ((0,), (1,), (2, 3), ())[t]:
                 slopes.append(neg_slope(j))
         v_mx = mx_tiles("v", N)
         quantize(v_mx, E4M3, 0, N, v_grouped[:].rearrange("p n t -> p (n t)"))
 
         do_dealt = sb.tile([P, PACK, P, PACK], BF16, name="do_dealt", align_bytes=64)
-        deal(do_dealt, do_raw[0], 0)
+        deal(do_dealt, do_raw[0], 0, 0, 2)
+        deal(do_dealt, do_raw[0], 0, 2, 4)
         deal(do_dealt, do_raw[1], 2, 0, 2)
         deal(do_dealt, do_raw[1], 2, 2, 4)
         do_mx = mx_tiles("do", R)
@@ -142,11 +147,10 @@ def tile_attend_gat_pl_sig_k_kernel(tc, qT, kT, vT, doT, rw, qm, offs, out_0, ou
         deal(qm_dealt, qm_raw)
 
         ds_grouped = sb.tile([P, N, PACK], BF16, name="ds_grouped", align_bytes=64)
-        for copy, c0, c1 in ((nc.vector.tensor_copy, 0, DS_VECTOR_SLOTS), (nc.scalar.copy, DS_VECTOR_SLOTS, N)):
-            copy(
-                out=ds_grouped[:, c0:c1, :].rearrange("p (c i) t -> p c t i", i=4),
-                in_=ds[:, :, c0:c1].rearrange("p t (c i) -> p c t i", i=4),
-            )
+        nc.vector.tensor_copy(
+            out=ds_grouped[:].rearrange("p (c i) t -> p c t i", i=4),
+            in_=ds[:].rearrange("p t (c i) -> p c t i", i=4),
+        )
         quantize(qm_mx, E4M3, 0, P, flat(qm_dealt, 0))
         ds_mx = mx_tiles("ds", N)
         quantize(ds_mx, E5M2, 0, N, ds_grouped[:].rearrange("p n t -> p (n t)"))
@@ -186,6 +190,14 @@ def tile_attend_gat_pl_sig_k_kernel(tc, qT, kT, vT, doT, rw, qm, offs, out_0, ou
                 in_=pairs[c][:].rearrange("p u n e -> p (u n e)").bitcast(F32).rearrange("p (u n) -> p n u", u=2),
             )
 
+        def store_scales(c0, c1):
+            for quad in range(4):
+                queue = nc.scalar if quad % 2 and c1 == T else nc.sync
+                queue.dma_start(
+                    out=out_2[0, 4 * quad : 4 * quad + 4, c0:c1].bitcast(I32),
+                    in_=out_mx[1][32 * quad : 32 * quad + 4, c0:c1].bitcast(I32),
+                )
+
         weave(0)
         for c, w in enumerate(CHUNKS):
             if c + 1 < len(CHUNKS):
@@ -193,9 +205,5 @@ def tile_attend_gat_pl_sig_k_kernel(tc, qT, kT, vT, doT, rw, qm, offs, out_0, ou
             c0, c1 = starts[c], starts[c] + w
             quantize(out_mx, E4M3, c0, c1, grouped[c][:])
             nc.sync.dma_start(out=words_out[:, c0:c1], in_=out_mx[0][:, c0:c1].bitcast(I32))
-        for quad in range(4):
-            queue = nc.scalar if quad % 2 else nc.sync
-            queue.dma_start(
-                out=out_2[0, 4 * quad : 4 * quad + 4, :].bitcast(I32),
-                in_=out_mx[1][32 * quad : 32 * quad + 4, :].bitcast(I32),
-            )
+            if c in (VECTOR_WEAVES - 1, len(CHUNKS) - 1):
+                store_scales(0 if c < VECTOR_WEAVES else starts[VECTOR_WEAVES], c1)

@@ -33,7 +33,7 @@ def tile_attend_gat_pl_sig_k_kernel(tc, qT, kT, vT, doT, rw, qm, offs, out_0, ou
             return x.rearrange("(p t) c -> p t c", t=PACK)
 
         def load(name, src):
-            t = sb.tile(list(src.shape), F32, name=name, align_bytes=64)
+            t = sb.tile(list(src.shape), F32, name=name, tag=name, align_bytes=64)
             nc.sync.dma_start(out=t[:], in_=src)
             return t
 
@@ -57,8 +57,8 @@ def tile_attend_gat_pl_sig_k_kernel(tc, qT, kT, vT, doT, rw, qm, offs, out_0, ou
                 stop=True,
             )
 
-        def deal(dealt, raw, t0=0, j0=0, j1=PACK):
-            nc.scalar.copy(
+        def deal(copy, dealt, raw, t0=0, j0=0, j1=PACK):
+            copy(
                 out=dealt[:, j0:j1, :, t0 : t0 + raw.shape[1]].rearrange("p j s t -> p s j t"),
                 in_=raw[:].rearrange("p t (s j) -> p s j t", j=PACK)[:, :, j0:j1, :],
             )
@@ -72,10 +72,8 @@ def tile_attend_gat_pl_sig_k_kernel(tc, qT, kT, vT, doT, rw, qm, offs, out_0, ou
         gate = sb.tile([P, PACK], F32, name="gate")
         nc.scalar.dma_start(out=gate[:], in_=rw[0].rearrange("(s j) o -> s (j o)", j=PACK))
         k_pool = [load("k_pool%d" % t, rows_of(kT)[:, t, :]) for t in range(PACK)]
-        v_pool = [load("v_pool%d" % t, rows_of(vT)[:, t, :]) for t in range(PACK - 1)]
-        do_raw = [load("do_raw0", rows_of(doT[0])[:, 0:2, :])]
-        v_pool.append(load("v_pool3", rows_of(vT)[:, PACK - 1, :]))
-        do_raw.append(load("do_raw1", rows_of(doT[0])[:, 2:4, :]))
+        v_pool = [load("v_pool%d" % t, rows_of(vT)[:, t, :]) for t in range(PACK)]
+        do_raw = [load("do_raw%d" % u, rows_of(doT[0])[:, 2 * u : 2 * u + 2, :]) for u in range(2)]
         qm_raw = load("qm_raw", rows_of(qm[0]))
 
         windows = [sb.tile([P, T], F32, name="window%d" % j, align_bytes=64) for j in range(PACK)]
@@ -86,7 +84,7 @@ def tile_attend_gat_pl_sig_k_kernel(tc, qT, kT, vT, doT, rw, qm, offs, out_0, ou
         nc.vector.tensor_scalar(out=neg_gate[:], in0=gate[:], scalar1=-1.0, scalar2=None, op0=ALU.mult)
 
         q_dealt = sb.tile([P, PACK, P, PACK], BF16, name="q_dealt", align_bytes=64)
-        deal(q_dealt, q_raw)
+        deal(nc.scalar.copy, q_dealt, q_raw)
         q_mx = mx_tiles("q", R)
         quantize(q_mx, E4M3, 0, R, q_dealt[:].rearrange("p j s t -> p (j s t)"))
 
@@ -104,31 +102,30 @@ def tile_attend_gat_pl_sig_k_kernel(tc, qT, kT, vT, doT, rw, qm, offs, out_0, ou
             nc.scalar.activation(out=prob[:], in_=score[:], func=ACT.Sigmoid)
             probs.append(prob)
 
-        def neg_slope(j):
-            s = sb.tile([P, N], F32, name="slope%d" % j, align_bytes=64)
-            nc.vector.scalar_tensor_tensor(
-                out=s[:], in0=probs[j][:], scalar=1.0, in1=probs[j][:], op0=ALU.subtract, op1=ALU.mult
-            )
-            return s
-
         v_grouped = sb.tile([P, N, PACK], BF16, name="v_grouped", align_bytes=64)
-        v_first = sb.tile([P, 2, N], BF16, name="v_first", align_bytes=64)
+        v_first = sb.tile([P, 2, N], BF16, name="v_first", tag="v_then_do", align_bytes=64)
         slopes = []
         for t in range(PACK):
             dst = v_first[:, t, :] if t < 2 else v_grouped[:, :, t]
             nc.vector.tensor_copy(out=dst, in_=v_pool[t][:].indirect(offsets[:]))
             if t == 1:
                 nc.scalar.copy(out=v_grouped[:, :, 0:2], in_=v_first[:].rearrange("p t n -> p n t"))
-            for j in ((0,), (1,), (2, 3), ())[t]:
-                slopes.append(neg_slope(j))
+            if t < 2:
+                two = sb.tile([P, 2, N], F32, name="slopes%d" % t, tag="v_pool%d" % t, align_bytes=64)
+                for u in range(2):
+                    prob = probs[2 * t + u]
+                    nc.vector.scalar_tensor_tensor(
+                        out=two[:, u, :], in0=prob[:], scalar=1.0, in1=prob[:], op0=ALU.subtract, op1=ALU.mult
+                    )
+                    slopes.append(two[:, u, :])
         v_mx = mx_tiles("v", N)
         quantize(v_mx, E4M3, 0, N, v_grouped[:].rearrange("p n t -> p (n t)"))
 
-        do_dealt = sb.tile([P, PACK, P, PACK], BF16, name="do_dealt", align_bytes=64)
-        deal(do_dealt, do_raw[0], 0, 0, 2)
-        deal(do_dealt, do_raw[0], 0, 2, 4)
-        deal(do_dealt, do_raw[1], 2, 0, 2)
-        deal(do_dealt, do_raw[1], 2, 2, 4)
+        do_dealt = sb.tile([P, PACK, P, PACK], BF16, name="do_dealt", tag="v_then_do", align_bytes=64)
+        deal(nc.scalar.copy, do_dealt, do_raw[0], 0, 0, 2)
+        deal(nc.scalar.copy, do_dealt, do_raw[0], 0, 2, 4)
+        deal(nc.vector.tensor_copy, do_dealt, do_raw[1], 2, 0, 2)
+        deal(nc.scalar.copy, do_dealt, do_raw[1], 2, 2, 4)
         do_mx = mx_tiles("do", R)
         ds = sb.tile([P, PACK, N], BF16, name="ds", align_bytes=64)
         dps = []
@@ -139,12 +136,12 @@ def tile_attend_gat_pl_sig_k_kernel(tc, qT, kT, vT, doT, rw, qm, offs, out_0, ou
             dps.append(dp)
         for j in range(PACK):
             nc.vector.scalar_tensor_tensor(
-                out=ds[:, j, :], in0=dps[j][:], scalar=neg_gate[:, j : j + 1], in1=slopes[j][:], op0=ALU.mult, op1=ALU.mult
+                out=ds[:, j, :], in0=dps[j][:], scalar=neg_gate[:, j : j + 1], in1=slopes[j], op0=ALU.mult, op1=ALU.mult
             )
 
         qm_dealt = sb.tile([P, PACK, P, PACK], BF16, name="qm_dealt", align_bytes=64)
         qm_mx = mx_tiles("qm", D)
-        deal(qm_dealt, qm_raw)
+        deal(nc.scalar.copy, qm_dealt, qm_raw)
 
         ds_grouped = sb.tile([P, N, PACK], BF16, name="ds_grouped", align_bytes=64)
         nc.vector.tensor_copy(
@@ -190,14 +187,6 @@ def tile_attend_gat_pl_sig_k_kernel(tc, qT, kT, vT, doT, rw, qm, offs, out_0, ou
                 in_=pairs[c][:].rearrange("p u n e -> p (u n e)").bitcast(F32).rearrange("p (u n) -> p n u", u=2),
             )
 
-        def store_scales(c0, c1):
-            for quad in range(4):
-                queue = nc.scalar if quad % 2 and c1 == T else nc.sync
-                queue.dma_start(
-                    out=out_2[0, 4 * quad : 4 * quad + 4, c0:c1].bitcast(I32),
-                    in_=out_mx[1][32 * quad : 32 * quad + 4, c0:c1].bitcast(I32),
-                )
-
         weave(0)
         for c, w in enumerate(CHUNKS):
             if c + 1 < len(CHUNKS):
@@ -205,5 +194,9 @@ def tile_attend_gat_pl_sig_k_kernel(tc, qT, kT, vT, doT, rw, qm, offs, out_0, ou
             c0, c1 = starts[c], starts[c] + w
             quantize(out_mx, E4M3, c0, c1, grouped[c][:])
             nc.sync.dma_start(out=words_out[:, c0:c1], in_=out_mx[0][:, c0:c1].bitcast(I32))
-            if c in (VECTOR_WEAVES - 1, len(CHUNKS) - 1):
-                store_scales(0 if c < VECTOR_WEAVES else starts[VECTOR_WEAVES], c1)
+        for quad in range(4):
+            queue = nc.scalar if quad % 2 else nc.sync
+            queue.dma_start(
+                out=out_2[0, 4 * quad : 4 * quad + 4, :].bitcast(I32),
+                in_=out_mx[1][32 * quad : 32 * quad + 4, :].bitcast(I32),
+            )

@@ -4,7 +4,10 @@ import concourse.mybir as mybir
 
 N, T, D, R = 512, 2048, 512, 512
 P = 128
-PACK = 4
+PLACES = 4
+LAST = PLACES - 1
+LIST_ROWS = 16
+QUADRANT = 32
 FLOPS = 3 * 2 * R * D * N
 
 F32 = mybir.dt.float32
@@ -18,7 +21,8 @@ E5M2 = mybir.dt.float8_e5m2_x4
 ALU = mybir.AluOpType
 ACT = mybir.ActivationFunctionType
 
-CHUNKS = (256, 512, 512, 256, 256, 256)
+CHUNKS = (256, 256, 512, 512, 256, 256)
+VECTOR_ROUNDS = 2
 VECTOR_WEAVES = 4
 
 
@@ -27,15 +31,15 @@ def tile_attend_gat_pl_sig_k_kernel(tc, qT, kT, vT, doT, rw, qm, offs, out_0, ou
 
     with ExitStack() as ctx:
         sb = ctx.enter_context(tc.tile_pool(name="sb", bufs=1))
-        psum = ctx.enter_context(tc.psum_pool(name="psum", bufs=PACK))
+        psum = ctx.enter_context(tc.psum_pool(name="psum", bufs=PLACES))
 
-        def rows_of(x):
-            return x.rearrange("(p t) c -> p t c", t=PACK)
+        def planes_of(x):
+            return x.rearrange("(p t) c -> p t c", t=PLACES)
 
         def load(name, src):
-            t = sb.tile(list(src.shape), F32, name=name, tag=name, align_bytes=64)
-            nc.sync.dma_start(out=t[:], in_=src)
-            return t
+            raw = sb.tile(list(src.shape), F32, name=name, tag=name, align_bytes=64)
+            nc.sync.dma_start(out=raw[:], in_=src)
+            return raw
 
         def mx_tiles(name, width):
             codes = sb.tile([P, width], U32, name=name + "_codes", align_bytes=64)
@@ -57,102 +61,120 @@ def tile_attend_gat_pl_sig_k_kernel(tc, qT, kT, vT, doT, rw, qm, offs, out_0, ou
                 stop=True,
             )
 
-        def deal(copy, dealt, raw, t0=0, j0=0, j1=PACK):
+        def deal(copy, dealt, raw, t0=0, j0=0, j1=PLACES):
             copy(
                 out=dealt[:, j0:j1, :, t0 : t0 + raw.shape[1]].rearrange("p j s t -> p s j t"),
-                in_=raw[:].rearrange("p t (s j) -> p s j t", j=PACK)[:, :, j0:j1, :],
+                in_=raw[:].rearrange("p t (s j) -> p s j t", j=PLACES)[:, :, j0:j1, :],
             )
 
-        def flat(dealt, j):
+        def dealt_tile(dealt, j):
             return dealt[:, j, :, :].rearrange("p s t -> p (s t)")
 
-        q_raw = load("q_raw", rows_of(qT[0]))
-        offsets = sb.tile([P, N // 16], U16, name="offsets")
+        halves = (slice(0, N // 2), slice(N // 2, N))
+
+        def gather_last_and_quantize(name, grouped, pool):
+            for cols in halves:
+                part = offsets[:, cols.start // LIST_ROWS : cols.stop // LIST_ROWS]
+                nc.vector.tensor_copy(out=grouped[:, cols, LAST], in_=pool[:].indirect(part))
+            mx = mx_tiles(name, N)
+            for cols in halves:
+                quantize(mx, E4M3, cols.start, cols.stop, grouped[:, cols, :].rearrange("p n t -> p (n t)"))
+            return mx
+
+        q_raw = load("q_raw", planes_of(qT[0]))
+        offsets = sb.tile([P, N // LIST_ROWS], U16, name="offsets")
         nc.sync.dma_start(offsets[:], offs)
-        gate = sb.tile([P, PACK], F32, name="gate")
-        nc.scalar.dma_start(out=gate[:], in_=rw[0].rearrange("(s j) o -> s (j o)", j=PACK))
-        k_pool = [load("k_pool%d" % t, rows_of(kT)[:, t, :]) for t in range(PACK)]
-        v_pool = [load("v_pool%d" % t, rows_of(vT)[:, t, :]) for t in range(PACK)]
-        do_raw = [load("do_raw%d" % u, rows_of(doT[0])[:, 2 * u : 2 * u + 2, :]) for u in range(2)]
-        qm_raw = load("qm_raw", rows_of(qm[0]))
+        gate = sb.tile([P, PLACES], F32, name="gate")
+        nc.scalar.dma_start(out=gate[:], in_=rw[0].rearrange("(s j) o -> s (j o)", j=PLACES))
+        k_pool = [load("k_pool%d" % t, planes_of(kT)[:, t, :]) for t in range(PLACES)]
+        v_pool = [load("v_pool%d" % t, planes_of(vT)[:, t, :]) for t in range(PLACES)]
+        do_raw = [load("do_raw%d" % u, planes_of(doT[0])[:, 2 * u : 2 * u + 2, :]) for u in range(2)]
+        qm_raw = load("qm_raw", planes_of(qm[0]))
 
-        windows = [sb.tile([P, T], F32, name="window%d" % j, align_bytes=64) for j in range(PACK)]
-        for w in windows:
-            nc.vector.memset(w[:], 0.0)
+        windows = [sb.tile([P, T], F32, name="window%d" % j, align_bytes=64) for j in range(PLACES)]
+        for window in windows:
+            nc.vector.memset(window[:], 0.0)
 
-        neg_gate = sb.tile([P, PACK], F32, name="neg_gate")
+        neg_gate = sb.tile([P, PLACES], F32, name="neg_gate")
         nc.vector.tensor_scalar(out=neg_gate[:], in0=gate[:], scalar1=-1.0, scalar2=None, op0=ALU.mult)
 
-        q_dealt = sb.tile([P, PACK, P, PACK], BF16, name="q_dealt", align_bytes=64)
+        q_dealt = sb.tile([P, PLACES, P, PLACES], BF16, name="q_dealt", align_bytes=64)
         deal(nc.scalar.copy, q_dealt, q_raw)
         q_mx = mx_tiles("q", R)
         quantize(q_mx, E4M3, 0, R, q_dealt[:].rearrange("p j s t -> p (j s t)"))
 
-        k_grouped = sb.tile([P, N, PACK], BF16, name="k_grouped", align_bytes=64)
-        for t in range(PACK):
+        k_grouped = sb.tile([P, N, PLACES], BF16, name="k_grouped", align_bytes=64)
+        for t in range(LAST):
             nc.vector.tensor_copy(out=k_grouped[:, :, t], in_=k_pool[t][:].indirect(offsets[:]))
-        k_mx = mx_tiles("k", N)
-        quantize(k_mx, E4M3, 0, N, k_grouped[:].rearrange("p n t -> p (n t)"))
+        k_mx = gather_last_and_quantize("k", k_grouped, k_pool[LAST])
 
         probs = []
-        for j in range(PACK):
+        for j in range(PLACES):
             score = psum.tile([P, N], F32, name="score", tag="first_last")
             product(score, q_mx, E4M3, j, k_mx, E4M3)
             prob = sb.tile([P, N], F32, name="prob%d" % j, align_bytes=64)
             nc.scalar.activation(out=prob[:], in_=score[:], func=ACT.Sigmoid)
             probs.append(prob)
 
-        v_grouped = sb.tile([P, N, PACK], BF16, name="v_grouped", align_bytes=64)
+        v_grouped = sb.tile([P, N, PLACES], BF16, name="v_grouped", align_bytes=64)
         v_first = sb.tile([P, 2, N], BF16, name="v_first", tag="v_then_do", align_bytes=64)
-        slopes = []
-        for t in range(PACK):
+        neg_slopes = []
+        for t in range(LAST):
             dst = v_first[:, t, :] if t < 2 else v_grouped[:, :, t]
             nc.vector.tensor_copy(out=dst, in_=v_pool[t][:].indirect(offsets[:]))
             if t == 1:
                 nc.scalar.copy(out=v_grouped[:, :, 0:2], in_=v_first[:].rearrange("p t n -> p n t"))
             if t < 2:
-                two = sb.tile([P, 2, N], F32, name="slopes%d" % t, tag="v_pool%d" % t, align_bytes=64)
+                two = sb.tile([P, 2, N], F32, name="neg_slopes%d" % t, tag="v_pool%d" % t, align_bytes=64)
                 for u in range(2):
                     prob = probs[2 * t + u]
                     nc.vector.scalar_tensor_tensor(
                         out=two[:, u, :], in0=prob[:], scalar=1.0, in1=prob[:], op0=ALU.subtract, op1=ALU.mult
                     )
-                    slopes.append(two[:, u, :])
-        v_mx = mx_tiles("v", N)
-        quantize(v_mx, E4M3, 0, N, v_grouped[:].rearrange("p n t -> p (n t)"))
+                    neg_slopes.append(two[:, u, :])
+        v_mx = gather_last_and_quantize("v", v_grouped, v_pool[LAST])
 
-        do_dealt = sb.tile([P, PACK, P, PACK], BF16, name="do_dealt", tag="v_then_do", align_bytes=64)
+        do_dealt = sb.tile([P, PLACES, P, PLACES], BF16, name="do_dealt", tag="v_then_do", align_bytes=64)
         deal(nc.scalar.copy, do_dealt, do_raw[0], 0, 0, 2)
         deal(nc.scalar.copy, do_dealt, do_raw[0], 0, 2, 4)
-        deal(nc.vector.tensor_copy, do_dealt, do_raw[1], 2, 0, 2)
+        deal(nc.vector.tensor_copy, do_dealt, do_raw[1], 2, 0, 1)
+        deal(nc.vector.tensor_copy, do_dealt, do_raw[1], 2, 1, 2)
         deal(nc.scalar.copy, do_dealt, do_raw[1], 2, 2, 4)
         do_mx = mx_tiles("do", R)
-        ds = sb.tile([P, PACK, N], BF16, name="ds", align_bytes=64)
+        ds = sb.tile([P, PLACES, N], BF16, name="ds", align_bytes=64)
         dps = []
-        for j in range(PACK):
-            quantize(do_mx, E5M2, j * P, (j + 1) * P, flat(do_dealt, j))
+        for j in range(PLACES):
+            quantize(do_mx, E5M2, j * P, (j + 1) * P, dealt_tile(do_dealt, j))
             dp = psum.tile([P, N], F32, name="dp", tag="dp")
             product(dp, do_mx, E5M2, j, v_mx, E4M3)
             dps.append(dp)
-        for j in range(PACK):
-            nc.vector.scalar_tensor_tensor(
-                out=ds[:, j, :], in0=dps[j][:], scalar=neg_gate[:, j : j + 1], in1=slopes[j], op0=ALU.mult, op1=ALU.mult
-            )
+        for j in range(PLACES):
+            for cols in halves if j == LAST else (slice(0, N),):
+                nc.vector.scalar_tensor_tensor(
+                    out=ds[:, j, cols],
+                    in0=dps[j][:, cols],
+                    scalar=neg_gate[:, j : j + 1],
+                    in1=neg_slopes[j][:, cols],
+                    op0=ALU.mult,
+                    op1=ALU.mult,
+                )
 
-        qm_dealt = sb.tile([P, PACK, P, PACK], BF16, name="qm_dealt", align_bytes=64)
+        qm_dealt = sb.tile([P, PLACES, P, PLACES], BF16, name="qm_dealt", align_bytes=64)
         qm_mx = mx_tiles("qm", D)
-        deal(nc.scalar.copy, qm_dealt, qm_raw)
+        deal(nc.scalar.copy, qm_dealt, qm_raw, 0, 0, 2)
+        deal(nc.scalar.copy, qm_dealt, qm_raw, 0, 2, 4)
 
-        ds_grouped = sb.tile([P, N, PACK], BF16, name="ds_grouped", align_bytes=64)
-        nc.vector.tensor_copy(
-            out=ds_grouped[:].rearrange("p (c i) t -> p c t i", i=4),
-            in_=ds[:].rearrange("p t (c i) -> p c t i", i=4),
-        )
-        quantize(qm_mx, E4M3, 0, P, flat(qm_dealt, 0))
+        ds_grouped = sb.tile([P, N, PLACES], BF16, name="ds_grouped", align_bytes=64)
+        for cols in halves:
+            nc.vector.tensor_copy(
+                out=ds_grouped[:, cols, :].rearrange("p (c i) t -> p c t i", i=2),
+                in_=ds[:, :, cols].rearrange("p t (c i) -> p c t i", i=2),
+            )
+        quantize(qm_mx, E4M3, 0, P, dealt_tile(qm_dealt, 0))
         ds_mx = mx_tiles("ds", N)
         quantize(ds_mx, E5M2, 0, N, ds_grouped[:].rearrange("p n t -> p (n t)"))
-        for j in range(1, PACK):
-            quantize(qm_mx, E4M3, j * P, (j + 1) * P, flat(qm_dealt, j))
+        for j in range(1, PLACES):
+            quantize(qm_mx, E4M3, j * P, (j + 1) * P, dealt_tile(qm_dealt, j))
 
         starts = [sum(CHUNKS[:c]) for c in range(len(CHUNKS))]
         pairs = [sb.tile([P, 2, w, 2], BF16, name="pairs%d" % c, align_bytes=64) for c, w in enumerate(CHUNKS)]
@@ -161,24 +183,27 @@ def tile_attend_gat_pl_sig_k_kernel(tc, qT, kT, vT, doT, rw, qm, offs, out_0, ou
             copy(out=pairs[c][:, j // 2, :, j % 2], in_=windows[j][:, starts[c] : starts[c] + CHUNKS[c]])
 
         dks = []
-        for j in range(PACK):
+        for j in range(PLACES):
             acc = psum.tile([P, N], F32, name="acc", tag="first_last")
             product(acc, qm_mx, E4M3, j, ds_mx, E5M2)
             dk = sb.tile([P, N], F32, name="dk%d" % j, align_bytes=64)
             nc.scalar.copy(out=dk[:], in_=acc[:])
             dks.append(dk)
-        for j in range(PACK):
+        for j in range(PLACES):
             nc.vector.tensor_copy(out=windows[j][:].indirect(offsets[:]), in_=dks[j][:])
-            nc.sync.dma_start(out=rows_of(out_0)[:, j, :], in_=windows[j][:])
-            for c in range(len(CHUNKS)):
-                if j < 2 or c > 0:
+            nc.sync.dma_start(out=planes_of(out_0)[:, j, :], in_=windows[j][:])
+            for c, w in enumerate(CHUNKS):
+                if j < 2 or c >= VECTOR_ROUNDS:
                     pair_up(nc.scalar.copy, j, c)
-        for j in (2, 3):
-            pair_up(nc.vector.tensor_copy, j, 0)
+                elif j == 2:
+                    both = windows[j][:, starts[c] : starts[c] + w].unsqueeze(2).to_broadcast([P, w, 2])
+                    nc.scalar.copy(out=pairs[c][:, 1, :, :], in_=both)
+                else:
+                    pair_up(nc.vector.tensor_copy, j, c)
 
         out_mx = mx_tiles("out", T)
         words_out = out_1[0].rearrange("p t l -> p (t l)").bitcast(I32)
-        grouped = [sb.tile([P, w * PACK], BF16, name="out_grouped%d" % c, align_bytes=64) for c, w in enumerate(CHUNKS)]
+        grouped = [sb.tile([P, w * PLACES], BF16, name="out_grouped%d" % c, align_bytes=64) for c, w in enumerate(CHUNKS)]
 
         def weave(c):
             copy = nc.vector.tensor_copy if c < VECTOR_WEAVES else nc.scalar.copy
@@ -194,9 +219,9 @@ def tile_attend_gat_pl_sig_k_kernel(tc, qT, kT, vT, doT, rw, qm, offs, out_0, ou
             c0, c1 = starts[c], starts[c] + w
             quantize(out_mx, E4M3, c0, c1, grouped[c][:])
             nc.sync.dma_start(out=words_out[:, c0:c1], in_=out_mx[0][:, c0:c1].bitcast(I32))
-        for quad in range(4):
-            queue = nc.scalar if quad % 2 else nc.sync
+        for q in range(P // QUADRANT):
+            queue = nc.scalar if q % 2 else nc.sync
             queue.dma_start(
-                out=out_2[0, 4 * quad : 4 * quad + 4, :].bitcast(I32),
-                in_=out_mx[1][32 * quad : 32 * quad + 4, :].bitcast(I32),
+                out=out_2[0, PLACES * q : PLACES * (q + 1), :].bitcast(I32),
+                in_=out_mx[1][QUADRANT * q : QUADRANT * q + PLACES, :].bitcast(I32),
             )

@@ -6,6 +6,7 @@ N, T, D, R = 512, 2048, 512, 512
 P = 128
 PLACES = 4
 LAST = PLACES - 1
+HALF = N // 2
 LIST_ROWS = 16
 QUADRANT = 32
 FLOPS = 3 * 2 * R * D * N
@@ -24,6 +25,8 @@ ACT = mybir.ActivationFunctionType
 CHUNKS = (256, 256, 512, 512, 256, 256)
 VECTOR_ROUNDS = 2
 VECTOR_WEAVES = 4
+PACK = 2
+SCALAR_TOKENS = 192
 
 
 def tile_attend_gat_pl_sig_k_kernel(tc, qT, kT, vT, doT, rw, qm, offs, out_0, out_1, out_2):
@@ -48,6 +51,9 @@ def tile_attend_gat_pl_sig_k_kernel(tc, qT, kT, vT, doT, rw, qm, offs, out_0, ou
 
         def quantize(mx, fmt, c0, c1, grouped):
             nc.vector.quantize_mx(out=mx[0][:, c0:c1].bitcast(fmt), scales=mx[1][:, c0:c1], in_=grouped)
+
+        def gpsimd_round(out, in_):
+            nc.gpsimd.tensor_scalar(out=out, in0=in_, scalar1=1.0, scalar2=0.0, op0=ALU.mult, op1=ALU.add)
 
         def product(out, lhs, lhs_fmt, j, rhs, rhs_fmt):
             cols = slice(j * P, (j + 1) * P)
@@ -159,22 +165,28 @@ def tile_attend_gat_pl_sig_k_kernel(tc, qT, kT, vT, doT, rw, qm, offs, out_0, ou
                     op1=ALU.mult,
                 )
 
-        qm_dealt = sb.tile([P, PLACES, P, PLACES], BF16, name="qm_dealt", align_bytes=64)
+        qm_dealt = [sb.tile([P, PLACES, P, PLACES], BF16, name="qm_dealt%d" % u, align_bytes=64) for u in range(2)]
         qm_mx = mx_tiles("qm", D)
-        deal(nc.scalar.copy, qm_dealt, qm_raw, 0, 0, 2)
-        deal(nc.scalar.copy, qm_dealt, qm_raw, 0, 2, 4)
+        deal(nc.scalar.copy, qm_dealt[0], qm_raw, 0, 0, 2)
+        deal(gpsimd_round, qm_dealt[1], qm_raw, 0, 2, 4)
 
         ds_grouped = sb.tile([P, N, PLACES], BF16, name="ds_grouped", align_bytes=64)
-        for cols in halves:
-            nc.vector.tensor_copy(
-                out=ds_grouped[:, cols, :].rearrange("p (c i) t -> p c t i", i=2),
-                in_=ds[:, :, cols].rearrange("p t (c i) -> p c t i", i=2),
+
+        def interleave(copy, c0, c1):
+            copy(
+                out=ds_grouped[:, c0:c1, :].rearrange("p (c i) t -> p c t i", i=2),
+                in_=ds[:, :, c0:c1].rearrange("p t (c i) -> p c t i", i=2),
             )
-        quantize(qm_mx, E4M3, 0, P, dealt_tile(qm_dealt, 0))
+
+        interleave(nc.scalar.copy, 0, SCALAR_TOKENS)
+        interleave(nc.vector.tensor_copy, SCALAR_TOKENS, HALF)
+        interleave(nc.vector.tensor_copy, HALF, N)
+        quantize(qm_mx, E4M3, 0, P, dealt_tile(qm_dealt[0], 0))
         ds_mx = mx_tiles("ds", N)
-        quantize(ds_mx, E5M2, 0, N, ds_grouped[:].rearrange("p n t -> p (n t)"))
+        for cols in reversed(halves):
+            quantize(ds_mx, E5M2, cols.start, cols.stop, ds_grouped[:, cols, :].rearrange("p n t -> p (n t)"))
         for j in range(1, PLACES):
-            quantize(qm_mx, E4M3, j * P, (j + 1) * P, dealt_tile(qm_dealt, j))
+            quantize(qm_mx, E4M3, j * P, (j + 1) * P, dealt_tile(qm_dealt[j // 2], j))
 
         starts = [sum(CHUNKS[:c]) for c in range(len(CHUNKS))]
         pairs = [sb.tile([P, 2, w, 2], BF16, name="pairs%d" % c, align_bytes=64) for c, w in enumerate(CHUNKS)]
@@ -201,7 +213,8 @@ def tile_attend_gat_pl_sig_k_kernel(tc, qT, kT, vT, doT, rw, qm, offs, out_0, ou
                 else:
                     pair_up(nc.vector.tensor_copy, j, c)
 
-        out_mx = mx_tiles("out", T)
+        out_codes = sb.tile([P, T], U32, name="out_codes", align_bytes=64)
+        out_scales = sb.tile([P, T // PACK], U8, name="out_scales", align_bytes=64)
         words_out = out_1[0].rearrange("p t l -> p (t l)").bitcast(I32)
         grouped = [sb.tile([P, w * PLACES], BF16, name="out_grouped%d" % c, align_bytes=64) for c, w in enumerate(CHUNKS)]
 
@@ -217,11 +230,16 @@ def tile_attend_gat_pl_sig_k_kernel(tc, qT, kT, vT, doT, rw, qm, offs, out_0, ou
             if c + 1 < len(CHUNKS):
                 weave(c + 1)
             c0, c1 = starts[c], starts[c] + w
-            quantize(out_mx, E4M3, c0, c1, grouped[c][:])
-            nc.sync.dma_start(out=words_out[:, c0:c1], in_=out_mx[0][:, c0:c1].bitcast(I32))
+            quarter, b0 = divmod(c0, T // PACK)
+            nc.vector.quantize_mx(
+                out=out_codes[:, c0:c1].bitcast(E4M3),
+                scales=out_scales[PLACES * quarter : P, b0 : b0 + w],
+                in_=grouped[c][:],
+            )
+            nc.sync.dma_start(out=words_out[:, c0:c1], in_=out_codes[:, c0:c1].bitcast(I32))
         for q in range(P // QUADRANT):
             queue = nc.scalar if q % 2 else nc.sync
             queue.dma_start(
-                out=out_2[0, PLACES * q : PLACES * (q + 1), :].bitcast(I32),
-                in_=out_mx[1][QUADRANT * q : QUADRANT * q + PLACES, :].bitcast(I32),
+                out=out_2[0, PLACES * q : PLACES * (q + 1), :].bitcast(I32).rearrange("r (a c) -> a r c", a=PACK),
+                in_=out_scales[QUADRANT * q : QUADRANT * q + PLACES * PACK, :].bitcast(I32),
             )

@@ -23,8 +23,7 @@ ALU = mybir.AluOpType
 ACT = mybir.ActivationFunctionType
 
 CHUNKS = (256, 256, 512, 512, 256, 256)
-VECTOR_ROUNDS = 2
-VECTOR_WEAVES = 4
+VECTOR_CHUNKS = (0, 1, 3)
 PACK = 2
 SCALAR_TOKENS = 192
 
@@ -189,10 +188,14 @@ def tile_attend_gat_pl_sig_k_kernel(tc, qT, kT, vT, doT, rw, qm, offs, out_0, ou
             quantize(qm_mx, E4M3, j * P, (j + 1) * P, dealt_tile(qm_dealt[j // 2], j))
 
         starts = [sum(CHUNKS[:c]) for c in range(len(CHUNKS))]
-        pairs = [sb.tile([P, 2, w, 2], BF16, name="pairs%d" % c, align_bytes=64) for c, w in enumerate(CHUNKS)]
+        grouped = [sb.tile([P, w, PLACES], BF16, name="out_grouped%d" % c, align_bytes=64) for c, w in enumerate(CHUNKS)]
 
-        def pair_up(copy, j, c):
-            copy(out=pairs[c][:, j // 2, :, j % 2], in_=windows[j][:, starts[c] : starts[c] + CHUNKS[c]])
+        def place(copy, j, c):
+            src = windows[j][:, starts[c] : starts[c] + CHUNKS[c]]
+            if j == 2:
+                copy(out=grouped[c][:, :, 2:4], in_=src.unsqueeze(2).to_broadcast([P, CHUNKS[c], 2]))
+            else:
+                copy(out=grouped[c][:, :, j], in_=src)
 
         dks = []
         for j in range(PLACES):
@@ -204,41 +207,31 @@ def tile_attend_gat_pl_sig_k_kernel(tc, qT, kT, vT, doT, rw, qm, offs, out_0, ou
         for j in range(PLACES):
             nc.vector.tensor_copy(out=windows[j][:].indirect(offsets[:]), in_=dks[j][:])
             nc.sync.dma_start(out=planes_of(out_0)[:, j, :], in_=windows[j][:])
-            for c, w in enumerate(CHUNKS):
-                if j < 2 or c >= VECTOR_ROUNDS:
-                    pair_up(nc.scalar.copy, j, c)
-                elif j == 2:
-                    both = windows[j][:, starts[c] : starts[c] + w].unsqueeze(2).to_broadcast([P, w, 2])
-                    nc.scalar.copy(out=pairs[c][:, 1, :, :], in_=both)
-                else:
-                    pair_up(nc.vector.tensor_copy, j, c)
+            if j < LAST:
+                for c in range(len(CHUNKS)):
+                    place(nc.scalar.copy if c in VECTOR_CHUNKS else gpsimd_round, j, c)
+        for c in range(len(CHUNKS)):
+            if c not in VECTOR_CHUNKS:
+                place(nc.scalar.copy, LAST, c)
 
         out_codes = sb.tile([P, T], U32, name="out_codes", align_bytes=64)
         out_scales = sb.tile([P, T // PACK], U8, name="out_scales", align_bytes=64)
         words_out = out_1[0].rearrange("p t l -> p (t l)").bitcast(I32)
-        grouped = [sb.tile([P, w * PLACES], BF16, name="out_grouped%d" % c, align_bytes=64) for c, w in enumerate(CHUNKS)]
-
-        def weave(c):
-            copy = nc.vector.tensor_copy if c < VECTOR_WEAVES else nc.scalar.copy
-            copy(
-                out=grouped[c][:].bitcast(F32).rearrange("p (n u) -> p n u", u=2),
-                in_=pairs[c][:].rearrange("p u n e -> p (u n e)").bitcast(F32).rearrange("p (u n) -> p n u", u=2),
-            )
-
-        weave(0)
+        to_place = list(VECTOR_CHUNKS)
+        place(nc.vector.tensor_copy, LAST, to_place[0])
         for c, w in enumerate(CHUNKS):
-            if c + 1 < len(CHUNKS):
-                weave(c + 1)
+            if c + 1 < len(to_place):
+                place(nc.vector.tensor_copy, LAST, to_place[c + 1])
             c0, c1 = starts[c], starts[c] + w
             quarter, b0 = divmod(c0, T // PACK)
             nc.vector.quantize_mx(
                 out=out_codes[:, c0:c1].bitcast(E4M3),
                 scales=out_scales[PLACES * quarter : P, b0 : b0 + w],
-                in_=grouped[c][:],
+                in_=grouped[c][:].rearrange("p n t -> p (n t)"),
             )
             nc.sync.dma_start(out=words_out[:, c0:c1], in_=out_codes[:, c0:c1].bitcast(I32))
         for q in range(P // QUADRANT):
-            queue = nc.scalar if q % 2 else nc.sync
+            queue = nc.sync
             queue.dma_start(
                 out=out_2[0, PLACES * q : PLACES * (q + 1), :].bitcast(I32).rearrange("r (a c) -> a r c", a=PACK),
                 in_=out_scales[QUADRANT * q : QUADRANT * q + PLACES * PACK, :].bitcast(I32),

@@ -24,6 +24,8 @@ ACT = mybir.ActivationFunctionType
 
 CHUNKS = (256, 256, 512, 512, 256, 256)
 VECTOR_CHUNKS = (0, 1, 3)
+VECTOR_PIECE = 320
+STORE_AFTER = (1, 2, 3, 4, 5)
 PACK = 2
 SCALAR_TOKENS = 192
 
@@ -190,12 +192,13 @@ def tile_attend_gat_pl_sig_k_kernel(tc, qT, kT, vT, doT, rw, qm, offs, out_0, ou
         starts = [sum(CHUNKS[:c]) for c in range(len(CHUNKS))]
         grouped = [sb.tile([P, w, PLACES], BF16, name="out_grouped%d" % c, align_bytes=64) for c, w in enumerate(CHUNKS)]
 
-        def place(copy, j, c):
-            src = windows[j][:, starts[c] : starts[c] + CHUNKS[c]]
+        def place(copy, j, c, w0=0, w1=None):
+            w1 = CHUNKS[c] if w1 is None else w1
+            src = windows[j][:, starts[c] + w0 : starts[c] + w1]
             if j == 2:
-                copy(out=grouped[c][:, :, 2:4], in_=src.unsqueeze(2).to_broadcast([P, CHUNKS[c], 2]))
+                copy(out=grouped[c][:, w0:w1, 2:4], in_=src.unsqueeze(2).to_broadcast([P, w1 - w0, 2]))
             else:
-                copy(out=grouped[c][:, :, j], in_=src)
+                copy(out=grouped[c][:, w0:w1, j], in_=src)
 
         dks = []
         for j in range(PLACES):
@@ -206,22 +209,26 @@ def tile_attend_gat_pl_sig_k_kernel(tc, qT, kT, vT, doT, rw, qm, offs, out_0, ou
             dks.append(dk)
         for j in range(PLACES):
             nc.vector.tensor_copy(out=windows[j][:].indirect(offsets[:]), in_=dks[j][:])
-            nc.sync.dma_start(out=planes_of(out_0)[:, j, :], in_=windows[j][:])
+            queue = nc.scalar if j in (1, 2) else nc.sync
+            queue.dma_start(out=planes_of(out_0)[:, j, :], in_=windows[j][:])
             if j < LAST:
                 for c in range(len(CHUNKS)):
                     place(nc.scalar.copy if c in VECTOR_CHUNKS else gpsimd_round, j, c)
         for c in range(len(CHUNKS)):
             if c not in VECTOR_CHUNKS:
                 place(nc.scalar.copy, LAST, c)
+            elif CHUNKS[c] > VECTOR_PIECE:
+                place(nc.scalar.copy, LAST, c, VECTOR_PIECE)
 
         out_codes = sb.tile([P, T], U32, name="out_codes", align_bytes=64)
         out_scales = sb.tile([P, T // PACK], U8, name="out_scales", align_bytes=64)
         words_out = out_1[0].rearrange("p t l -> p (t l)").bitcast(I32)
         to_place = list(VECTOR_CHUNKS)
+        stored = 0
         place(nc.vector.tensor_copy, LAST, to_place[0])
         for c, w in enumerate(CHUNKS):
             if c + 1 < len(to_place):
-                place(nc.vector.tensor_copy, LAST, to_place[c + 1])
+                place(nc.vector.tensor_copy, LAST, to_place[c + 1], 0, min(VECTOR_PIECE, CHUNKS[to_place[c + 1]]))
             c0, c1 = starts[c], starts[c] + w
             quarter, b0 = divmod(c0, T // PACK)
             nc.vector.quantize_mx(
@@ -229,9 +236,11 @@ def tile_attend_gat_pl_sig_k_kernel(tc, qT, kT, vT, doT, rw, qm, offs, out_0, ou
                 scales=out_scales[PLACES * quarter : P, b0 : b0 + w],
                 in_=grouped[c][:].rearrange("p n t -> p (n t)"),
             )
-            nc.sync.dma_start(out=words_out[:, c0:c1], in_=out_codes[:, c0:c1].bitcast(I32))
+            if c in STORE_AFTER:
+                nc.sync.dma_start(out=words_out[:, stored:c1], in_=out_codes[:, stored:c1].bitcast(I32))
+                stored = c1
         for q in range(P // QUADRANT):
-            queue = nc.sync
+            queue = nc.scalar if q % 2 else nc.sync
             queue.dma_start(
                 out=out_2[0, PLACES * q : PLACES * (q + 1), :].bitcast(I32).rearrange("r (a c) -> a r c", a=PACK),
                 in_=out_scales[QUADRANT * q : QUADRANT * q + PLACES * PACK, :].bitcast(I32),

@@ -23,11 +23,9 @@ ALU = mybir.AluOpType
 ACT = mybir.ActivationFunctionType
 
 CHUNKS = (256, 256, 512, 512, 256, 256)
-VECTOR_CHUNKS = (0, 1, 3)
+SCALAR_CHUNKS = (0, 1, 3)
 VECTOR_PIECE = 320
-STORE_AFTER = (1, 2, 3, 4, 5)
-PACK = 2
-SCALAR_TOKENS = 192
+SCALE_BANDS = 2
 
 
 def tile_attend_gat_pl_sig_k_kernel(tc, qT, kT, vT, doT, rw, qm, offs, out_0, out_1, out_2):
@@ -56,14 +54,14 @@ def tile_attend_gat_pl_sig_k_kernel(tc, qT, kT, vT, doT, rw, qm, offs, out_0, ou
         def gpsimd_round(out, in_):
             nc.gpsimd.tensor_scalar(out=out, in0=in_, scalar1=1.0, scalar2=0.0, op0=ALU.mult, op1=ALU.add)
 
-        def product(out, lhs, lhs_fmt, j, rhs, rhs_fmt):
+        def product(out, lhs, lhs_fmt, j, rhs, rhs_fmt, c0=0):
             cols = slice(j * P, (j + 1) * P)
             nc.tensor.matmul_mx(
                 out=out[:],
                 lhsT=lhs[0][:, cols].bitcast(lhs_fmt),
                 lhsT_scale=lhs[1][:, cols],
-                rhs=rhs[0][:].bitcast(rhs_fmt),
-                rhs_scale=rhs[1][:],
+                rhs=rhs[0][:, c0 : c0 + N].bitcast(rhs_fmt),
+                rhs_scale=rhs[1][:, c0 : c0 + N],
                 start=True,
                 stop=True,
             )
@@ -77,12 +75,14 @@ def tile_attend_gat_pl_sig_k_kernel(tc, qT, kT, vT, doT, rw, qm, offs, out_0, ou
         def dealt_tile(dealt, j):
             return dealt[:, j, :, :].rearrange("p s t -> p (s t)")
 
-        halves = (slice(0, N // 2), slice(N // 2, N))
+        halves = (slice(0, HALF), slice(HALF, N))
+
+        def entries(cols):
+            return offsets[:, cols.start // LIST_ROWS : cols.stop // LIST_ROWS]
 
         def gather_last_and_quantize(name, grouped, pool):
             for cols in halves:
-                part = offsets[:, cols.start // LIST_ROWS : cols.stop // LIST_ROWS]
-                nc.vector.tensor_copy(out=grouped[:, cols, LAST], in_=pool[:].indirect(part))
+                nc.vector.tensor_copy(out=grouped[:, cols, LAST], in_=pool[:].indirect(entries(cols)))
             mx = mx_tiles(name, N)
             for cols in halves:
                 quantize(mx, E4M3, cols.start, cols.stop, grouped[:, cols, :].rearrange("p n t -> p (n t)"))
@@ -101,6 +101,10 @@ def tile_attend_gat_pl_sig_k_kernel(tc, qT, kT, vT, doT, rw, qm, offs, out_0, ou
         windows = [sb.tile([P, T], F32, name="window%d" % j, align_bytes=64) for j in range(PLACES)]
         for window in windows:
             nc.vector.memset(window[:], 0.0)
+
+        ds_mx = mx_tiles("ds", HALF + N)
+        nc.gpsimd.memset(ds_mx[0][:, 0:HALF], 0)
+        nc.gpsimd.memset(ds_mx[1][:, 0:HALF], 0)
 
         neg_gate = sb.tile([P, PLACES], F32, name="neg_gate")
         nc.vector.tensor_scalar(out=neg_gate[:], in0=gate[:], scalar1=-1.0, scalar2=None, op0=ALU.mult)
@@ -166,10 +170,10 @@ def tile_attend_gat_pl_sig_k_kernel(tc, qT, kT, vT, doT, rw, qm, offs, out_0, ou
                     op1=ALU.mult,
                 )
 
-        qm_dealt = [sb.tile([P, PLACES, P, PLACES], BF16, name="qm_dealt%d" % u, align_bytes=64) for u in range(2)]
+        qm_dealt = sb.tile([P, PLACES, P, PLACES], BF16, name="qm_dealt", align_bytes=64)
         qm_mx = mx_tiles("qm", D)
-        deal(nc.scalar.copy, qm_dealt[0], qm_raw, 0, 0, 2)
-        deal(gpsimd_round, qm_dealt[1], qm_raw, 0, 2, 4)
+        deal(nc.scalar.copy, qm_dealt, qm_raw, 0, 0, 2)
+        deal(gpsimd_round, qm_dealt, qm_raw, 0, 2, 4)
 
         ds_grouped = sb.tile([P, N, PLACES], BF16, name="ds_grouped", align_bytes=64)
 
@@ -179,69 +183,82 @@ def tile_attend_gat_pl_sig_k_kernel(tc, qT, kT, vT, doT, rw, qm, offs, out_0, ou
                 in_=ds[:, :, c0:c1].rearrange("p t (c i) -> p c t i", i=2),
             )
 
-        interleave(nc.scalar.copy, 0, SCALAR_TOKENS)
-        interleave(nc.vector.tensor_copy, SCALAR_TOKENS, HALF)
+        def quantize_ds(cols):
+            grouped = ds_grouped[:, cols, :].rearrange("p n t -> p (n t)")
+            quantize(ds_mx, E5M2, HALF + cols.start, HALF + cols.stop, grouped)
+
+        def quantize_qm(j):
+            quantize(qm_mx, E4M3, j * P, (j + 1) * P, dealt_tile(qm_dealt, j))
+
+        interleave(nc.scalar.copy, 0, HALF // 2)
+        interleave(nc.vector.tensor_copy, HALF // 2, HALF)
+        quantize_qm(0)
+        quantize_ds(halves[0])
+        early = psum.tile([P, N], F32, name="early", tag="first_last")
+        product(early, qm_mx, E4M3, 0, ds_mx, E5M2)
+        dk_early = sb.tile([P, HALF], F32, name="dk_early", align_bytes=64)
+        nc.scalar.copy(out=dk_early[:], in_=early[:, HALF:N])
         interleave(nc.vector.tensor_copy, HALF, N)
-        quantize(qm_mx, E4M3, 0, P, dealt_tile(qm_dealt[0], 0))
-        ds_mx = mx_tiles("ds", N)
-        for cols in reversed(halves):
-            quantize(ds_mx, E5M2, cols.start, cols.stop, ds_grouped[:, cols, :].rearrange("p n t -> p (n t)"))
-        for j in range(1, PLACES):
-            quantize(qm_mx, E4M3, j * P, (j + 1) * P, dealt_tile(qm_dealt[j // 2], j))
+        quantize_qm(1)
+        quantize_ds(halves[1])
+        nc.vector.tensor_copy(out=windows[0][:].indirect(entries(halves[0])), in_=dk_early[:])
+        for j in range(2, PLACES):
+            quantize_qm(j)
+
+        left = [halves[1]] + [slice(0, N)] * LAST
+        dks = []
+        for j in range(PLACES):
+            acc = psum.tile([P, N], F32, name="acc", tag="first_last")
+            product(acc, qm_mx, E4M3, j, ds_mx, E5M2, HALF)
+            dk = sb.tile([P, left[j].stop - left[j].start], F32, name="dk%d" % j, align_bytes=64)
+            nc.scalar.copy(out=dk[:], in_=acc[:, left[j]])
+            dks.append(dk)
 
         starts = [sum(CHUNKS[:c]) for c in range(len(CHUNKS))]
         grouped = [sb.tile([P, w, PLACES], BF16, name="out_grouped%d" % c, align_bytes=64) for c, w in enumerate(CHUNKS)]
 
-        def place(copy, j, c, w0=0, w1=None):
-            w1 = CHUNKS[c] if w1 is None else w1
+        def place(copy, j, c, w0, w1):
             src = windows[j][:, starts[c] + w0 : starts[c] + w1]
-            if j == 2:
-                copy(out=grouped[c][:, w0:w1, 2:4], in_=src.unsqueeze(2).to_broadcast([P, w1 - w0, 2]))
+            if j == LAST - 1:
+                copy(out=grouped[c][:, w0:w1, j:PLACES], in_=src.unsqueeze(2).to_broadcast([P, w1 - w0, 2]))
             else:
                 copy(out=grouped[c][:, w0:w1, j], in_=src)
 
-        dks = []
         for j in range(PLACES):
-            acc = psum.tile([P, N], F32, name="acc", tag="first_last")
-            product(acc, qm_mx, E4M3, j, ds_mx, E5M2)
-            dk = sb.tile([P, N], F32, name="dk%d" % j, align_bytes=64)
-            nc.scalar.copy(out=dk[:], in_=acc[:])
-            dks.append(dk)
-        for j in range(PLACES):
-            nc.vector.tensor_copy(out=windows[j][:].indirect(offsets[:]), in_=dks[j][:])
-            queue = nc.scalar if j in (1, 2) else nc.sync
+            nc.vector.tensor_copy(out=windows[j][:].indirect(entries(left[j])), in_=dks[j][:])
+            queue = nc.sync if j in (0, LAST) else nc.scalar
             queue.dma_start(out=planes_of(out_0)[:, j, :], in_=windows[j][:])
             if j < LAST:
-                for c in range(len(CHUNKS)):
-                    place(nc.scalar.copy if c in VECTOR_CHUNKS else gpsimd_round, j, c)
-        for c in range(len(CHUNKS)):
-            if c not in VECTOR_CHUNKS:
-                place(nc.scalar.copy, LAST, c)
-            elif CHUNKS[c] > VECTOR_PIECE:
-                place(nc.scalar.copy, LAST, c, VECTOR_PIECE)
-
-        out_codes = sb.tile([P, T], U32, name="out_codes", align_bytes=64)
-        out_scales = sb.tile([P, T // PACK], U8, name="out_scales", align_bytes=64)
-        words_out = out_1[0].rearrange("p t l -> p (t l)").bitcast(I32)
-        to_place = list(VECTOR_CHUNKS)
-        stored = 0
-        place(nc.vector.tensor_copy, LAST, to_place[0])
+                for c, w in enumerate(CHUNKS):
+                    place(nc.scalar.copy if c in SCALAR_CHUNKS else gpsimd_round, j, c, 0, w)
+        vector_tokens = [min(w, VECTOR_PIECE) if c in SCALAR_CHUNKS else 0 for c, w in enumerate(CHUNKS)]
         for c, w in enumerate(CHUNKS):
-            if c + 1 < len(to_place):
-                place(nc.vector.tensor_copy, LAST, to_place[c + 1], 0, min(VECTOR_PIECE, CHUNKS[to_place[c + 1]]))
+            if vector_tokens[c] < w:
+                place(nc.scalar.copy, LAST, c, vector_tokens[c], w)
+
+        band = T // SCALE_BANDS
+        out_codes = sb.tile([P, T], U32, name="out_codes", align_bytes=64)
+        out_scales = sb.tile([P, band], U8, name="out_scales", align_bytes=64)
+        words_out = out_1[0].rearrange("p t l -> p (t l)").bitcast(I32)
+        place(nc.vector.tensor_copy, LAST, SCALAR_CHUNKS[0], 0, vector_tokens[SCALAR_CHUNKS[0]])
+        stored = 0
+        for c, w in enumerate(CHUNKS):
+            for ahead in SCALAR_CHUNKS[c + 1 : c + 2]:
+                place(nc.vector.tensor_copy, LAST, ahead, 0, vector_tokens[ahead])
             c0, c1 = starts[c], starts[c] + w
-            quarter, b0 = divmod(c0, T // PACK)
+            a, b0 = divmod(c0, band)
             nc.vector.quantize_mx(
                 out=out_codes[:, c0:c1].bitcast(E4M3),
-                scales=out_scales[PLACES * quarter : P, b0 : b0 + w],
+                scales=out_scales[PLACES * a : P, b0 : b0 + w],
                 in_=grouped[c][:].rearrange("p n t -> p (n t)"),
             )
-            if c in STORE_AFTER:
+            if c > 0:
                 nc.sync.dma_start(out=words_out[:, stored:c1], in_=out_codes[:, stored:c1].bitcast(I32))
                 stored = c1
         for q in range(P // QUADRANT):
             queue = nc.scalar if q % 2 else nc.sync
+            rows = out_2[0, PLACES * q : PLACES * (q + 1), :].bitcast(I32)
             queue.dma_start(
-                out=out_2[0, PLACES * q : PLACES * (q + 1), :].bitcast(I32).rearrange("r (a c) -> a r c", a=PACK),
-                in_=out_scales[QUADRANT * q : QUADRANT * q + PLACES * PACK, :].bitcast(I32),
+                out=rows.rearrange("r (a c) -> a r c", a=SCALE_BANDS),
+                in_=out_scales[QUADRANT * q : QUADRANT * q + PLACES * SCALE_BANDS, :].bitcast(I32),
             )

@@ -25,7 +25,8 @@ ACT = mybir.ActivationFunctionType
 CHUNKS = (256, 256, 512, 512, 256, 256)
 SCALAR_CHUNKS = (0, 1, 3)
 VECTOR_PIECE = 320
-SCALE_BANDS = 2
+SCALE_BANDS = 4
+QUANT_TOKENS = T // SCALE_BANDS // 2
 
 
 def tile_attend_gat_pl_sig_k_kernel(tc, qT, kT, vT, doT, rw, qm, offs, out_0, out_1, out_2):
@@ -245,14 +246,16 @@ def tile_attend_gat_pl_sig_k_kernel(tc, qT, kT, vT, doT, rw, qm, offs, out_0, ou
         for c, w in enumerate(CHUNKS):
             for ahead in SCALAR_CHUNKS[c + 1 : c + 2]:
                 place(nc.vector.tensor_copy, LAST, ahead, 0, vector_tokens[ahead])
-            c0, c1 = starts[c], starts[c] + w
-            a, b0 = divmod(c0, band)
-            nc.vector.quantize_mx(
-                out=out_codes[:, c0:c1].bitcast(E4M3),
-                scales=out_scales[PLACES * a : P, b0 : b0 + w],
-                in_=grouped[c][:].rearrange("p n t -> p (n t)"),
-            )
+            for w0 in range(0, w, QUANT_TOKENS):
+                c0 = starts[c] + w0
+                a, b0 = divmod(c0, band)
+                nc.vector.quantize_mx(
+                    out=out_codes[:, c0 : c0 + QUANT_TOKENS].bitcast(E4M3),
+                    scales=out_scales[PLACES * a : P, b0 : b0 + QUANT_TOKENS],
+                    in_=grouped[c][:, w0 : w0 + QUANT_TOKENS, :].rearrange("p n t -> p (n t)"),
+                )
             if c > 0:
+                c1 = starts[c] + w
                 nc.sync.dma_start(out=words_out[:, stored:c1], in_=out_codes[:, stored:c1].bitcast(I32))
                 stored = c1
         for q in range(P // QUADRANT):

@@ -148,7 +148,8 @@ def tile_attend_gat_pl_sig_k_kernel(tc, qT, kT, vT, doT, rw, qm, offs, out_0, ou
 
         do_dealt = sb.tile([P, PLACES, P, PLACES], BF16, name="do_dealt", tag="v_then_do", align_bytes=64)
         deal(nc.scalar.copy, do_dealt, do_raw[0], 0, 0, 2)
-        deal(nc.scalar.copy, do_dealt, do_raw[0], 0, 2, 4)
+        deal(nc.scalar.copy, do_dealt, do_raw[0], 0, 2, 3)
+        deal(gpsimd_round, do_dealt, do_raw[0], 0, 3, 4)
         deal(nc.vector.tensor_copy, do_dealt, do_raw[1], 2, 0, 1)
         deal(nc.vector.tensor_copy, do_dealt, do_raw[1], 2, 1, 2)
         deal(nc.scalar.copy, do_dealt, do_raw[1], 2, 2, 4)

@@ -1,6 +1,7 @@
 from contextlib import ExitStack
 
 import concourse.mybir as mybir
+from concourse.masks import make_identity
 
 N, T, D, R = 512, 2048, 512, 512
 P = 128
@@ -27,6 +28,7 @@ SCALAR_CHUNKS = (0, 1, 3)
 VECTOR_PIECE = 320
 SCALE_BANDS = 4
 QUANT_TOKENS = T // SCALE_BANDS // 2
+DO_VECTOR = 128
 
 
 def tile_attend_gat_pl_sig_k_kernel(tc, qT, kT, vT, doT, rw, qm, offs, out_0, out_1, out_2):
@@ -44,8 +46,8 @@ def tile_attend_gat_pl_sig_k_kernel(tc, qT, kT, vT, doT, rw, qm, offs, out_0, ou
             nc.sync.dma_start(out=raw[:], in_=src)
             return raw
 
-        def mx_tiles(name, width):
-            codes = sb.tile([P, width], U32, name=name + "_codes", align_bytes=64)
+        def mx_tiles(name, width, tag=None):
+            codes = sb.tile([P, width], U32, name=name + "_codes", tag=tag or name + "_codes", align_bytes=64)
             scales = sb.tile([P, width], U8, name=name + "_scales", align_bytes=64)
             return codes, scales
 
@@ -73,6 +75,12 @@ def tile_attend_gat_pl_sig_k_kernel(tc, qT, kT, vT, doT, rw, qm, offs, out_0, ou
                 in_=raw[:].rearrange("p t (s j) -> p s j t", j=PLACES)[:, :, j0:j1, :],
             )
 
+        def deal_rows(copy, dealt, raw, s0, s1):
+            copy(
+                out=dealt[:, :, s0:s1, :].rearrange("p j s t -> p s j t"),
+                in_=raw[:].rearrange("p t (s j) -> p s j t", j=PLACES)[:, s0:s1, :, :],
+            )
+
         def dealt_tile(dealt, j):
             return dealt[:, j, :, :].rearrange("p s t -> p (s t)")
 
@@ -89,6 +97,15 @@ def tile_attend_gat_pl_sig_k_kernel(tc, qT, kT, vT, doT, rw, qm, offs, out_0, ou
                 quantize(mx, E4M3, cols.start, cols.stop, grouped[:, cols, :].rearrange("p n t -> p (n t)"))
             return mx
 
+        def group(copy, grouped, raw, c0, c1, r0=0):
+            copy(
+                out=grouped[:, c0:c1, :].rearrange("p (c i) t -> p c t i", i=PLACES),
+                in_=raw[:, :, c0 - r0 : c1 - r0].rearrange("p t (c i) -> p c t i", i=PLACES),
+            )
+
+        def flat(grouped, c0, c1):
+            return grouped[:, c0:c1, :].rearrange("p n t -> p (n t)")
+
         q_raw = load("q_raw", planes_of(qT[0]))
         offsets = sb.tile([P, N // LIST_ROWS], U16, name="offsets")
         nc.sync.dma_start(offsets[:], offs)
@@ -100,118 +117,133 @@ def tile_attend_gat_pl_sig_k_kernel(tc, qT, kT, vT, doT, rw, qm, offs, out_0, ou
         qm_raw = load("qm_raw", planes_of(qm[0]))
 
         windows = [sb.tile([P, T], F32, name="window%d" % j, align_bytes=64) for j in range(PLACES)]
-        for window in windows:
+        for window in windows[:LAST]:
             nc.vector.memset(window[:], 0.0)
 
         ds_mx = mx_tiles("ds", HALF + N)
         nc.gpsimd.memset(ds_mx[0][:, 0:HALF], 0)
         nc.gpsimd.memset(ds_mx[1][:, 0:HALF], 0)
+        identity = sb.tile([P, P], F32, name="identity", align_bytes=64)
+        make_identity(nc, identity[:])
+        nc.gpsimd.memset(windows[LAST][:], 0.0)
 
-        neg_gate = sb.tile([P, PLACES], F32, name="neg_gate")
-        nc.vector.tensor_scalar(out=neg_gate[:], in0=gate[:], scalar1=-1.0, scalar2=None, op0=ALU.mult)
+        gate_bank = psum.tile([P, PLACES, P], F32, name="gate_bank", tag="second")
+        for j in range(PLACES):
+            nc.tensor.transpose(gate_bank[:, j, :], gate[:, j : j + 1].to_broadcast([P, P]), identity[:])
+        gate_row = sb.tile([P, R], F32, name="gate_row", align_bytes=64)
+        nc.scalar.activation(
+            out=gate_row[:].rearrange("p (s j) -> p s j", j=PLACES),
+            in_=gate_bank[:].rearrange("p j s -> p s j"),
+            func=ACT.Copy,
+            scale=-0.25,
+        )
 
-        q_dealt = sb.tile([P, PLACES, P, PLACES], BF16, name="q_dealt", align_bytes=64)
-        deal(nc.scalar.copy, q_dealt, q_raw)
+        q_grouped = sb.tile([P, R, PLACES], BF16, name="q_grouped", align_bytes=64)
+        group(nc.scalar.copy, q_grouped, q_raw, 0, R)
         q_mx = mx_tiles("q", R)
-        quantize(q_mx, E4M3, 0, R, q_dealt[:].rearrange("p j s t -> p (j s t)"))
+        quantize(q_mx, E4M3, 0, R, flat(q_grouped, 0, R))
 
         k_grouped = sb.tile([P, N, PLACES], BF16, name="k_grouped", align_bytes=64)
         for t in range(LAST):
             nc.vector.tensor_copy(out=k_grouped[:, :, t], in_=k_pool[t][:].indirect(offsets[:]))
         k_mx = gather_last_and_quantize("k", k_grouped, k_pool[LAST])
 
-        probs = []
-        for j in range(PLACES):
-            score = psum.tile([P, N], F32, name="score", tag="first_last")
-            product(score, q_mx, E4M3, j, k_mx, E4M3)
-            prob = sb.tile([P, N], F32, name="prob%d" % j, align_bytes=64)
-            nc.scalar.activation(out=prob[:], in_=score[:], func=ACT.Sigmoid)
-            probs.append(prob)
+        squares = []
+        for c in range(PLACES):
+            score = psum.tile([P, R], F32, name="score", tag="first_last")
+            product(score, k_mx, E4M3, c, q_mx, E4M3)
+            tanh = sb.tile([P, R], F32, name="tanh%d" % c, align_bytes=64)
+            nc.scalar.activation(out=tanh[:], in_=score[:], func=ACT.Tanh, scale=0.5)
+            square = sb.tile([P, R], F32, name="square%d" % c, align_bytes=64)
+            nc.scalar.activation(out=square[:], in_=tanh[:], func=ACT.Square)
+            squares.append(square)
 
         v_grouped = sb.tile([P, N, PLACES], BF16, name="v_grouped", align_bytes=64)
-        v_first = sb.tile([P, 2, N], BF16, name="v_first", tag="v_then_do", align_bytes=64)
-        neg_slopes = []
+        v_first = sb.tile([P, 2, N], BF16, name="v_first", align_bytes=64)
+        slopes = []
+
+        def form_slopes(chunks, tag):
+            some = sb.tile([P, len(chunks), R], F32, name="slopes%d" % chunks[0], tag=tag, align_bytes=64)
+            for u, c in enumerate(chunks):
+                nc.vector.scalar_tensor_tensor(
+                    out=some[:, u, :], in0=squares[c][:], scalar=1.0, in1=gate_row[:], op0=ALU.subtract, op1=ALU.mult
+                )
+            return [some[:, u, :] for u in range(len(chunks))]
+
         for t in range(LAST):
             dst = v_first[:, t, :] if t < 2 else v_grouped[:, :, t]
             nc.vector.tensor_copy(out=dst, in_=v_pool[t][:].indirect(offsets[:]))
             if t == 1:
                 nc.scalar.copy(out=v_grouped[:, :, 0:2], in_=v_first[:].rearrange("p t n -> p n t"))
             if t < 2:
-                two = sb.tile([P, 2, N], F32, name="neg_slopes%d" % t, tag="v_pool%d" % t, align_bytes=64)
-                for u in range(2):
-                    prob = probs[2 * t + u]
-                    nc.vector.scalar_tensor_tensor(
-                        out=two[:, u, :], in0=prob[:], scalar=1.0, in1=prob[:], op0=ALU.subtract, op1=ALU.mult
-                    )
-                    neg_slopes.append(two[:, u, :])
+                slopes.extend(form_slopes(range(t, 2 * t + 1), "v_pool%d" % t))
         v_mx = gather_last_and_quantize("v", v_grouped, v_pool[LAST])
 
-        do_dealt = sb.tile([P, PLACES, P, PLACES], BF16, name="do_dealt", tag="v_then_do", align_bytes=64)
-        deal(nc.scalar.copy, do_dealt, do_raw[0], 0, 0, 2)
-        deal(nc.scalar.copy, do_dealt, do_raw[0], 0, 2, 3)
-        deal(gpsimd_round, do_dealt, do_raw[0], 0, 3, 4)
-        deal(nc.vector.tensor_copy, do_dealt, do_raw[1], 2, 0, 1)
-        deal(nc.vector.tensor_copy, do_dealt, do_raw[1], 2, 1, 2)
-        deal(nc.scalar.copy, do_dealt, do_raw[1], 2, 2, 4)
+        for c in (0, LAST):
+            warm = psum.tile([P, R], F32, name="warm", tag="first_last")
+            product(warm, v_mx, E4M3, c, q_mx, E4M3)
+
+        do_grouped = sb.tile([P, R, PLACES], BF16, name="do_grouped", tag="v_then_do", align_bytes=64)
         do_mx = mx_tiles("do", R)
-        ds = sb.tile([P, PLACES, N], BF16, name="ds", align_bytes=64)
+
+        def place_pair(copy, u, c0, c1):
+            copy(out=do_grouped[:, c0:c1, 2 * u : 2 * u + 2], in_=do_raw[u][:, :, c0:c1].rearrange("p t c -> p c t"))
+
+        place_pair(nc.scalar.copy, 0, 0, HALF)
+        place_pair(nc.scalar.copy, 0, HALF, HALF + DO_VECTOR)
+        place_pair(nc.vector.tensor_copy, 0, HALF + DO_VECTOR, R)
+        place_pair(nc.vector.tensor_copy, 1, 0, HALF)
+        place_pair(nc.vector.tensor_copy, 1, HALF, HALF + DO_VECTOR)
+        place_pair(nc.scalar.copy, 1, HALF + DO_VECTOR, R)
+        quantize(do_mx, E5M2, 0, HALF, flat(do_grouped, 0, HALF))
+        quantize(do_mx, E5M2, HALF, R, flat(do_grouped, HALF, R))
+
+        slopes.extend(form_slopes(range(LAST, PLACES), "v_then_do"))
         dps = []
-        for j in range(PLACES):
-            quantize(do_mx, E5M2, j * P, (j + 1) * P, dealt_tile(do_dealt, j))
-            dp = psum.tile([P, N], F32, name="dp", tag="dp")
-            product(dp, do_mx, E5M2, j, v_mx, E4M3)
+        for c in range(PLACES):
+            dp = psum.tile([P, R], F32, name="dp", tag="second")
+            product(dp, v_mx, E4M3, c, do_mx, E5M2)
             dps.append(dp)
-        for j in range(PLACES):
-            for cols in halves if j == LAST else (slice(0, N),):
-                nc.vector.scalar_tensor_tensor(
-                    out=ds[:, j, cols],
-                    in0=dps[j][:, cols],
-                    scalar=neg_gate[:, j : j + 1],
-                    in1=neg_slopes[j][:, cols],
-                    op0=ALU.mult,
-                    op1=ALU.mult,
-                )
 
         qm_dealt = sb.tile([P, PLACES, P, PLACES], BF16, name="qm_dealt", align_bytes=64)
-        qm_mx = mx_tiles("qm", D)
-        deal(nc.scalar.copy, qm_dealt, qm_raw, 0, 0, 2)
-        deal(gpsimd_round, qm_dealt, qm_raw, 0, 2, 4)
+        deal_rows(nc.scalar.copy, qm_dealt, qm_raw, 0, P // 2)
+        deal_rows(gpsimd_round, qm_dealt, qm_raw, P // 2, P)
 
-        ds_grouped = sb.tile([P, N, PLACES], BF16, name="ds_grouped", align_bytes=64)
-
-        def interleave(copy, c0, c1):
-            copy(
-                out=ds_grouped[:, c0:c1, :].rearrange("p (c i) t -> p c t i", i=2),
-                in_=ds[:, :, c0:c1].rearrange("p t (c i) -> p c t i", i=2),
+        ds_grouped = [sb.tile([P, HALF, PLACES], BF16, name="ds_grouped%d" % h, tag="ds_grouped%d" % h, align_bytes=64) for h in range(2)]
+        for c in range(PLACES):
+            ds = sb.tile([P, R], BF16, name="ds%d" % c, align_bytes=64)
+            nc.vector.tensor_tensor(out=ds[:], in0=dps[c][:], in1=slopes[c], op=ALU.mult)
+            words = ds[:].bitcast(F32)
+            turned = psum.tile([P, 2, P], F32, name="turned", tag="first_last")
+            for u in range(2):
+                nc.tensor.transpose(turned[:, u, :], words[:, u : R // 2 : 2], identity[:])
+            h, s0 = divmod(c * P, HALF)
+            nc.scalar.copy(
+                out=flat(ds_grouped[h], s0, s0 + P).bitcast(F32).rearrange("p (s u) -> p s u", u=2),
+                in_=turned[:].rearrange("p u s -> p s u"),
             )
 
-        def quantize_ds(cols):
-            grouped = ds_grouped[:, cols, :].rearrange("p n t -> p (n t)")
-            quantize(ds_mx, E5M2, HALF + cols.start, HALF + cols.stop, grouped)
+        def quantize_ds(h):
+            quantize(ds_mx, E5M2, HALF + h * HALF, N + h * HALF, flat(ds_grouped[h], 0, HALF))
 
-        def quantize_qm(j):
-            quantize(qm_mx, E4M3, j * P, (j + 1) * P, dealt_tile(qm_dealt, j))
-
-        interleave(nc.scalar.copy, 0, HALF // 2)
-        interleave(nc.vector.tensor_copy, HALF // 2, HALF)
-        quantize_qm(0)
-        quantize_ds(halves[0])
-        early = psum.tile([P, N], F32, name="early", tag="first_last")
-        product(early, qm_mx, E4M3, 0, ds_mx, E5M2)
+        quantize_ds(0)
+        qm_first = mx_tiles("qm_first", P, "v_pool1")
+        qm_rest = mx_tiles("qm_rest", D - P, "ds_grouped0")
+        quantize(qm_first, E4M3, 0, P, dealt_tile(qm_dealt, 0))
+        early = psum.tile([P, N], F32, name="early", tag="second")
+        product(early, qm_first, E4M3, 0, ds_mx, E5M2)
         dk_early = sb.tile([P, HALF], F32, name="dk_early", align_bytes=64)
         nc.scalar.copy(out=dk_early[:], in_=early[:, HALF:N])
-        interleave(nc.vector.tensor_copy, HALF, N)
-        quantize_qm(1)
-        quantize_ds(halves[1])
+        quantize(qm_rest, E4M3, 0, 2 * P, qm_dealt[:, 1:3, :, :].rearrange("p j s t -> p (j s t)"))
+        quantize(qm_rest, E4M3, 2 * P, 3 * P, dealt_tile(qm_dealt, LAST))
+        quantize_ds(1)
         nc.vector.tensor_copy(out=windows[0][:].indirect(entries(halves[0])), in_=dk_early[:])
-        for j in range(2, PLACES):
-            quantize_qm(j)
 
         left = [halves[1]] + [slice(0, N)] * LAST
         dks = []
         for j in range(PLACES):
-            acc = psum.tile([P, N], F32, name="acc", tag="first_last")
-            product(acc, qm_mx, E4M3, j, ds_mx, E5M2, HALF)
+            acc = psum.tile([P, N], F32, name="acc", tag="second")
+            product(acc, qm_rest if j else qm_first, E4M3, max(j - 1, 0), ds_mx, E5M2, HALF)
             dk = sb.tile([P, left[j].stop - left[j].start], F32, name="dk%d" % j, align_bytes=64)
             nc.scalar.copy(out=dk[:], in_=acc[:, left[j]])
             dks.append(dk)

@@ -28,7 +28,7 @@ SCALAR_CHUNKS = (0, 1, 3)
 VECTOR_PIECE = 320
 SCALE_BANDS = 4
 QUANT_TOKENS = T // SCALE_BANDS // 2
-DO_VECTOR = 128
+DO_VECTOR = 96
 
 
 def tile_attend_gat_pl_sig_k_kernel(tc, qT, kT, vT, doT, rw, qm, offs, out_0, out_1, out_2):
@@ -97,12 +97,6 @@ def tile_attend_gat_pl_sig_k_kernel(tc, qT, kT, vT, doT, rw, qm, offs, out_0, ou
                 quantize(mx, E4M3, cols.start, cols.stop, grouped[:, cols, :].rearrange("p n t -> p (n t)"))
             return mx
 
-        def group(copy, grouped, raw, c0, c1, r0=0):
-            copy(
-                out=grouped[:, c0:c1, :].rearrange("p (c i) t -> p c t i", i=PLACES),
-                in_=raw[:, :, c0 - r0 : c1 - r0].rearrange("p t (c i) -> p c t i", i=PLACES),
-            )
-
         def flat(grouped, c0, c1):
             return grouped[:, c0:c1, :].rearrange("p n t -> p (n t)")
 
@@ -132,14 +126,17 @@ def tile_attend_gat_pl_sig_k_kernel(tc, qT, kT, vT, doT, rw, qm, offs, out_0, ou
             nc.tensor.transpose(gate_bank[:, j, :], gate[:, j : j + 1].to_broadcast([P, P]), identity[:])
         gate_row = sb.tile([P, R], F32, name="gate_row", align_bytes=64)
         nc.scalar.activation(
-            out=gate_row[:].rearrange("p (s j) -> p s j", j=PLACES),
-            in_=gate_bank[:].rearrange("p j s -> p s j"),
+            out=gate_row[:].rearrange("p (u s e) -> p u s e", u=2, e=2),
+            in_=gate_bank[:].rearrange("p (u e) s -> p u s e", u=2),
             func=ACT.Copy,
             scale=-0.25,
         )
 
         q_grouped = sb.tile([P, R, PLACES], BF16, name="q_grouped", align_bytes=64)
-        group(nc.scalar.copy, q_grouped, q_raw, 0, R)
+        nc.scalar.copy(
+            out=q_grouped[:].rearrange("p (u s e) t -> p s u t e", u=2, e=2),
+            in_=q_raw[:].rearrange("p t (s u e) -> p s u t e", u=2, e=2),
+        )
         q_mx = mx_tiles("q", R)
         quantize(q_mx, E4M3, 0, R, flat(q_grouped, 0, R))
 
@@ -186,12 +183,17 @@ def tile_attend_gat_pl_sig_k_kernel(tc, qT, kT, vT, doT, rw, qm, offs, out_0, ou
         do_grouped = sb.tile([P, R, PLACES], BF16, name="do_grouped", tag="v_then_do", align_bytes=64)
         do_mx = mx_tiles("do", R)
 
-        def place_pair(copy, u, c0, c1):
-            copy(out=do_grouped[:, c0:c1, 2 * u : 2 * u + 2], in_=do_raw[u][:, :, c0:c1].rearrange("p t c -> p c t"))
+        def place_pair(copy, w, c0, c1):
+            u, s0 = divmod(c0 // 2, P)
+            s1 = s0 + (c1 - c0) // 2
+            copy(
+                out=do_grouped[:, c0:c1, 2 * w : 2 * w + 2].rearrange("p (s e) t -> p s e t", e=2),
+                in_=do_raw[w][:].rearrange("p t (s u e) -> p u s e t", u=2, e=2)[:, u, s0:s1, :, :],
+            )
 
         place_pair(nc.scalar.copy, 0, 0, HALF)
-        place_pair(nc.scalar.copy, 0, HALF, HALF + DO_VECTOR)
-        place_pair(nc.vector.tensor_copy, 0, HALF + DO_VECTOR, R)
+        place_pair(nc.scalar.copy, 0, HALF, HALF + P)
+        place_pair(gpsimd_round, 0, HALF + P, R)
         place_pair(nc.vector.tensor_copy, 1, 0, HALF)
         place_pair(nc.vector.tensor_copy, 1, HALF, HALF + DO_VECTOR)
         place_pair(nc.scalar.copy, 1, HALF + DO_VECTOR, R)
@@ -216,7 +218,7 @@ def tile_attend_gat_pl_sig_k_kernel(tc, qT, kT, vT, doT, rw, qm, offs, out_0, ou
             words = ds[:].bitcast(F32)
             turned = psum.tile([P, 2, P], F32, name="turned", tag="first_last")
             for u in range(2):
-                nc.tensor.transpose(turned[:, u, :], words[:, u : R // 2 : 2], identity[:])
+                nc.tensor.transpose(turned[:, u, :], words[:, u * P : (u + 1) * P], identity[:])
             h, s0 = divmod(c * P, HALF)
             nc.scalar.copy(
                 out=flat(ds_grouped[h], s0, s0 + P).bitcast(F32).rearrange("p (s u) -> p s u", u=2),

@@ -151,7 +151,7 @@ def tile_attend_gat_pl_sig_k_kernel(tc, qT, kT, vT, doT, rw, qm, offs, out_0, ou
             product(score, k_mx, E4M3, c, q_mx, E4M3)
             tanh = sb.tile([P, R], F32, name="tanh%d" % c, align_bytes=64)
             nc.scalar.activation(out=tanh[:], in_=score[:], func=ACT.Tanh, scale=0.5)
-            square = sb.tile([P, R], F32, name="square%d" % c, align_bytes=64)
+            square = sb.tile([P, R], F32, name="square%d" % c, tag="square%d" % c, align_bytes=64)
             nc.scalar.activation(out=square[:], in_=tanh[:], func=ACT.Square)
             squares.append(square)
 
@@ -207,7 +207,7 @@ def tile_attend_gat_pl_sig_k_kernel(tc, qT, kT, vT, doT, rw, qm, offs, out_0, ou
             product(dp, v_mx, E4M3, c, do_mx, E5M2)
             dps.append(dp)
 
-        qm_dealt = sb.tile([P, PLACES, P, PLACES], BF16, name="qm_dealt", align_bytes=64)
+        qm_dealt = sb.tile([P, PLACES, P, PLACES], BF16, name="qm_dealt", tag="square%d" % LAST, align_bytes=64)
         deal_rows(nc.scalar.copy, qm_dealt, qm_raw, 0, P // 2)
         deal_rows(gpsimd_round, qm_dealt, qm_raw, P // 2, P)
 

@@ -29,6 +29,7 @@ VECTOR_PIECE = 320
 SCALE_BANDS = 4
 QUANT_TOKENS = T // SCALE_BANDS // 2
 DO_VECTOR = 96
+SLOPES_BEHIND = ((0,), (1, 2))
 
 
 def tile_attend_gat_pl_sig_k_kernel(tc, qT, kT, vT, doT, rw, qm, offs, out_0, out_1, out_2):
@@ -89,14 +90,6 @@ def tile_attend_gat_pl_sig_k_kernel(tc, qT, kT, vT, doT, rw, qm, offs, out_0, ou
         def entries(cols):
             return offsets[:, cols.start // LIST_ROWS : cols.stop // LIST_ROWS]
 
-        def gather_last_and_quantize(name, grouped, pool):
-            for cols in halves:
-                nc.vector.tensor_copy(out=grouped[:, cols, LAST], in_=pool[:].indirect(entries(cols)))
-            mx = mx_tiles(name, N)
-            for cols in halves:
-                quantize(mx, E4M3, cols.start, cols.stop, grouped[:, cols, :].rearrange("p n t -> p (n t)"))
-            return mx
-
         def flat(grouped, c0, c1):
             return grouped[:, c0:c1, :].rearrange("p n t -> p (n t)")
 
@@ -143,7 +136,10 @@ def tile_attend_gat_pl_sig_k_kernel(tc, qT, kT, vT, doT, rw, qm, offs, out_0, ou
         k_grouped = sb.tile([P, N, PLACES], BF16, name="k_grouped", align_bytes=64)
         for t in range(LAST):
             nc.vector.tensor_copy(out=k_grouped[:, :, t], in_=k_pool[t][:].indirect(offsets[:]))
-        k_mx = gather_last_and_quantize("k", k_grouped, k_pool[LAST])
+        k_mx = mx_tiles("k", N)
+        for cols in halves:
+            nc.vector.tensor_copy(out=k_grouped[:, cols, LAST], in_=k_pool[LAST][:].indirect(entries(cols)))
+            quantize(k_mx, E4M3, cols.start, cols.stop, flat(k_grouped, cols.start, cols.stop))
 
         squares = []
         for c in range(PLACES):
@@ -155,7 +151,7 @@ def tile_attend_gat_pl_sig_k_kernel(tc, qT, kT, vT, doT, rw, qm, offs, out_0, ou
             nc.scalar.activation(out=square[:], in_=tanh[:], func=ACT.Square)
             squares.append(square)
 
-        v_grouped = sb.tile([P, N, PLACES], BF16, name="v_grouped", align_bytes=64)
+        v_grouped = sb.tile([P, N, PLACES], BF16, name="v_grouped", tag="v_grouped", align_bytes=64)
         v_first = sb.tile([P, 2, N], BF16, name="v_first", align_bytes=64)
         slopes = []
 
@@ -173,12 +169,20 @@ def tile_attend_gat_pl_sig_k_kernel(tc, qT, kT, vT, doT, rw, qm, offs, out_0, ou
             if t == 1:
                 nc.scalar.copy(out=v_grouped[:, :, 0:2], in_=v_first[:].rearrange("p t n -> p n t"))
             if t < 2:
-                slopes.extend(form_slopes(range(t, 2 * t + 1), "v_pool%d" % t))
-        v_mx = gather_last_and_quantize("v", v_grouped, v_pool[LAST])
+                slopes.extend(form_slopes(SLOPES_BEHIND[t], "slopes%d" % t))
+        shifted = sb.tile([P, R], F32, name="shifted", tag="square%d" % (LAST - 1), align_bytes=64)
+        nc.gpsimd.tensor_scalar(out=shifted[:], in0=squares[LAST][:], scalar1=1.0, scalar2=-1.0, op0=ALU.mult, op1=ALU.add)
+        last_slope = sb.tile([P, R], F32, name="last_slope", align_bytes=64)
+        nc.gpsimd.tensor_tensor(out=last_slope[:], in0=shifted[:], in1=gate_row[:], op=ALU.mult)
+        slopes.append(last_slope[:])
+        for cols in halves:
+            nc.vector.tensor_copy(out=v_grouped[:, cols, LAST], in_=v_pool[LAST][:].indirect(entries(cols)))
+        v_mx = [mx_tiles("v0", HALF)]
+        quantize(v_mx[0], E4M3, 0, HALF, flat(v_grouped, 0, HALF))
 
-        for c in (0, LAST):
+        for c in range(2):
             warm = psum.tile([P, R], F32, name="warm", tag="first_last")
-            product(warm, v_mx, E4M3, c, q_mx, E4M3)
+            product(warm, v_mx[0], E4M3, c, q_mx, E4M3)
 
         do_grouped = sb.tile([P, R, PLACES], BF16, name="do_grouped", tag="v_then_do", align_bytes=64)
         do_mx = mx_tiles("do", R)
@@ -200,14 +204,15 @@ def tile_attend_gat_pl_sig_k_kernel(tc, qT, kT, vT, doT, rw, qm, offs, out_0, ou
         quantize(do_mx, E5M2, 0, HALF, flat(do_grouped, 0, HALF))
         quantize(do_mx, E5M2, HALF, R, flat(do_grouped, HALF, R))
 
-        slopes.extend(form_slopes(range(LAST, PLACES), "v_then_do"))
+        v_mx.append(mx_tiles("v1", HALF, "v_then_do"))
+        quantize(v_mx[1], E4M3, 0, HALF, flat(v_grouped, HALF, N))
         dps = []
         for c in range(PLACES):
             dp = psum.tile([P, R], F32, name="dp", tag="second")
-            product(dp, v_mx, E4M3, c, do_mx, E5M2)
+            product(dp, v_mx[c // 2], E4M3, c % 2, do_mx, E5M2)
             dps.append(dp)
 
-        qm_dealt = sb.tile([P, PLACES, P, PLACES], BF16, name="qm_dealt", tag="square%d" % LAST, align_bytes=64)
+        qm_dealt = sb.tile([P, PLACES, P, PLACES], BF16, name="qm_dealt", tag="v_grouped", align_bytes=64)
         deal_rows(nc.scalar.copy, qm_dealt, qm_raw, 0, P // 2)
         deal_rows(gpsimd_round, qm_dealt, qm_raw, P // 2, P)
 
@@ -229,7 +234,7 @@ def tile_attend_gat_pl_sig_k_kernel(tc, qT, kT, vT, doT, rw, qm, offs, out_0, ou
             quantize(ds_mx, E5M2, HALF + h * HALF, N + h * HALF, flat(ds_grouped[h], 0, HALF))
 
         quantize_ds(0)
-        qm_first = mx_tiles("qm_first", P, "v_pool1")
+        qm_first = mx_tiles("qm_first", P, "slopes1")
         qm_rest = mx_tiles("qm_rest", D - P, "ds_grouped0")
         quantize(qm_first, E4M3, 0, P, dealt_tile(qm_dealt, 0))
         early = psum.tile([P, N], F32, name="early", tag="second")

@@ -25,10 +25,11 @@ ACT = mybir.ActivationFunctionType
 
 CHUNKS = (256, 256, 512, 512, 256, 256)
 SCALAR_CHUNKS = (0, 1, 3)
-VECTOR_PIECE = 320
+VECTOR_PIECE = 400
+DO_GPSIMD = 192
 SCALE_BANDS = 4
 QUANT_TOKENS = T // SCALE_BANDS // 2
-DO_VECTOR = 96
+DO_VECTOR = 48
 SLOPES_BEHIND = ((0,), (1, 2))
 
 
@@ -196,8 +197,8 @@ def tile_attend_gat_pl_sig_k_kernel(tc, qT, kT, vT, doT, rw, qm, offs, out_0, ou
             )
 
         place_pair(nc.scalar.copy, 0, 0, HALF)
-        place_pair(nc.scalar.copy, 0, HALF, HALF + P)
-        place_pair(gpsimd_round, 0, HALF + P, R)
+        place_pair(nc.scalar.copy, 0, HALF, R - DO_GPSIMD)
+        place_pair(gpsimd_round, 0, R - DO_GPSIMD, R)
         place_pair(nc.vector.tensor_copy, 1, 0, HALF)
         place_pair(nc.vector.tensor_copy, 1, HALF, HALF + DO_VECTOR)
         place_pair(nc.scalar.copy, 1, HALF + DO_VECTOR, R)
@@ -219,7 +220,8 @@ def tile_attend_gat_pl_sig_k_kernel(tc, qT, kT, vT, doT, rw, qm, offs, out_0, ou
         ds_grouped = [sb.tile([P, HALF, PLACES], BF16, name="ds_grouped%d" % h, tag="ds_grouped%d" % h, align_bytes=64) for h in range(2)]
         for c in range(PLACES):
             ds = sb.tile([P, R], BF16, name="ds%d" % c, align_bytes=64)
-            nc.vector.tensor_tensor(out=ds[:], in0=dps[c][:], in1=slopes[c], op=ALU.mult)
+            for cols in halves if c % 2 else (slice(0, R),):
+                nc.vector.tensor_tensor(out=ds[:, cols], in0=dps[c][:, cols], in1=slopes[c][:, cols], op=ALU.mult)
             words = ds[:].bitcast(F32)
             turned = psum.tile([P, 2, P], F32, name="turned", tag="first_last")
             for u in range(2):
@@ -243,7 +245,8 @@ def tile_attend_gat_pl_sig_k_kernel(tc, qT, kT, vT, doT, rw, qm, offs, out_0, ou
         nc.scalar.copy(out=dk_early[:], in_=early[:, HALF:N])
         quantize(qm_rest, E4M3, 0, 2 * P, qm_dealt[:, 1:3, :, :].rearrange("p j s t -> p (j s t)"))
         quantize(qm_rest, E4M3, 2 * P, 3 * P, dealt_tile(qm_dealt, LAST))
-        quantize_ds(1)
+        for s0 in (0, P):
+            quantize(ds_mx, E5M2, N + s0, N + s0 + P, flat(ds_grouped[1], s0, s0 + P))
         nc.vector.tensor_copy(out=windows[0][:].indirect(entries(halves[0])), in_=dk_early[:])
 
         left = [halves[1]] + [slice(0, N)] * LAST
@@ -274,8 +277,9 @@ def tile_attend_gat_pl_sig_k_kernel(tc, qT, kT, vT, doT, rw, qm, offs, out_0, ou
                     place(nc.scalar.copy if c in SCALAR_CHUNKS else gpsimd_round, j, c, 0, w)
         vector_tokens = [min(w, VECTOR_PIECE) if c in SCALAR_CHUNKS else 0 for c, w in enumerate(CHUNKS)]
         for c, w in enumerate(CHUNKS):
-            if vector_tokens[c] < w:
-                place(nc.scalar.copy, LAST, c, vector_tokens[c], w)
+            step = w // 2 if c == len(CHUNKS) - 1 else w
+            for w0 in range(vector_tokens[c], w, step):
+                place(nc.scalar.copy, LAST, c, w0, min(w0 + step, w))
 
         band = T // SCALE_BANDS
         out_codes = sb.tile([P, T], U32, name="out_codes", align_bytes=64)
@@ -286,13 +290,14 @@ def tile_attend_gat_pl_sig_k_kernel(tc, qT, kT, vT, doT, rw, qm, offs, out_0, ou
         for c, w in enumerate(CHUNKS):
             for ahead in SCALAR_CHUNKS[c + 1 : c + 2]:
                 place(nc.vector.tensor_copy, LAST, ahead, 0, vector_tokens[ahead])
-            for w0 in range(0, w, QUANT_TOKENS):
+            step = w // 2 if c == len(CHUNKS) - 1 else QUANT_TOKENS
+            for w0 in range(0, w, step):
                 c0 = starts[c] + w0
                 a, b0 = divmod(c0, band)
                 nc.vector.quantize_mx(
-                    out=out_codes[:, c0 : c0 + QUANT_TOKENS].bitcast(E4M3),
-                    scales=out_scales[PLACES * a : P, b0 : b0 + QUANT_TOKENS],
-                    in_=grouped[c][:, w0 : w0 + QUANT_TOKENS, :].rearrange("p n t -> p (n t)"),
+                    out=out_codes[:, c0 : c0 + step].bitcast(E4M3),
+                    scales=out_scales[PLACES * a : P, b0 : b0 + step],
+                    in_=grouped[c][:, w0 : w0 + step, :].rearrange("p n t -> p (n t)"),
                 )
             if c > 0:
                 c1 = starts[c] + w

@@ -7,9 +7,11 @@ N, T, D, R = 512, 2048, 512, 512
 P = 128
 PLACES = 4
 LAST = PLACES - 1
+BATCHES = N // P
 HALF = N // 2
 LIST_ROWS = 16
 QUADRANT = 32
+WARM_UPS = 2
 FLOPS = 3 * 2 * R * D * N
 
 F32 = mybir.dt.float32
@@ -23,14 +25,16 @@ E5M2 = mybir.dt.float8_e5m2_x4
 ALU = mybir.AluOpType
 ACT = mybir.ActivationFunctionType
 
-CHUNKS = (256, 256, 512, 512, 256, 256)
-SCALAR_CHUNKS = (0, 1, 3)
-VECTOR_PIECE = 400
+SLOPES_BEHIND = ((0,), (1, 2))
 DO_GPSIMD = 192
+DO_VECTOR = 48
+CHUNKS = (256, 256, 512, 512, 256, 256)
+LAST_CHUNK = len(CHUNKS) - 1
+SCALAR_CHUNKS = (0, 1, 3)
+SCALAR_EXTRA = 96
+VECTOR_PIECE = 400
 SCALE_BANDS = 4
 QUANT_TOKENS = T // SCALE_BANDS // 2
-DO_VECTOR = 48
-SLOPES_BEHIND = ((0,), (1, 2))
 
 
 def tile_attend_gat_pl_sig_k_kernel(tc, qT, kT, vT, doT, rw, qm, offs, out_0, out_1, out_2):
@@ -38,7 +42,7 @@ def tile_attend_gat_pl_sig_k_kernel(tc, qT, kT, vT, doT, rw, qm, offs, out_0, ou
 
     with ExitStack() as ctx:
         sb = ctx.enter_context(tc.tile_pool(name="sb", bufs=1))
-        psum = ctx.enter_context(tc.psum_pool(name="psum", bufs=PLACES))
+        psum = ctx.enter_context(tc.psum_pool(name="psum", bufs=BATCHES))
 
         def planes_of(x):
             return x.rearrange("(p t) c -> p t c", t=PLACES)
@@ -71,28 +75,13 @@ def tile_attend_gat_pl_sig_k_kernel(tc, qT, kT, vT, doT, rw, qm, offs, out_0, ou
                 stop=True,
             )
 
-        def deal(copy, dealt, raw, t0=0, j0=0, j1=PLACES):
-            copy(
-                out=dealt[:, j0:j1, :, t0 : t0 + raw.shape[1]].rearrange("p j s t -> p s j t"),
-                in_=raw[:].rearrange("p t (s j) -> p s j t", j=PLACES)[:, :, j0:j1, :],
-            )
-
-        def deal_rows(copy, dealt, raw, s0, s1):
-            copy(
-                out=dealt[:, :, s0:s1, :].rearrange("p j s t -> p s j t"),
-                in_=raw[:].rearrange("p t (s j) -> p s j t", j=PLACES)[:, s0:s1, :, :],
-            )
-
-        def dealt_tile(dealt, j):
-            return dealt[:, j, :, :].rearrange("p s t -> p (s t)")
+        def flat(grouped, c0, c1):
+            return grouped[:, c0:c1, :].rearrange("p n t -> p (n t)")
 
         halves = (slice(0, HALF), slice(HALF, N))
 
         def entries(cols):
             return offsets[:, cols.start // LIST_ROWS : cols.stop // LIST_ROWS]
-
-        def flat(grouped, c0, c1):
-            return grouped[:, c0:c1, :].rearrange("p n t -> p (n t)")
 
         q_raw = load("q_raw", planes_of(qT[0]))
         offsets = sb.tile([P, N // LIST_ROWS], U16, name="offsets")
@@ -101,7 +90,7 @@ def tile_attend_gat_pl_sig_k_kernel(tc, qT, kT, vT, doT, rw, qm, offs, out_0, ou
         nc.scalar.dma_start(out=gate[:], in_=rw[0].rearrange("(s j) o -> s (j o)", j=PLACES))
         k_pool = [load("k_pool%d" % t, planes_of(kT)[:, t, :]) for t in range(PLACES)]
         v_pool = [load("v_pool%d" % t, planes_of(vT)[:, t, :]) for t in range(PLACES)]
-        do_raw = [load("do_raw%d" % u, planes_of(doT[0])[:, 2 * u : 2 * u + 2, :]) for u in range(2)]
+        do_raw = [load("do_raw%d" % w, planes_of(doT[0])[:, 2 * w : 2 * w + 2, :]) for w in range(2)]
         qm_raw = load("qm_raw", planes_of(qm[0]))
 
         windows = [sb.tile([P, T], F32, name="window%d" % j, align_bytes=64) for j in range(PLACES)]
@@ -143,36 +132,35 @@ def tile_attend_gat_pl_sig_k_kernel(tc, qT, kT, vT, doT, rw, qm, offs, out_0, ou
             quantize(k_mx, E4M3, cols.start, cols.stop, flat(k_grouped, cols.start, cols.stop))
 
         squares = []
-        for c in range(PLACES):
-            score = psum.tile([P, R], F32, name="score", tag="first_last")
-            product(score, k_mx, E4M3, c, q_mx, E4M3)
-            tanh = sb.tile([P, R], F32, name="tanh%d" % c, align_bytes=64)
+        for b in range(BATCHES):
+            score = psum.tile([P, R], F32, name="score", tag="first")
+            product(score, k_mx, E4M3, b, q_mx, E4M3)
+            tanh = sb.tile([P, R], F32, name="tanh%d" % b, align_bytes=64)
             nc.scalar.activation(out=tanh[:], in_=score[:], func=ACT.Tanh, scale=0.5)
-            square = sb.tile([P, R], F32, name="square%d" % c, tag="square%d" % c, align_bytes=64)
+            square = sb.tile([P, R], F32, name="square%d" % b, tag="square%d" % b, align_bytes=64)
             nc.scalar.activation(out=square[:], in_=tanh[:], func=ACT.Square)
             squares.append(square)
 
         v_grouped = sb.tile([P, N, PLACES], BF16, name="v_grouped", tag="v_grouped", align_bytes=64)
         v_first = sb.tile([P, 2, N], BF16, name="v_first", align_bytes=64)
         slopes = []
-
-        def form_slopes(chunks, tag):
-            some = sb.tile([P, len(chunks), R], F32, name="slopes%d" % chunks[0], tag=tag, align_bytes=64)
-            for u, c in enumerate(chunks):
-                nc.vector.scalar_tensor_tensor(
-                    out=some[:, u, :], in0=squares[c][:], scalar=1.0, in1=gate_row[:], op0=ALU.subtract, op1=ALU.mult
-                )
-            return [some[:, u, :] for u in range(len(chunks))]
-
         for t in range(LAST):
             dst = v_first[:, t, :] if t < 2 else v_grouped[:, :, t]
             nc.vector.tensor_copy(out=dst, in_=v_pool[t][:].indirect(offsets[:]))
             if t == 1:
                 nc.scalar.copy(out=v_grouped[:, :, 0:2], in_=v_first[:].rearrange("p t n -> p n t"))
             if t < 2:
-                slopes.extend(form_slopes(SLOPES_BEHIND[t], "slopes%d" % t))
-        shifted = sb.tile([P, R], F32, name="shifted", tag="square%d" % (LAST - 1), align_bytes=64)
-        nc.gpsimd.tensor_scalar(out=shifted[:], in0=squares[LAST][:], scalar1=1.0, scalar2=-1.0, op0=ALU.mult, op1=ALU.add)
+                batches = SLOPES_BEHIND[t]
+                some = sb.tile([P, len(batches), R], F32, name="slopes%d" % t, tag="slopes%d" % t, align_bytes=64)
+                for i, b in enumerate(batches):
+                    nc.vector.scalar_tensor_tensor(
+                        out=some[:, i, :], in0=squares[b][:], scalar=1.0, in1=gate_row[:], op0=ALU.subtract, op1=ALU.mult
+                    )
+                    slopes.append(some[:, i, :])
+        shifted = sb.tile([P, R], F32, name="shifted", tag="square%d" % SLOPES_BEHIND[-1][-1], align_bytes=64)
+        nc.gpsimd.tensor_scalar(
+            out=shifted[:], in0=squares[BATCHES - 1][:], scalar1=1.0, scalar2=-1.0, op0=ALU.mult, op1=ALU.add
+        )
         last_slope = sb.tile([P, R], F32, name="last_slope", align_bytes=64)
         nc.gpsimd.tensor_tensor(out=last_slope[:], in0=shifted[:], in1=gate_row[:], op=ALU.mult)
         slopes.append(last_slope[:])
@@ -181,11 +169,11 @@ def tile_attend_gat_pl_sig_k_kernel(tc, qT, kT, vT, doT, rw, qm, offs, out_0, ou
         v_mx = [mx_tiles("v0", HALF)]
         quantize(v_mx[0], E4M3, 0, HALF, flat(v_grouped, 0, HALF))
 
-        for c in range(2):
-            warm = psum.tile([P, R], F32, name="warm", tag="first_last")
-            product(warm, v_mx[0], E4M3, c, q_mx, E4M3)
+        for b in range(WARM_UPS):
+            warm = psum.tile([P, R], F32, name="warm", tag="first")
+            product(warm, v_mx[0], E4M3, b, q_mx, E4M3)
 
-        do_grouped = sb.tile([P, R, PLACES], BF16, name="do_grouped", tag="v_then_do", align_bytes=64)
+        do_grouped = sb.tile([P, R, PLACES], BF16, name="do_grouped", tag="do_grouped", align_bytes=64)
         do_mx = mx_tiles("do", R)
 
         def place_pair(copy, w, c0, c1):
@@ -202,71 +190,77 @@ def tile_attend_gat_pl_sig_k_kernel(tc, qT, kT, vT, doT, rw, qm, offs, out_0, ou
         place_pair(nc.vector.tensor_copy, 1, 0, HALF)
         place_pair(nc.vector.tensor_copy, 1, HALF, HALF + DO_VECTOR)
         place_pair(nc.scalar.copy, 1, HALF + DO_VECTOR, R)
-        quantize(do_mx, E5M2, 0, HALF, flat(do_grouped, 0, HALF))
-        quantize(do_mx, E5M2, HALF, R, flat(do_grouped, HALF, R))
+        for cols in halves:
+            quantize(do_mx, E5M2, cols.start, cols.stop, flat(do_grouped, cols.start, cols.stop))
 
-        v_mx.append(mx_tiles("v1", HALF, "v_then_do"))
+        v_mx.append(mx_tiles("v1", HALF, "do_grouped"))
         quantize(v_mx[1], E4M3, 0, HALF, flat(v_grouped, HALF, N))
         dps = []
-        for c in range(PLACES):
+        for b in range(BATCHES):
             dp = psum.tile([P, R], F32, name="dp", tag="second")
-            product(dp, v_mx[c // 2], E4M3, c % 2, do_mx, E5M2)
+            product(dp, v_mx[b // 2], E4M3, b % 2, do_mx, E5M2)
             dps.append(dp)
 
         qm_dealt = sb.tile([P, PLACES, P, PLACES], BF16, name="qm_dealt", tag="v_grouped", align_bytes=64)
-        deal_rows(nc.scalar.copy, qm_dealt, qm_raw, 0, P // 2)
-        deal_rows(gpsimd_round, qm_dealt, qm_raw, P // 2, P)
-
-        ds_grouped = [sb.tile([P, HALF, PLACES], BF16, name="ds_grouped%d" % h, tag="ds_grouped%d" % h, align_bytes=64) for h in range(2)]
-        for c in range(PLACES):
-            ds = sb.tile([P, R], BF16, name="ds%d" % c, align_bytes=64)
-            for cols in halves if c % 2 else (slice(0, R),):
-                nc.vector.tensor_tensor(out=ds[:, cols], in0=dps[c][:, cols], in1=slopes[c][:, cols], op=ALU.mult)
-            words = ds[:].bitcast(F32)
-            turned = psum.tile([P, 2, P], F32, name="turned", tag="first_last")
-            for u in range(2):
-                nc.tensor.transpose(turned[:, u, :], words[:, u * P : (u + 1) * P], identity[:])
-            h, s0 = divmod(c * P, HALF)
-            nc.scalar.copy(
-                out=flat(ds_grouped[h], s0, s0 + P).bitcast(F32).rearrange("p (s u) -> p s u", u=2),
-                in_=turned[:].rearrange("p u s -> p s u"),
+        for copy, s0, s1 in ((nc.scalar.copy, 0, P // 2), (gpsimd_round, P // 2, P)):
+            copy(
+                out=qm_dealt[:, :, s0:s1, :].rearrange("p j s t -> p s j t"),
+                in_=qm_raw[:].rearrange("p t (s j) -> p s j t", j=PLACES)[:, s0:s1, :, :],
             )
 
-        def quantize_ds(h):
-            quantize(ds_mx, E5M2, HALF + h * HALF, N + h * HALF, flat(ds_grouped[h], 0, HALF))
+        ds_grouped = [
+            sb.tile([P, HALF, PLACES], BF16, name="ds_grouped%d" % h, tag="ds_grouped%d" % h, align_bytes=64)
+            for h in range(2)
+        ]
+        for b in range(BATCHES):
+            ds = sb.tile([P, R], BF16, name="ds%d" % b, align_bytes=64)
+            for cols in halves if b % 2 else (slice(0, R),):
+                nc.vector.tensor_tensor(out=ds[:, cols], in0=dps[b][:, cols], in1=slopes[b][:, cols], op=ALU.mult)
+            words = ds[:].bitcast(F32)
+            turned = psum.tile([P, 2, P], F32, name="turned", tag="first")
+            for u in range(2):
+                nc.tensor.transpose(turned[:, u, :], words[:, u * P : (u + 1) * P], identity[:])
+            h, n0 = divmod(b * P, HALF)
+            nc.scalar.copy(
+                out=flat(ds_grouped[h], n0, n0 + P).bitcast(F32).rearrange("p (n u) -> p n u", u=2),
+                in_=turned[:].rearrange("p u n -> p n u"),
+            )
 
-        quantize_ds(0)
+        quantize(ds_mx, E5M2, HALF, N, flat(ds_grouped[0], 0, HALF))
         qm_first = mx_tiles("qm_first", P, "slopes1")
         qm_rest = mx_tiles("qm_rest", D - P, "ds_grouped0")
-        quantize(qm_first, E4M3, 0, P, dealt_tile(qm_dealt, 0))
+        quantize(qm_first, E4M3, 0, P, qm_dealt[:, 0, :, :].rearrange("p s t -> p (s t)"))
         early = psum.tile([P, N], F32, name="early", tag="second")
         product(early, qm_first, E4M3, 0, ds_mx, E5M2)
         dk_early = sb.tile([P, HALF], F32, name="dk_early", align_bytes=64)
         nc.scalar.copy(out=dk_early[:], in_=early[:, HALF:N])
-        quantize(qm_rest, E4M3, 0, 2 * P, qm_dealt[:, 1:3, :, :].rearrange("p j s t -> p (j s t)"))
-        quantize(qm_rest, E4M3, 2 * P, 3 * P, dealt_tile(qm_dealt, LAST))
-        for s0 in (0, P):
-            quantize(ds_mx, E5M2, N + s0, N + s0 + P, flat(ds_grouped[1], s0, s0 + P))
+        quantize(qm_rest, E4M3, 0, 2 * P, qm_dealt[:, 1:LAST, :, :].rearrange("p j s t -> p (j s t)"))
+        quantize(qm_rest, E4M3, 2 * P, LAST * P, qm_dealt[:, LAST, :, :].rearrange("p s t -> p (s t)"))
+        for n0 in (0, P):
+            quantize(ds_mx, E5M2, N + n0, N + n0 + P, flat(ds_grouped[1], n0, n0 + P))
         nc.vector.tensor_copy(out=windows[0][:].indirect(entries(halves[0])), in_=dk_early[:])
 
         left = [halves[1]] + [slice(0, N)] * LAST
+        qm_tiles = [(qm_first, 0)] + [(qm_rest, j) for j in range(LAST)]
         dks = []
-        for j in range(PLACES):
+        for j, (qm_mx, tile_j) in enumerate(qm_tiles):
             acc = psum.tile([P, N], F32, name="acc", tag="second")
-            product(acc, qm_rest if j else qm_first, E4M3, max(j - 1, 0), ds_mx, E5M2, HALF)
+            product(acc, qm_mx, E4M3, tile_j, ds_mx, E5M2, HALF)
             dk = sb.tile([P, left[j].stop - left[j].start], F32, name="dk%d" % j, align_bytes=64)
             nc.scalar.copy(out=dk[:], in_=acc[:, left[j]])
             dks.append(dk)
 
         starts = [sum(CHUNKS[:c]) for c in range(len(CHUNKS))]
-        grouped = [sb.tile([P, w, PLACES], BF16, name="out_grouped%d" % c, align_bytes=64) for c, w in enumerate(CHUNKS)]
+        out_grouped = [
+            sb.tile([P, w, PLACES], BF16, name="out_grouped%d" % c, align_bytes=64) for c, w in enumerate(CHUNKS)
+        ]
 
         def place(copy, j, c, w0, w1):
             src = windows[j][:, starts[c] + w0 : starts[c] + w1]
             if j == LAST - 1:
-                copy(out=grouped[c][:, w0:w1, j:PLACES], in_=src.unsqueeze(2).to_broadcast([P, w1 - w0, 2]))
+                copy(out=out_grouped[c][:, w0:w1, j:PLACES], in_=src.unsqueeze(2).to_broadcast([P, w1 - w0, 2]))
             else:
-                copy(out=grouped[c][:, w0:w1, j], in_=src)
+                copy(out=out_grouped[c][:, w0:w1, j], in_=src)
 
         for j in range(PLACES):
             nc.vector.tensor_copy(out=windows[j][:].indirect(entries(left[j])), in_=dks[j][:])
@@ -274,10 +268,14 @@ def tile_attend_gat_pl_sig_k_kernel(tc, qT, kT, vT, doT, rw, qm, offs, out_0, ou
             queue.dma_start(out=planes_of(out_0)[:, j, :], in_=windows[j][:])
             if j < LAST:
                 for c, w in enumerate(CHUNKS):
-                    place(nc.scalar.copy if c in SCALAR_CHUNKS else gpsimd_round, j, c, 0, w)
+                    w0 = 0
+                    if j == LAST - 1 and c == LAST_CHUNK:
+                        w0 = SCALAR_EXTRA
+                        place(nc.scalar.copy, j, c, 0, w0)
+                    place(nc.scalar.copy if c in SCALAR_CHUNKS else gpsimd_round, j, c, w0, w)
         vector_tokens = [min(w, VECTOR_PIECE) if c in SCALAR_CHUNKS else 0 for c, w in enumerate(CHUNKS)]
         for c, w in enumerate(CHUNKS):
-            step = w // 2 if c == len(CHUNKS) - 1 else w
+            step = w // 2 if c == LAST_CHUNK else w
             for w0 in range(vector_tokens[c], w, step):
                 place(nc.scalar.copy, LAST, c, w0, min(w0 + step, w))
 
@@ -290,14 +288,14 @@ def tile_attend_gat_pl_sig_k_kernel(tc, qT, kT, vT, doT, rw, qm, offs, out_0, ou
         for c, w in enumerate(CHUNKS):
             for ahead in SCALAR_CHUNKS[c + 1 : c + 2]:
                 place(nc.vector.tensor_copy, LAST, ahead, 0, vector_tokens[ahead])
-            step = w // 2 if c == len(CHUNKS) - 1 else QUANT_TOKENS
+            step = w // 2 if c == LAST_CHUNK else QUANT_TOKENS
             for w0 in range(0, w, step):
                 c0 = starts[c] + w0
                 a, b0 = divmod(c0, band)
                 nc.vector.quantize_mx(
                     out=out_codes[:, c0 : c0 + step].bitcast(E4M3),
                     scales=out_scales[PLACES * a : P, b0 : b0 + step],
-                    in_=grouped[c][:, w0 : w0 + step, :].rearrange("p n t -> p (n t)"),
+                    in_=flat(out_grouped[c], w0, w0 + step),
                 )
             if c > 0:
                 c1 = starts[c] + w

@@ -28,11 +28,10 @@ ACT = mybir.ActivationFunctionType
 SLOPES_BEHIND = ((0,), (1, 2))
 DO_GPSIMD = 192
 DO_VECTOR = 48
-CHUNKS = (256, 256, 512, 512, 256, 256)
-LAST_CHUNK = len(CHUNKS) - 1
-SCALAR_CHUNKS = (0, 1, 3)
-SCALAR_EXTRA = 96
-VECTOR_PIECE = 400
+CHUNKS = (128, 128, 256, 512, 512, 256, 128, 128)
+GPSIMD_CHUNKS = (3, 4)
+VECTOR_WEAVES = (2,)
+STORE_BEHIND = (2, 3, 4, 5, 7)
 SCALE_BANDS = 4
 QUANT_TOKENS = T // SCALE_BANDS // 2
 
@@ -63,14 +62,14 @@ def tile_attend_gat_pl_sig_k_kernel(tc, qT, kT, vT, doT, rw, qm, offs, out_0, ou
         def gpsimd_round(out, in_):
             nc.gpsimd.tensor_scalar(out=out, in0=in_, scalar1=1.0, scalar2=0.0, op0=ALU.mult, op1=ALU.add)
 
-        def product(out, lhs, lhs_fmt, j, rhs, rhs_fmt, c0=0):
+        def product(out, lhs, lhs_fmt, j, rhs, rhs_fmt, moving=slice(0, N)):
             cols = slice(j * P, (j + 1) * P)
             nc.tensor.matmul_mx(
-                out=out[:],
+                out=out,
                 lhsT=lhs[0][:, cols].bitcast(lhs_fmt),
                 lhsT_scale=lhs[1][:, cols],
-                rhs=rhs[0][:, c0 : c0 + N].bitcast(rhs_fmt),
-                rhs_scale=rhs[1][:, c0 : c0 + N],
+                rhs=rhs[0][:, moving].bitcast(rhs_fmt),
+                rhs_scale=rhs[1][:, moving],
                 start=True,
                 stop=True,
             )
@@ -97,9 +96,7 @@ def tile_attend_gat_pl_sig_k_kernel(tc, qT, kT, vT, doT, rw, qm, offs, out_0, ou
         for window in windows[:LAST]:
             nc.vector.memset(window[:], 0.0)
 
-        ds_mx = mx_tiles("ds", HALF + N)
-        nc.gpsimd.memset(ds_mx[0][:, 0:HALF], 0)
-        nc.gpsimd.memset(ds_mx[1][:, 0:HALF], 0)
+        ds_mx = mx_tiles("ds", N)
         identity = sb.tile([P, P], F32, name="identity", align_bytes=64)
         make_identity(nc, identity[:])
         nc.gpsimd.memset(windows[LAST][:], 0.0)
@@ -134,7 +131,7 @@ def tile_attend_gat_pl_sig_k_kernel(tc, qT, kT, vT, doT, rw, qm, offs, out_0, ou
         squares = []
         for b in range(BATCHES):
             score = psum.tile([P, R], F32, name="score", tag="first")
-            product(score, k_mx, E4M3, b, q_mx, E4M3)
+            product(score[:], k_mx, E4M3, b, q_mx, E4M3)
             tanh = sb.tile([P, R], F32, name="tanh%d" % b, align_bytes=64)
             nc.scalar.activation(out=tanh[:], in_=score[:], func=ACT.Tanh, scale=0.5)
             square = sb.tile([P, R], F32, name="square%d" % b, tag="square%d" % b, align_bytes=64)
@@ -171,7 +168,7 @@ def tile_attend_gat_pl_sig_k_kernel(tc, qT, kT, vT, doT, rw, qm, offs, out_0, ou
 
         for b in range(WARM_UPS):
             warm = psum.tile([P, R], F32, name="warm", tag="first")
-            product(warm, v_mx[0], E4M3, b, q_mx, E4M3)
+            product(warm[:], v_mx[0], E4M3, b, q_mx, E4M3)
 
         do_grouped = sb.tile([P, R, PLACES], BF16, name="do_grouped", tag="do_grouped", align_bytes=64)
         do_mx = mx_tiles("do", R)
@@ -198,7 +195,7 @@ def tile_attend_gat_pl_sig_k_kernel(tc, qT, kT, vT, doT, rw, qm, offs, out_0, ou
         dps = []
         for b in range(BATCHES):
             dp = psum.tile([P, R], F32, name="dp", tag="second")
-            product(dp, v_mx[b // 2], E4M3, b % 2, do_mx, E5M2)
+            product(dp[:], v_mx[b // 2], E4M3, b % 2, do_mx, E5M2)
             dps.append(dp)
 
         qm_dealt = sb.tile([P, PLACES, P, PLACES], BF16, name="qm_dealt", tag="v_grouped", align_bytes=64)
@@ -226,70 +223,79 @@ def tile_attend_gat_pl_sig_k_kernel(tc, qT, kT, vT, doT, rw, qm, offs, out_0, ou
                 in_=turned[:].rearrange("p u n -> p n u"),
             )
 
-        quantize(ds_mx, E5M2, HALF, N, flat(ds_grouped[0], 0, HALF))
+        quantize(ds_mx, E5M2, 0, HALF, flat(ds_grouped[0], 0, HALF))
         qm_first = mx_tiles("qm_first", P, "slopes1")
         qm_rest = mx_tiles("qm_rest", D - P, "ds_grouped0")
         quantize(qm_first, E4M3, 0, P, qm_dealt[:, 0, :, :].rearrange("p s t -> p (s t)"))
-        early = psum.tile([P, N], F32, name="early", tag="second")
-        product(early, qm_first, E4M3, 0, ds_mx, E5M2)
-        dk_early = sb.tile([P, HALF], F32, name="dk_early", align_bytes=64)
-        nc.scalar.copy(out=dk_early[:], in_=early[:, HALF:N])
+
+        def gradient(copy, qm_mx, tile_j, cols, name):
+            width = cols.stop - cols.start
+            acc = psum.tile([P, N], F32, name="acc", tag="second")
+            product(acc[:, 0:width], qm_mx, E4M3, tile_j, ds_mx, E5M2, cols)
+            dk = sb.tile([P, width], F32, name=name, align_bytes=64)
+            copy(out=dk[:], in_=acc[:, 0:width])
+            return dk
+
+        def scalar_scatter(j, cols, src):
+            nc.scalar.activation(out=windows[j][:].indirect(entries(cols)), in_=src, func=ACT.Copy)
+
+        def store_plane(j):
+            nc.sync.dma_start(out=planes_of(out_0)[:, j, :], in_=windows[j][:])
+
+        dk_early = gradient(nc.scalar.copy, qm_first, 0, halves[0], "dk_early")
+        scalar_scatter(0, halves[0], dk_early[:])
         quantize(qm_rest, E4M3, 0, 2 * P, qm_dealt[:, 1:LAST, :, :].rearrange("p j s t -> p (j s t)"))
         quantize(qm_rest, E4M3, 2 * P, LAST * P, qm_dealt[:, LAST, :, :].rearrange("p s t -> p (s t)"))
         for n0 in (0, P):
-            quantize(ds_mx, E5M2, N + n0, N + n0 + P, flat(ds_grouped[1], n0, n0 + P))
-        nc.vector.tensor_copy(out=windows[0][:].indirect(entries(halves[0])), in_=dk_early[:])
+            quantize(ds_mx, E5M2, HALF + n0, HALF + n0 + P, flat(ds_grouped[1], n0, n0 + P))
 
-        left = [halves[1]] + [slice(0, N)] * LAST
-        qm_tiles = [(qm_first, 0)] + [(qm_rest, j) for j in range(LAST)]
-        dks = []
-        for j, (qm_mx, tile_j) in enumerate(qm_tiles):
-            acc = psum.tile([P, N], F32, name="acc", tag="second")
-            product(acc, qm_mx, E4M3, tile_j, ds_mx, E5M2, HALF)
-            dk = sb.tile([P, left[j].stop - left[j].start], F32, name="dk%d" % j, align_bytes=64)
-            nc.scalar.copy(out=dk[:], in_=acc[:, left[j]])
-            dks.append(dk)
+        every = slice(0, N)
+        dk_late = gradient(nc.vector.tensor_copy, qm_first, 0, halves[1], "dk_late")
+        scalar_scatter(0, halves[1], dk_late[:])
+        store_plane(0)
+        dk1 = gradient(nc.vector.tensor_copy, qm_rest, 0, every, "dk1")
+        dk2 = gradient(nc.vector.tensor_copy, qm_rest, 1, every, "dk2")
+        nc.vector.tensor_copy(out=windows[1][:].indirect(offsets[:]), in_=dk1[:])
+        store_plane(1)
+        for cols in halves:
+            scalar_scatter(2, cols, dk2[:, cols])
+        store_plane(2)
+        dk3 = gradient(nc.vector.tensor_copy, qm_rest, 2, every, "dk3")
+        for cols in halves:
+            scalar_scatter(LAST, cols, dk3[:, cols])
+        store_plane(LAST)
 
         starts = [sum(CHUNKS[:c]) for c in range(len(CHUNKS))]
+        pairs = [
+            sb.tile([P, 2, w, 2], BF16, name="pairs%d" % c, align_bytes=64) for c, w in enumerate(CHUNKS)
+        ]
         out_grouped = [
             sb.tile([P, w, PLACES], BF16, name="out_grouped%d" % c, align_bytes=64) for c, w in enumerate(CHUNKS)
         ]
 
-        def place(copy, j, c, w0, w1):
-            src = windows[j][:, starts[c] + w0 : starts[c] + w1]
-            if j == LAST - 1:
-                copy(out=out_grouped[c][:, w0:w1, j:PLACES], in_=src.unsqueeze(2).to_broadcast([P, w1 - w0, 2]))
-            else:
-                copy(out=out_grouped[c][:, w0:w1, j], in_=src)
-
         for j in range(PLACES):
-            nc.vector.tensor_copy(out=windows[j][:].indirect(entries(left[j])), in_=dks[j][:])
-            queue = nc.sync if j in (0, LAST) else nc.scalar
-            queue.dma_start(out=planes_of(out_0)[:, j, :], in_=windows[j][:])
-            if j < LAST:
-                for c, w in enumerate(CHUNKS):
-                    w0 = 0
-                    if j == LAST - 1 and c == LAST_CHUNK:
-                        w0 = SCALAR_EXTRA
-                        place(nc.scalar.copy, j, c, 0, w0)
-                    place(nc.scalar.copy if c in SCALAR_CHUNKS else gpsimd_round, j, c, w0, w)
-        vector_tokens = [min(w, VECTOR_PIECE) if c in SCALAR_CHUNKS else 0 for c, w in enumerate(CHUNKS)]
-        for c, w in enumerate(CHUNKS):
-            step = w // 2 if c == LAST_CHUNK else w
-            for w0 in range(vector_tokens[c], w, step):
-                place(nc.scalar.copy, LAST, c, w0, min(w0 + step, w))
+            u, e = divmod(j, 2)
+            for c, w in enumerate(CHUNKS):
+                src = windows[j][:, starts[c] : starts[c] + w]
+                if j == 0 and c in GPSIMD_CHUNKS:
+                    gpsimd_round(out=pairs[c][:, 0, :, :], in_=src.unsqueeze(2).to_broadcast([P, w, 2]))
+                else:
+                    nc.vector.tensor_copy(out=pairs[c][:, u, :, e], in_=src)
 
         band = T // SCALE_BANDS
         out_codes = sb.tile([P, T], U32, name="out_codes", align_bytes=64)
         out_scales = sb.tile([P, band], U8, name="out_scales", align_bytes=64)
         words_out = out_1[0].rearrange("p t l -> p (t l)").bitcast(I32)
-        place(nc.vector.tensor_copy, LAST, SCALAR_CHUNKS[0], 0, vector_tokens[SCALAR_CHUNKS[0]])
         stored = 0
         for c, w in enumerate(CHUNKS):
-            for ahead in SCALAR_CHUNKS[c + 1 : c + 2]:
-                place(nc.vector.tensor_copy, LAST, ahead, 0, vector_tokens[ahead])
-            step = w // 2 if c == LAST_CHUNK else QUANT_TOKENS
-            for w0 in range(0, w, step):
+            weave = nc.vector.tensor_copy if c in VECTOR_WEAVES else nc.scalar.copy
+            weave(
+                out=flat(out_grouped[c], 0, w).bitcast(F32).rearrange("p (n u) -> p n u", u=2),
+                in_=pairs[c][:].rearrange("p u n e -> p u (n e)").bitcast(F32).rearrange("p u n -> p n u"),
+            )
+        for c, w in enumerate(CHUNKS):
+            for w0 in range(0, w, QUANT_TOKENS):
+                step = min(w, QUANT_TOKENS)
                 c0 = starts[c] + w0
                 a, b0 = divmod(c0, band)
                 nc.vector.quantize_mx(
@@ -297,12 +303,12 @@ def tile_attend_gat_pl_sig_k_kernel(tc, qT, kT, vT, doT, rw, qm, offs, out_0, ou
                     scales=out_scales[PLACES * a : P, b0 : b0 + step],
                     in_=flat(out_grouped[c], w0, w0 + step),
                 )
-            if c > 0:
+            if c in STORE_BEHIND:
                 c1 = starts[c] + w
                 nc.sync.dma_start(out=words_out[:, stored:c1], in_=out_codes[:, stored:c1].bitcast(I32))
                 stored = c1
         for q in range(P // QUADRANT):
-            queue = nc.scalar if q % 2 else nc.sync
+            queue = nc.sync
             rows = out_2[0, PLACES * q : PLACES * (q + 1), :].bitcast(I32)
             queue.dma_start(
                 out=rows.rearrange("r (a c) -> a r c", a=SCALE_BANDS),

@@ -28,10 +28,9 @@ ACT = mybir.ActivationFunctionType
 SLOPES_BEHIND = ((0,), (1, 2))
 DO_GPSIMD = 192
 DO_VECTOR = 48
-CHUNKS = (128, 128, 256, 512, 512, 256, 128, 128)
-GPSIMD_CHUNKS = (3, 4)
-VECTOR_WEAVES = (2,)
-STORE_BEHIND = (2, 3, 4, 5, 7)
+GPSIMD_STRIPS = 10
+PIECES = ((14, 16), (0, 2), (2, 4), (4, 6), (6, 8), (8, 10), (10, 12), (12, 13), (13, 14))
+STORE_BEHIND = {0: (14, 16), 2: (0, 4), 4: (4, 8), 6: (8, 12), 8: (12, 14)}
 SCALE_BANDS = 4
 QUANT_TOKENS = T // SCALE_BANDS // 2
 
@@ -158,7 +157,7 @@ def tile_attend_gat_pl_sig_k_kernel(tc, qT, kT, vT, doT, rw, qm, offs, out_0, ou
         nc.gpsimd.tensor_scalar(
             out=shifted[:], in0=squares[BATCHES - 1][:], scalar1=1.0, scalar2=-1.0, op0=ALU.mult, op1=ALU.add
         )
-        last_slope = sb.tile([P, R], F32, name="last_slope", align_bytes=64)
+        last_slope = sb.tile([P, R], F32, name="last_slope", tag="last_slope", align_bytes=64)
         nc.gpsimd.tensor_tensor(out=last_slope[:], in0=shifted[:], in1=gate_row[:], op=ALU.mult)
         slopes.append(last_slope[:])
         for cols in halves:
@@ -209,104 +208,142 @@ def tile_attend_gat_pl_sig_k_kernel(tc, qT, kT, vT, doT, rw, qm, offs, out_0, ou
             sb.tile([P, HALF, PLACES], BF16, name="ds_grouped%d" % h, tag="ds_grouped%d" % h, align_bytes=64)
             for h in range(2)
         ]
-        for b in range(BATCHES):
-            ds = sb.tile([P, R], BF16, name="ds%d" % b, align_bytes=64)
-            for cols in halves if b % 2 else (slice(0, R),):
-                nc.vector.tensor_tensor(out=ds[:, cols], in0=dps[b][:, cols], in1=slopes[b][:, cols], op=ALU.mult)
+
+        def form_ds(b, cols, turned, tag):
+            ds = sb.tile([P, cols.stop - cols.start], BF16, name=tag + "_ds", tag=tag, align_bytes=64)
+            nc.vector.tensor_tensor(out=ds[:], in0=dps[b][:, cols], in1=slopes[b][:, cols], op=ALU.mult)
             words = ds[:].bitcast(F32)
-            turned = psum.tile([P, 2, P], F32, name="turned", tag="first")
-            for u in range(2):
-                nc.tensor.transpose(turned[:, u, :], words[:, u * P : (u + 1) * P], identity[:])
+            for u in range(cols.start // HALF, cols.stop // HALF):
+                w0 = u * P - cols.start // 2
+                nc.tensor.transpose(turned[:, u, :], words[:, w0 : w0 + P], identity[:])
+
+        def empty_turned(copy, b, turned):
             h, n0 = divmod(b * P, HALF)
-            nc.scalar.copy(
+            copy(
                 out=flat(ds_grouped[h], n0, n0 + P).bitcast(F32).rearrange("p (n u) -> p n u", u=2),
                 in_=turned[:].rearrange("p u n -> p n u"),
             )
 
-        quantize(ds_mx, E5M2, 0, HALF, flat(ds_grouped[0], 0, HALF))
+        for b in range(LAST):
+            turned = psum.tile([P, 2, P], F32, name="turned", tag="first")
+            for cols in halves if b % 2 else (slice(0, R),):
+                form_ds(b, cols, turned, "ds%d_%d" % (b, cols.start))
+            empty_turned(nc.scalar.copy, b, turned)
         qm_first = mx_tiles("qm_first", P, "slopes1")
-        qm_rest = mx_tiles("qm_rest", D - P, "ds_grouped0")
         quantize(qm_first, E4M3, 0, P, qm_dealt[:, 0, :, :].rearrange("p s t -> p (s t)"))
+        turned = psum.tile([P, 2, P], F32, name="turned", tag="first")
+        form_ds(LAST, halves[0], turned, "ds3_0")
+        form_ds(LAST, halves[1], turned, "ds3_1")
+        empty_turned(nc.scalar.copy, LAST, turned)
+        quantize(ds_mx, E5M2, 0, HALF, flat(ds_grouped[0], 0, HALF))
 
-        def gradient(copy, qm_mx, tile_j, cols, name):
-            width = cols.stop - cols.start
-            acc = psum.tile([P, N], F32, name="acc", tag="second")
-            product(acc[:, 0:width], qm_mx, E4M3, tile_j, ds_mx, E5M2, cols)
-            dk = sb.tile([P, width], F32, name=name, align_bytes=64)
-            copy(out=dk[:], in_=acc[:, 0:width])
+        accs = [psum.tile([P, N], F32, name="acc", tag="second") for j in range(PLACES)]
+        every = slice(0, N)
+
+        def empty(copy, src, name, tag):
+            dk = sb.tile(list(src.shape), F32, name=name, tag=tag, align_bytes=64)
+            copy(out=dk[:], in_=src)
             return dk
 
         def scalar_scatter(j, cols, src):
             nc.scalar.activation(out=windows[j][:].indirect(entries(cols)), in_=src, func=ACT.Copy)
 
+        def vector_scatter(j, cols, src):
+            nc.vector.tensor_copy(out=windows[j][:].indirect(entries(cols)), in_=src)
+
         def store_plane(j):
             nc.sync.dma_start(out=planes_of(out_0)[:, j, :], in_=windows[j][:])
 
-        dk_early = gradient(nc.scalar.copy, qm_first, 0, halves[0], "dk_early")
-        scalar_scatter(0, halves[0], dk_early[:])
+        product(accs[0][:, halves[0]], qm_first, E4M3, 0, ds_mx, E5M2, halves[0])
+        scalar_scatter(0, halves[0], empty(nc.scalar.copy, accs[0][:, halves[0]], "dk_first", "dk_first")[:])
+        qm_rest = mx_tiles("qm_rest", D - P, "ds_grouped0")
         quantize(qm_rest, E4M3, 0, 2 * P, qm_dealt[:, 1:LAST, :, :].rearrange("p j s t -> p (j s t)"))
         quantize(qm_rest, E4M3, 2 * P, LAST * P, qm_dealt[:, LAST, :, :].rearrange("p s t -> p (s t)"))
+        for j in range(1, PLACES):
+            product(accs[j][:, halves[0]], qm_rest, E4M3, j - 1, ds_mx, E5M2, halves[0])
         for n0 in (0, P):
             quantize(ds_mx, E5M2, HALF + n0, HALF + n0 + P, flat(ds_grouped[1], n0, n0 + P))
-
-        every = slice(0, N)
-        dk_late = gradient(nc.vector.tensor_copy, qm_first, 0, halves[1], "dk_late")
-        scalar_scatter(0, halves[1], dk_late[:])
+        product(accs[1][:, halves[1]], qm_first, E4M3, 0, ds_mx, E5M2, halves[1])
+        product(accs[0][:, halves[1]], qm_rest, E4M3, 0, ds_mx, E5M2, halves[1])
+        for j in (2, LAST):
+            product(accs[j][:, halves[1]], qm_rest, E4M3, j - 1, ds_mx, E5M2, halves[1])
+        crossed = empty(nc.vector.tensor_copy, accs[1][:], "dk_crossed", "dk_crossed")
+        vector_scatter(1, halves[0], crossed[:, halves[0]])
+        scalar_scatter(0, halves[1], crossed[:, halves[1]])
         store_plane(0)
-        dk1 = gradient(nc.vector.tensor_copy, qm_rest, 0, every, "dk1")
-        dk2 = gradient(nc.vector.tensor_copy, qm_rest, 1, every, "dk2")
-        nc.vector.tensor_copy(out=windows[1][:].indirect(offsets[:]), in_=dk1[:])
+        vector_scatter(1, halves[1], empty(nc.vector.tensor_copy, accs[0][:, halves[1]], "dk_second", "dk_second")[:])
         store_plane(1)
+        dk_rest = sb.tile([P, 2 * N], F32, name="dk_rest", tag="dk_crossed", align_bytes=64)
+        for j in (2, LAST):
+            nc.scalar.copy(out=dk_rest[:, (j - 2) * N : (j - 1) * N], in_=accs[j][:])
         for cols in halves:
-            scalar_scatter(2, cols, dk2[:, cols])
+            scalar_scatter(2, cols, dk_rest[:, cols])
         store_plane(2)
-        dk3 = gradient(nc.vector.tensor_copy, qm_rest, 2, every, "dk3")
-        for cols in halves:
-            scalar_scatter(LAST, cols, dk3[:, cols])
+        vector_scatter(LAST, every, dk_rest[:, N : 2 * N])
         store_plane(LAST)
 
-        starts = [sum(CHUNKS[:c]) for c in range(len(CHUNKS))]
-        pairs = [
-            sb.tile([P, 2, w, 2], BF16, name="pairs%d" % c, align_bytes=64) for c, w in enumerate(CHUNKS)
-        ]
-        out_grouped = [
-            sb.tile([P, w, PLACES], BF16, name="out_grouped%d" % c, align_bytes=64) for c, w in enumerate(CHUNKS)
-        ]
+        strips = T // P
+        early_pairs = sb.tile([P, GPSIMD_STRIPS * P * PLACES], BF16, name="early_pairs", align_bytes=64)
+        late_pairs = sb.tile(
+            [P, (strips - GPSIMD_STRIPS) * P * PLACES], BF16, name="late_pairs", tag="dk_crossed", align_bytes=64
+        )
 
-        for j in range(PLACES):
+        def runs(s0, s1):
+            found = []
+            for a0, a1, pairs, first in ((s0, min(s1, GPSIMD_STRIPS), early_pairs, 0),
+                                         (max(s0, GPSIMD_STRIPS), s1, late_pairs, GPSIMD_STRIPS)):
+                if a0 < a1:
+                    found.append((a0, a1, pairs[:, (a0 - first) * P * PLACES : (a1 - first) * P * PLACES]))
+            return found
+
+        def round_plane(copy, j, s0, s1):
             u, e = divmod(j, 2)
-            for c, w in enumerate(CHUNKS):
-                src = windows[j][:, starts[c] : starts[c] + w]
-                if j == 0 and c in GPSIMD_CHUNKS:
-                    gpsimd_round(out=pairs[c][:, 0, :, :], in_=src.unsqueeze(2).to_broadcast([P, w, 2]))
-                else:
-                    nc.vector.tensor_copy(out=pairs[c][:, u, :, e], in_=src)
+            for a0, a1, pairs in runs(s0, s1):
+                copy(
+                    out=pairs.rearrange("p (s u n e) -> p s u n e", u=2, n=P, e=2)[:, :, u, :, e],
+                    in_=windows[j][:, a0 * P : a1 * P].rearrange("p (s n) -> p s n", n=P),
+                )
+
+        for j in range(2):
+            round_plane(gpsimd_round, j, 0, GPSIMD_STRIPS)
+        for j in range(2):
+            round_plane(nc.vector.tensor_copy, j, GPSIMD_STRIPS, strips)
+        for j in (2, LAST):
+            round_plane(nc.vector.tensor_copy, j, *PIECES[0])
+        for s0, s1 in PIECES[1:]:
+            for j in (2, LAST):
+                round_plane(nc.scalar.copy, j, s0, s1)
 
         band = T // SCALE_BANDS
         out_codes = sb.tile([P, T], U32, name="out_codes", align_bytes=64)
         out_scales = sb.tile([P, band], U8, name="out_scales", align_bytes=64)
         words_out = out_1[0].rearrange("p t l -> p (t l)").bitcast(I32)
-        stored = 0
-        for c, w in enumerate(CHUNKS):
-            weave = nc.vector.tensor_copy if c in VECTOR_WEAVES else nc.scalar.copy
-            weave(
-                out=flat(out_grouped[c], 0, w).bitcast(F32).rearrange("p (n u) -> p n u", u=2),
-                in_=pairs[c][:].rearrange("p u n e -> p u (n e)").bitcast(F32).rearrange("p u n -> p n u"),
-            )
-        for c, w in enumerate(CHUNKS):
-            for w0 in range(0, w, QUANT_TOKENS):
-                step = min(w, QUANT_TOKENS)
-                c0 = starts[c] + w0
-                a, b0 = divmod(c0, band)
-                nc.vector.quantize_mx(
-                    out=out_codes[:, c0 : c0 + step].bitcast(E4M3),
-                    scales=out_scales[PLACES * a : P, b0 : b0 + step],
-                    in_=flat(out_grouped[c], w0, w0 + step),
+        out_grouped = [
+            sb.tile([P, (s1 - s0) * P * PLACES], BF16, name="out_grouped%d" % s0, align_bytes=64) for s0, s1 in PIECES
+        ]
+
+        def weave(c):
+            s0, s1 = PIECES[c]
+            for a0, a1, pairs in runs(s0, s1):
+                words = out_grouped[c][:, (a0 - s0) * P * PLACES : (a1 - s0) * P * PLACES].bitcast(F32)
+                nc.vector.tensor_copy(
+                    out=words.rearrange("p (s n u) -> p s n u", n=P, u=2),
+                    in_=pairs.bitcast(F32).rearrange("p (s u n) -> p s n u", u=2, n=P),
                 )
+
+        weave(0)
+        for c, (s0, s1) in enumerate(PIECES):
+            if c + 1 < len(PIECES):
+                weave(c + 1)
+            a, b0 = divmod(s0 * P, band)
+            nc.vector.quantize_mx(
+                out=out_codes[:, s0 * P : s1 * P].bitcast(E4M3),
+                scales=out_scales[PLACES * a : P, b0 : b0 + (s1 - s0) * P],
+                in_=out_grouped[c][:],
+            )
             if c in STORE_BEHIND:
-                c1 = starts[c] + w
-                nc.sync.dma_start(out=words_out[:, stored:c1], in_=out_codes[:, stored:c1].bitcast(I32))
-                stored = c1
+                c0, c1 = STORE_BEHIND[c][0] * P, STORE_BEHIND[c][1] * P
+                nc.sync.dma_start(out=words_out[:, c0:c1], in_=out_codes[:, c0:c1].bitcast(I32))
         for q in range(P // QUADRANT):
             queue = nc.sync
             rows = out_2[0, PLACES * q : PLACES * (q + 1), :].bitcast(I32)

@@ -28,9 +28,11 @@ ACT = mybir.ActivationFunctionType
 SLOPES_BEHIND = ((0,), (1, 2))
 DO_GPSIMD = 192
 DO_VECTOR = 48
-GPSIMD_STRIPS = 10
-PIECES = ((14, 16), (0, 2), (2, 4), (4, 6), (6, 8), (8, 10), (10, 12), (12, 13), (13, 14))
-STORE_BEHIND = {0: (14, 16), 2: (0, 4), 4: (4, 8), 6: (8, 12), 8: (12, 14)}
+GPSIMD_STRIPS = 6
+LAST_RUNS = ((0, 2), (2, 8), (8, 16))
+PIECES = ((0, 2), (2, 4), (4, 6), (6, 8), (8, 10), (10, 12), (12, 14), (14, 15), (15, 16))
+VECTOR_WEAVES = (3,)
+STORE_BEHIND = {1: (0, 4), 3: (4, 8), 5: (8, 12), 6: (12, 14), 8: (14, 16)}
 SCALE_BANDS = 4
 QUANT_TOKENS = T // SCALE_BANDS // 2
 
@@ -238,10 +240,9 @@ def tile_attend_gat_pl_sig_k_kernel(tc, qT, kT, vT, doT, rw, qm, offs, out_0, ou
         quantize(ds_mx, E5M2, 0, HALF, flat(ds_grouped[0], 0, HALF))
 
         accs = [psum.tile([P, N], F32, name="acc", tag="second") for j in range(PLACES)]
-        every = slice(0, N)
 
-        def empty(copy, src, name, tag):
-            dk = sb.tile(list(src.shape), F32, name=name, tag=tag, align_bytes=64)
+        def empty(copy, src, name):
+            dk = sb.tile(list(src.shape), F32, name=name, align_bytes=64)
             copy(out=dk[:], in_=src)
             return dk
 
@@ -255,64 +256,63 @@ def tile_attend_gat_pl_sig_k_kernel(tc, qT, kT, vT, doT, rw, qm, offs, out_0, ou
             nc.sync.dma_start(out=planes_of(out_0)[:, j, :], in_=windows[j][:])
 
         product(accs[0][:, halves[0]], qm_first, E4M3, 0, ds_mx, E5M2, halves[0])
-        scalar_scatter(0, halves[0], empty(nc.scalar.copy, accs[0][:, halves[0]], "dk_first", "dk_first")[:])
+        scalar_scatter(0, halves[0], empty(nc.scalar.copy, accs[0][:, halves[0]], "dk0a")[:])
         qm_rest = mx_tiles("qm_rest", D - P, "ds_grouped0")
         quantize(qm_rest, E4M3, 0, 2 * P, qm_dealt[:, 1:LAST, :, :].rearrange("p j s t -> p (j s t)"))
         quantize(qm_rest, E4M3, 2 * P, LAST * P, qm_dealt[:, LAST, :, :].rearrange("p s t -> p (s t)"))
-        for j in range(1, PLACES):
-            product(accs[j][:, halves[0]], qm_rest, E4M3, j - 1, ds_mx, E5M2, halves[0])
+        first, second = halves
+        product(accs[1][:, first], qm_rest, E4M3, 0, ds_mx, E5M2, first)
+        product(accs[1][:, second], qm_rest, E4M3, 1, ds_mx, E5M2, first)
+        product(accs[2][:, first], qm_rest, E4M3, 2, ds_mx, E5M2, first)
         for n0 in (0, P):
             quantize(ds_mx, E5M2, HALF + n0, HALF + n0 + P, flat(ds_grouped[1], n0, n0 + P))
-        product(accs[1][:, halves[1]], qm_first, E4M3, 0, ds_mx, E5M2, halves[1])
-        product(accs[0][:, halves[1]], qm_rest, E4M3, 0, ds_mx, E5M2, halves[1])
-        for j in (2, LAST):
-            product(accs[j][:, halves[1]], qm_rest, E4M3, j - 1, ds_mx, E5M2, halves[1])
-        crossed = empty(nc.vector.tensor_copy, accs[1][:], "dk_crossed", "dk_crossed")
-        vector_scatter(1, halves[0], crossed[:, halves[0]])
-        scalar_scatter(0, halves[1], crossed[:, halves[1]])
+        product(accs[0][:, second], qm_first, E4M3, 0, ds_mx, E5M2, second)
+        product(accs[2][:, second], qm_rest, E4M3, 0, ds_mx, E5M2, second)
+        product(accs[LAST][:, first], qm_rest, E4M3, 1, ds_mx, E5M2, second)
+        product(accs[LAST][:, second], qm_rest, E4M3, 2, ds_mx, E5M2, second)
+        dk1a2a = empty(nc.vector.tensor_copy, accs[1][:], "dk1a2a")
+        dk0b = empty(nc.vector.tensor_copy, accs[0][:, second], "dk0b")
+        dk3a1b = empty(nc.vector.tensor_copy, accs[2][:], "dk3a1b")
+        dk2b = empty(nc.vector.tensor_copy, accs[LAST][:, first], "dk2b")
+        scalar_scatter(1, first, dk1a2a[:, first])
+        vector_scatter(0, second, dk0b[:])
         store_plane(0)
-        vector_scatter(1, halves[1], empty(nc.vector.tensor_copy, accs[0][:, halves[1]], "dk_second", "dk_second")[:])
+        vector_scatter(1, second, dk3a1b[:, second])
         store_plane(1)
-        dk_rest = sb.tile([P, 2 * N], F32, name="dk_rest", tag="dk_crossed", align_bytes=64)
-        for j in (2, LAST):
-            nc.scalar.copy(out=dk_rest[:, (j - 2) * N : (j - 1) * N], in_=accs[j][:])
-        for cols in halves:
-            scalar_scatter(2, cols, dk_rest[:, cols])
+        dk3b = empty(nc.vector.tensor_copy, accs[LAST][:, second], "dk3b")
+        scalar_scatter(2, first, dk1a2a[:, second])
+        scalar_scatter(LAST, first, dk3a1b[:, first])
+        scalar_scatter(2, second, dk2b[:])
         store_plane(2)
-        vector_scatter(LAST, every, dk_rest[:, N : 2 * N])
+        scalar_scatter(LAST, second, dk3b[:])
         store_plane(LAST)
 
         strips = T // P
-        early_pairs = sb.tile([P, GPSIMD_STRIPS * P * PLACES], BF16, name="early_pairs", align_bytes=64)
-        late_pairs = sb.tile(
-            [P, (strips - GPSIMD_STRIPS) * P * PLACES], BF16, name="late_pairs", tag="dk_crossed", align_bytes=64
-        )
+        pairs = sb.tile([P, T * PLACES], BF16, name="pairs", align_bytes=64)
 
-        def runs(s0, s1):
-            found = []
-            for a0, a1, pairs, first in ((s0, min(s1, GPSIMD_STRIPS), early_pairs, 0),
-                                         (max(s0, GPSIMD_STRIPS), s1, late_pairs, GPSIMD_STRIPS)):
-                if a0 < a1:
-                    found.append((a0, a1, pairs[:, (a0 - first) * P * PLACES : (a1 - first) * P * PLACES]))
-            return found
+        def strip_range(s0, s1):
+            return pairs[:, s0 * P * PLACES : s1 * P * PLACES]
 
         def round_plane(copy, j, s0, s1):
             u, e = divmod(j, 2)
-            for a0, a1, pairs in runs(s0, s1):
-                copy(
-                    out=pairs.rearrange("p (s u n e) -> p s u n e", u=2, n=P, e=2)[:, :, u, :, e],
-                    in_=windows[j][:, a0 * P : a1 * P].rearrange("p (s n) -> p s n", n=P),
-                )
+            copy(
+                out=strip_range(s0, s1).rearrange("p (s u n e) -> p s u n e", u=2, n=P, e=2)[:, :, u, :, e],
+                in_=windows[j][:, s0 * P : s1 * P].rearrange("p (s n) -> p s n", n=P),
+            )
 
-        for j in range(2):
-            round_plane(gpsimd_round, j, 0, GPSIMD_STRIPS)
-        for j in range(2):
-            round_plane(nc.vector.tensor_copy, j, GPSIMD_STRIPS, strips)
-        for j in (2, LAST):
-            round_plane(nc.vector.tensor_copy, j, *PIECES[0])
-        for s0, s1 in PIECES[1:]:
-            for j in (2, LAST):
-                round_plane(nc.scalar.copy, j, s0, s1)
+        last = GPSIMD_STRIPS - 1
+        round_plane(gpsimd_round, 0, 0, last)
+        gpsimd_round(
+            out=strip_range(last, last + 1)[:, 0 : 2 * P].rearrange("p (n e) -> p n e", e=2),
+            in_=windows[0][:, last * P : (last + 1) * P].unsqueeze(2).to_broadcast([P, P, 2]),
+        )
+        round_plane(nc.vector.tensor_copy, 0, GPSIMD_STRIPS, strips)
+        round_plane(nc.vector.tensor_copy, 1, GPSIMD_STRIPS, strips)
+        round_plane(nc.vector.tensor_copy, 1, 0, GPSIMD_STRIPS)
+        round_plane(nc.vector.tensor_copy, 2, 0, strips // 2)
+        round_plane(nc.vector.tensor_copy, 2, strips // 2, strips)
+        for s0, s1 in LAST_RUNS:
+            round_plane(nc.vector.tensor_copy, LAST, s0, s1)
 
         band = T // SCALE_BANDS
         out_codes = sb.tile([P, T], U32, name="out_codes", align_bytes=64)
@@ -324,12 +324,11 @@ def tile_attend_gat_pl_sig_k_kernel(tc, qT, kT, vT, doT, rw, qm, offs, out_0, ou
 
         def weave(c):
             s0, s1 = PIECES[c]
-            for a0, a1, pairs in runs(s0, s1):
-                words = out_grouped[c][:, (a0 - s0) * P * PLACES : (a1 - s0) * P * PLACES].bitcast(F32)
-                nc.vector.tensor_copy(
-                    out=words.rearrange("p (s n u) -> p s n u", n=P, u=2),
-                    in_=pairs.bitcast(F32).rearrange("p (s u n) -> p s n u", u=2, n=P),
-                )
+            copy = nc.vector.tensor_copy if c in VECTOR_WEAVES else nc.scalar.copy
+            copy(
+                out=out_grouped[c][:].bitcast(F32).rearrange("p (s n u) -> p s n u", n=P, u=2),
+                in_=strip_range(s0, s1).bitcast(F32).rearrange("p (s u n) -> p s n u", u=2, n=P),
+            )
 
         weave(0)
         for c, (s0, s1) in enumerate(PIECES):

@@ -191,15 +191,18 @@ def tile_attend_gat_pl_sig_k_kernel(tc, qT, kT, vT, doT, rw, qm, offs, out_0, ou
         for cols in halves:
             quantize(do_mx, E5M2, cols.start, cols.stop, flat(do_grouped, cols.start, cols.stop))
 
-        v_mx.append(mx_tiles("v1", HALF, "do_grouped"))
+        v_mx.append(mx_tiles("v1", HALF))
         quantize(v_mx[1], E4M3, 0, HALF, flat(v_grouped, HALF, N))
+        dp_first = psum.tile([P, HALF], F32, name="dp_first", tag="first")
+        product(dp_first[:], v_mx[0], E4M3, 0, do_mx, E5M2, halves[0])
         dps = []
         for b in range(BATCHES):
             dp = psum.tile([P, R], F32, name="dp", tag="second")
-            product(dp[:], v_mx[b // 2], E4M3, b % 2, do_mx, E5M2)
+            cols = slice(0, R) if b else halves[1]
+            product(dp[:, cols], v_mx[b // 2], E4M3, b % 2, do_mx, E5M2, cols)
             dps.append(dp)
 
-        qm_dealt = sb.tile([P, PLACES, P, PLACES], BF16, name="qm_dealt", tag="v_grouped", align_bytes=64)
+        qm_dealt = sb.tile([P, PLACES, P, PLACES], BF16, name="qm_dealt", tag="do_grouped", align_bytes=64)
         for copy, s0, s1 in ((nc.scalar.copy, 0, P // 2), (gpsimd_round, P // 2, P)):
             copy(
                 out=qm_dealt[:, :, s0:s1, :].rearrange("p j s t -> p s j t"),
@@ -213,7 +216,7 @@ def tile_attend_gat_pl_sig_k_kernel(tc, qT, kT, vT, doT, rw, qm, offs, out_0, ou
 
         def form_ds(b, cols, turned, tag):
             ds = sb.tile([P, cols.stop - cols.start], BF16, name=tag + "_ds", tag=tag, align_bytes=64)
-            nc.vector.tensor_tensor(out=ds[:], in0=dps[b][:, cols], in1=slopes[b][:, cols], op=ALU.mult)
+            nc.vector.tensor_tensor(out=ds[:], in0=dp_first[:] if (b, cols) == (0, halves[0]) else dps[b][:, cols], in1=slopes[b][:, cols], op=ALU.mult)
             words = ds[:].bitcast(F32)
             for u in range(cols.start // HALF, cols.stop // HALF):
                 w0 = u * P - cols.start // 2
@@ -228,7 +231,7 @@ def tile_attend_gat_pl_sig_k_kernel(tc, qT, kT, vT, doT, rw, qm, offs, out_0, ou
 
         for b in range(LAST):
             turned = psum.tile([P, 2, P], F32, name="turned", tag="first")
-            for cols in halves if b % 2 else (slice(0, R),):
+            for cols in halves if b < 2 else (slice(0, R),):
                 form_ds(b, cols, turned, "ds%d_%d" % (b, cols.start))
             empty_turned(nc.scalar.copy, b, turned)
         qm_first = mx_tiles("qm_first", P, "slopes1")

@@ -10,8 +10,8 @@ LAST = PLACES - 1
 BATCHES = N // P
 HALF = N // 2
 LIST_ROWS = 16
+STRIPS = T // P
 QUADRANT = 32
-WARM_UPS = 2
 FLOPS = 3 * 2 * R * D * N
 
 F32 = mybir.dt.float32
@@ -29,12 +29,11 @@ SLOPES_BEHIND = ((0,), (1, 2))
 DO_GPSIMD = 192
 DO_VECTOR = 48
 GPSIMD_STRIPS = 6
-LAST_RUNS = ((0, 2), (2, 8), (8, 16))
-PIECES = ((0, 2), (2, 4), (4, 6), (6, 8), (8, 10), (10, 12), (12, 14), (14, 15), (15, 16))
-VECTOR_WEAVES = (3,)
-STORE_BEHIND = {1: (0, 4), 3: (4, 8), 5: (8, 12), 6: (12, 14), 8: (14, 16)}
+LAST_RUNS = ((0, 2), (2, 8), (8, STRIPS))
+PIECES = ((0, 2), (2, 4), (4, 6), (6, 8), (8, 10), (10, 12), (12, 14), (14, 15), (15, STRIPS))
+VECTOR_PIECE = 3
+STORE_ENDS = (4, 8, 12, 14, STRIPS)
 SCALE_BANDS = 4
-QUANT_TOKENS = T // SCALE_BANDS // 2
 
 
 def tile_attend_gat_pl_sig_k_kernel(tc, qT, kT, vT, doT, rw, qm, offs, out_0, out_1, out_2):
@@ -78,7 +77,8 @@ def tile_attend_gat_pl_sig_k_kernel(tc, qT, kT, vT, doT, rw, qm, offs, out_0, ou
         def flat(grouped, c0, c1):
             return grouped[:, c0:c1, :].rearrange("p n t -> p (n t)")
 
-        halves = (slice(0, HALF), slice(HALF, N))
+        halves = first, second = slice(0, HALF), slice(HALF, N)
+        whole = slice(0, N)
 
         def entries(cols):
             return offsets[:, cols.start // LIST_ROWS : cols.stop // LIST_ROWS]
@@ -139,7 +139,7 @@ def tile_attend_gat_pl_sig_k_kernel(tc, qT, kT, vT, doT, rw, qm, offs, out_0, ou
             nc.scalar.activation(out=square[:], in_=tanh[:], func=ACT.Square)
             squares.append(square)
 
-        v_grouped = sb.tile([P, N, PLACES], BF16, name="v_grouped", tag="v_grouped", align_bytes=64)
+        v_grouped = sb.tile([P, N, PLACES], BF16, name="v_grouped", align_bytes=64)
         v_first = sb.tile([P, 2, N], BF16, name="v_first", align_bytes=64)
         slopes = []
         for t in range(LAST):
@@ -152,24 +152,25 @@ def tile_attend_gat_pl_sig_k_kernel(tc, qT, kT, vT, doT, rw, qm, offs, out_0, ou
                 some = sb.tile([P, len(batches), R], F32, name="slopes%d" % t, tag="slopes%d" % t, align_bytes=64)
                 for i, b in enumerate(batches):
                     nc.vector.scalar_tensor_tensor(
-                        out=some[:, i, :], in0=squares[b][:], scalar=1.0, in1=gate_row[:], op0=ALU.subtract, op1=ALU.mult
+                        out=some[:, i, :],
+                        in0=squares[b][:],
+                        scalar=1.0,
+                        in1=gate_row[:],
+                        op0=ALU.subtract,
+                        op1=ALU.mult,
                     )
                     slopes.append(some[:, i, :])
         shifted = sb.tile([P, R], F32, name="shifted", tag="square%d" % SLOPES_BEHIND[-1][-1], align_bytes=64)
         nc.gpsimd.tensor_scalar(
             out=shifted[:], in0=squares[BATCHES - 1][:], scalar1=1.0, scalar2=-1.0, op0=ALU.mult, op1=ALU.add
         )
-        last_slope = sb.tile([P, R], F32, name="last_slope", tag="last_slope", align_bytes=64)
+        last_slope = sb.tile([P, R], F32, name="last_slope", align_bytes=64)
         nc.gpsimd.tensor_tensor(out=last_slope[:], in0=shifted[:], in1=gate_row[:], op=ALU.mult)
         slopes.append(last_slope[:])
         for cols in halves:
             nc.vector.tensor_copy(out=v_grouped[:, cols, LAST], in_=v_pool[LAST][:].indirect(entries(cols)))
         v_mx = [mx_tiles("v0", HALF)]
         quantize(v_mx[0], E4M3, 0, HALF, flat(v_grouped, 0, HALF))
-
-        for b in range(WARM_UPS):
-            warm = psum.tile([P, R], F32, name="warm", tag="first")
-            product(warm[:], v_mx[0], E4M3, b, q_mx, E4M3)
 
         do_grouped = sb.tile([P, R, PLACES], BF16, name="do_grouped", tag="do_grouped", align_bytes=64)
         do_mx = mx_tiles("do", R)
@@ -194,11 +195,11 @@ def tile_attend_gat_pl_sig_k_kernel(tc, qT, kT, vT, doT, rw, qm, offs, out_0, ou
         v_mx.append(mx_tiles("v1", HALF))
         quantize(v_mx[1], E4M3, 0, HALF, flat(v_grouped, HALF, N))
         dp_first = psum.tile([P, HALF], F32, name="dp_first", tag="first")
-        product(dp_first[:], v_mx[0], E4M3, 0, do_mx, E5M2, halves[0])
+        product(dp_first[:], v_mx[0], E4M3, 0, do_mx, E5M2, first)
         dps = []
         for b in range(BATCHES):
             dp = psum.tile([P, R], F32, name="dp", tag="second")
-            cols = slice(0, R) if b else halves[1]
+            cols = whole if b else second
             product(dp[:, cols], v_mx[b // 2], E4M3, b % 2, do_mx, E5M2, cols)
             dps.append(dp)
 
@@ -214,35 +215,35 @@ def tile_attend_gat_pl_sig_k_kernel(tc, qT, kT, vT, doT, rw, qm, offs, out_0, ou
             for h in range(2)
         ]
 
-        def form_ds(b, cols, turned, tag):
-            ds = sb.tile([P, cols.stop - cols.start], BF16, name=tag + "_ds", tag=tag, align_bytes=64)
-            nc.vector.tensor_tensor(out=ds[:], in0=dp_first[:] if (b, cols) == (0, halves[0]) else dps[b][:, cols], in1=slopes[b][:, cols], op=ALU.mult)
+        def form_ds(b, cols, dp, turned):
+            ds = sb.tile([P, cols.stop - cols.start], BF16, name="ds%d_%d" % (b, cols.start), align_bytes=64)
+            nc.vector.tensor_tensor(out=ds[:], in0=dp, in1=slopes[b][:, cols], op=ALU.mult)
             words = ds[:].bitcast(F32)
             for u in range(cols.start // HALF, cols.stop // HALF):
                 w0 = u * P - cols.start // 2
                 nc.tensor.transpose(turned[:, u, :], words[:, w0 : w0 + P], identity[:])
 
-        def empty_turned(copy, b, turned):
+        def empty_turned(b, turned):
             h, n0 = divmod(b * P, HALF)
-            copy(
+            nc.scalar.copy(
                 out=flat(ds_grouped[h], n0, n0 + P).bitcast(F32).rearrange("p (n u) -> p n u", u=2),
                 in_=turned[:].rearrange("p u n -> p n u"),
             )
 
         for b in range(LAST):
             turned = psum.tile([P, 2, P], F32, name="turned", tag="first")
-            for cols in halves if b < 2 else (slice(0, R),):
-                form_ds(b, cols, turned, "ds%d_%d" % (b, cols.start))
-            empty_turned(nc.scalar.copy, b, turned)
+            for cols in halves if b < 2 else (whole,):
+                form_ds(b, cols, dp_first[:] if (b, cols) == (0, first) else dps[b][:, cols], turned)
+            empty_turned(b, turned)
         qm_first = mx_tiles("qm_first", P, "slopes1")
         quantize(qm_first, E4M3, 0, P, qm_dealt[:, 0, :, :].rearrange("p s t -> p (s t)"))
         turned = psum.tile([P, 2, P], F32, name="turned", tag="first")
-        form_ds(LAST, halves[0], turned, "ds3_0")
-        form_ds(LAST, halves[1], turned, "ds3_1")
-        empty_turned(nc.scalar.copy, LAST, turned)
+        for cols in halves:
+            form_ds(LAST, cols, dps[LAST][:, cols], turned)
+        empty_turned(LAST, turned)
         quantize(ds_mx, E5M2, 0, HALF, flat(ds_grouped[0], 0, HALF))
 
-        accs = [psum.tile([P, N], F32, name="acc", tag="second") for j in range(PLACES)]
+        banks = [psum.tile([P, N], F32, name="acc", tag="second") for j in range(PLACES)]
 
         def empty(copy, src, name):
             dk = sb.tile(list(src.shape), F32, name=name, align_bytes=64)
@@ -258,39 +259,38 @@ def tile_attend_gat_pl_sig_k_kernel(tc, qT, kT, vT, doT, rw, qm, offs, out_0, ou
         def store_plane(j):
             nc.sync.dma_start(out=planes_of(out_0)[:, j, :], in_=windows[j][:])
 
-        product(accs[0][:, halves[0]], qm_first, E4M3, 0, ds_mx, E5M2, halves[0])
-        scalar_scatter(0, halves[0], empty(nc.scalar.copy, accs[0][:, halves[0]], "dk0a")[:])
+        product(banks[0][:, first], qm_first, E4M3, 0, ds_mx, E5M2, first)
+        scalar_scatter(0, first, empty(nc.scalar.copy, banks[0][:, first], "dk_00")[:])
         qm_rest = mx_tiles("qm_rest", D - P, "ds_grouped0")
         quantize(qm_rest, E4M3, 0, 2 * P, qm_dealt[:, 1:LAST, :, :].rearrange("p j s t -> p (j s t)"))
         quantize(qm_rest, E4M3, 2 * P, LAST * P, qm_dealt[:, LAST, :, :].rearrange("p s t -> p (s t)"))
-        first, second = halves
-        product(accs[1][:, first], qm_rest, E4M3, 0, ds_mx, E5M2, first)
-        product(accs[1][:, second], qm_rest, E4M3, 1, ds_mx, E5M2, first)
-        product(accs[2][:, first], qm_rest, E4M3, 2, ds_mx, E5M2, first)
+        product(banks[1][:, first], qm_rest, E4M3, 0, ds_mx, E5M2, first)
+        product(banks[1][:, second], qm_rest, E4M3, 1, ds_mx, E5M2, first)
+        product(banks[2][:, first], qm_rest, E4M3, 2, ds_mx, E5M2, first)
         for n0 in (0, P):
             quantize(ds_mx, E5M2, HALF + n0, HALF + n0 + P, flat(ds_grouped[1], n0, n0 + P))
-        product(accs[0][:, second], qm_first, E4M3, 0, ds_mx, E5M2, second)
-        product(accs[2][:, second], qm_rest, E4M3, 0, ds_mx, E5M2, second)
-        product(accs[LAST][:, first], qm_rest, E4M3, 1, ds_mx, E5M2, second)
-        product(accs[LAST][:, second], qm_rest, E4M3, 2, ds_mx, E5M2, second)
-        dk1a2a = empty(nc.vector.tensor_copy, accs[1][:], "dk1a2a")
-        dk0b = empty(nc.vector.tensor_copy, accs[0][:, second], "dk0b")
-        dk3a1b = empty(nc.vector.tensor_copy, accs[2][:], "dk3a1b")
-        dk2b = empty(nc.vector.tensor_copy, accs[LAST][:, first], "dk2b")
-        scalar_scatter(1, first, dk1a2a[:, first])
-        vector_scatter(0, second, dk0b[:])
+        product(banks[0][:, second], qm_first, E4M3, 0, ds_mx, E5M2, second)
+        product(banks[2][:, second], qm_rest, E4M3, 0, ds_mx, E5M2, second)
+        product(banks[LAST][:, first], qm_rest, E4M3, 1, ds_mx, E5M2, second)
+        product(banks[LAST][:, second], qm_rest, E4M3, 2, ds_mx, E5M2, second)
+
+        dk_10_20 = empty(nc.vector.tensor_copy, banks[1][:], "dk_10_20")
+        dk_01 = empty(nc.vector.tensor_copy, banks[0][:, second], "dk_01")
+        dk_30_11 = empty(nc.vector.tensor_copy, banks[2][:], "dk_30_11")
+        dk_21 = empty(nc.vector.tensor_copy, banks[LAST][:, first], "dk_21")
+        scalar_scatter(1, first, dk_10_20[:, first])
+        vector_scatter(0, second, dk_01[:])
         store_plane(0)
-        vector_scatter(1, second, dk3a1b[:, second])
+        vector_scatter(1, second, dk_30_11[:, second])
         store_plane(1)
-        dk3b = empty(nc.vector.tensor_copy, accs[LAST][:, second], "dk3b")
-        scalar_scatter(2, first, dk1a2a[:, second])
-        scalar_scatter(LAST, first, dk3a1b[:, first])
-        scalar_scatter(2, second, dk2b[:])
+        dk_31 = empty(nc.vector.tensor_copy, banks[LAST][:, second], "dk_31")
+        scalar_scatter(2, first, dk_10_20[:, second])
+        scalar_scatter(LAST, first, dk_30_11[:, first])
+        scalar_scatter(2, second, dk_21[:])
         store_plane(2)
-        scalar_scatter(LAST, second, dk3b[:])
+        scalar_scatter(LAST, second, dk_31[:])
         store_plane(LAST)
 
-        strips = T // P
         pairs = sb.tile([P, T * PLACES], BF16, name="pairs", align_bytes=64)
 
         def strip_range(s0, s1):
@@ -303,17 +303,17 @@ def tile_attend_gat_pl_sig_k_kernel(tc, qT, kT, vT, doT, rw, qm, offs, out_0, ou
                 in_=windows[j][:, s0 * P : s1 * P].rearrange("p (s n) -> p s n", n=P),
             )
 
-        last = GPSIMD_STRIPS - 1
-        round_plane(gpsimd_round, 0, 0, last)
+        shared = GPSIMD_STRIPS - 1
+        round_plane(gpsimd_round, 0, 0, shared)
         gpsimd_round(
-            out=strip_range(last, last + 1)[:, 0 : 2 * P].rearrange("p (n e) -> p n e", e=2),
-            in_=windows[0][:, last * P : (last + 1) * P].unsqueeze(2).to_broadcast([P, P, 2]),
+            out=strip_range(shared, shared + 1)[:, 0 : 2 * P].rearrange("p (n e) -> p n e", e=2),
+            in_=windows[0][:, shared * P : (shared + 1) * P].unsqueeze(2).to_broadcast([P, P, 2]),
         )
-        round_plane(nc.vector.tensor_copy, 0, GPSIMD_STRIPS, strips)
-        round_plane(nc.vector.tensor_copy, 1, GPSIMD_STRIPS, strips)
+        round_plane(nc.vector.tensor_copy, 0, GPSIMD_STRIPS, STRIPS)
+        round_plane(nc.vector.tensor_copy, 1, GPSIMD_STRIPS, STRIPS)
         round_plane(nc.vector.tensor_copy, 1, 0, GPSIMD_STRIPS)
-        round_plane(nc.vector.tensor_copy, 2, 0, strips // 2)
-        round_plane(nc.vector.tensor_copy, 2, strips // 2, strips)
+        round_plane(nc.vector.tensor_copy, 2, 0, STRIPS // 2)
+        round_plane(nc.vector.tensor_copy, 2, STRIPS // 2, STRIPS)
         for s0, s1 in LAST_RUNS:
             round_plane(nc.vector.tensor_copy, LAST, s0, s1)
 
@@ -327,13 +327,14 @@ def tile_attend_gat_pl_sig_k_kernel(tc, qT, kT, vT, doT, rw, qm, offs, out_0, ou
 
         def weave(c):
             s0, s1 = PIECES[c]
-            copy = nc.vector.tensor_copy if c in VECTOR_WEAVES else nc.scalar.copy
+            copy = nc.vector.tensor_copy if c == VECTOR_PIECE else nc.scalar.copy
             copy(
                 out=out_grouped[c][:].bitcast(F32).rearrange("p (s n u) -> p s n u", n=P, u=2),
                 in_=strip_range(s0, s1).bitcast(F32).rearrange("p (s u n) -> p s n u", u=2, n=P),
             )
 
         weave(0)
+        stored = 0
         for c, (s0, s1) in enumerate(PIECES):
             if c + 1 < len(PIECES):
                 weave(c + 1)
@@ -343,13 +344,12 @@ def tile_attend_gat_pl_sig_k_kernel(tc, qT, kT, vT, doT, rw, qm, offs, out_0, ou
                 scales=out_scales[PLACES * a : P, b0 : b0 + (s1 - s0) * P],
                 in_=out_grouped[c][:],
             )
-            if c in STORE_BEHIND:
-                c0, c1 = STORE_BEHIND[c][0] * P, STORE_BEHIND[c][1] * P
-                nc.sync.dma_start(out=words_out[:, c0:c1], in_=out_codes[:, c0:c1].bitcast(I32))
+            if s1 in STORE_ENDS:
+                nc.sync.dma_start(out=words_out[:, stored : s1 * P], in_=out_codes[:, stored : s1 * P].bitcast(I32))
+                stored = s1 * P
         for q in range(P // QUADRANT):
-            queue = nc.sync
             rows = out_2[0, PLACES * q : PLACES * (q + 1), :].bitcast(I32)
-            queue.dma_start(
+            nc.sync.dma_start(
                 out=rows.rearrange("r (a c) -> a r c", a=SCALE_BANDS),
                 in_=out_scales[QUADRANT * q : QUADRANT * q + PLACES * SCALE_BANDS, :].bitcast(I32),
             )

@@ -194,6 +194,8 @@ def tile_attend_gat_pl_sig_k_kernel(tc, qT, kT, vT, doT, rw, qm, offs, out_0, ou
 
         v_mx.append(mx_tiles("v1", HALF))
         quantize(v_mx[1], E4M3, 0, HALF, flat(v_grouped, HALF, N))
+        warm = psum.tile([P, R], F32, name="warm", tag="first")
+        product(warm[:], v_mx[1], E4M3, 0, q_mx, E4M3)
         dp_first = psum.tile([P, HALF], F32, name="dp_first", tag="first")
         product(dp_first[:], v_mx[0], E4M3, 0, do_mx, E5M2, first)
         dps = []

@@ -1,7 +1,6 @@
 from contextlib import ExitStack
 
 import concourse.mybir as mybir
-from concourse.masks import make_identity
 
 N, T, D, R = 512, 2048, 512, 512
 P = 128
@@ -26,12 +25,13 @@ ALU = mybir.AluOpType
 ACT = mybir.ActivationFunctionType
 
 SLOPES_BEHIND = ((0,), (1, 2))
-DO_GPSIMD = 192
-DO_VECTOR = 48
-GPSIMD_STRIPS = 6
-LAST_RUNS = ((0, 2), (2, 8), (8, STRIPS))
+DO_GPSIMD = 48
+DO_VECTOR = 80
+QM_VECTOR = 32
+QM_GPSIMD = 68
+GPSIMD_STRIPS = 10
+SCALAR_STRIPS = 2
 PIECES = ((0, 2), (2, 4), (4, 6), (6, 8), (8, 10), (10, 12), (12, 14), (14, 15), (15, STRIPS))
-VECTOR_PIECE = 3
 STORE_ENDS = (4, 8, 12, 14, STRIPS)
 SCALE_BANDS = 4
 
@@ -62,7 +62,7 @@ def tile_attend_gat_pl_sig_k_kernel(tc, qT, kT, vT, doT, rw, qm, offs, out_0, ou
         def gpsimd_round(out, in_):
             nc.gpsimd.tensor_scalar(out=out, in0=in_, scalar1=1.0, scalar2=0.0, op0=ALU.mult, op1=ALU.add)
 
-        def product(out, lhs, lhs_fmt, j, rhs, rhs_fmt, moving=slice(0, N)):
+        def product(out, lhs, lhs_fmt, j, rhs, rhs_fmt, moving):
             cols = slice(j * P, (j + 1) * P)
             nc.tensor.matmul_mx(
                 out=out,
@@ -75,13 +75,25 @@ def tile_attend_gat_pl_sig_k_kernel(tc, qT, kT, vT, doT, rw, qm, offs, out_0, ou
             )
 
         def flat(grouped, c0, c1):
-            return grouped[:, c0:c1, :].rearrange("p n t -> p (n t)")
+            return grouped[:, c0 * PLACES : c1 * PLACES]
+
+        def place(grouped, cols, t):
+            return grouped[:].rearrange("p (n t) -> p n t", t=PLACES)[:, cols, t]
+
+        def deal(copy, dealt, raw, t0, s0, s1):
+            planes = raw.shape[1]
+            copy(
+                out=dealt[:].rearrange("p (j s t) -> p s j t", j=PLACES, t=PLACES)[:, s0:s1, :, t0 : t0 + planes],
+                in_=raw[:].rearrange("p t (s j) -> p s j t", j=PLACES)[:, s0:s1, :, :],
+            )
 
         halves = first, second = slice(0, HALF), slice(HALF, N)
-        whole = slice(0, N)
 
         def entries(cols):
             return offsets[:, cols.start // LIST_ROWS : cols.stop // LIST_ROWS]
+
+        def batch(b):
+            return slice(b * P, (b + 1) * P)
 
         q_raw = load("q_raw", planes_of(qT[0]))
         offsets = sb.tile([P, N // LIST_ROWS], U16, name="offsets")
@@ -91,62 +103,61 @@ def tile_attend_gat_pl_sig_k_kernel(tc, qT, kT, vT, doT, rw, qm, offs, out_0, ou
         k_pool = [load("k_pool%d" % t, planes_of(kT)[:, t, :]) for t in range(PLACES)]
         v_pool = [load("v_pool%d" % t, planes_of(vT)[:, t, :]) for t in range(PLACES)]
         do_raw = [load("do_raw%d" % w, planes_of(doT[0])[:, 2 * w : 2 * w + 2, :]) for w in range(2)]
-        qm_raw = load("qm_raw", planes_of(qm[0]))
+        qm_raw = [load("qm_raw%d" % w, planes_of(qm[0])[:, 2 * w : 2 * w + 2, :]) for w in range(2)]
 
         windows = [sb.tile([P, T], F32, name="window%d" % j, align_bytes=64) for j in range(PLACES)]
         for window in windows[:LAST]:
             nc.vector.memset(window[:], 0.0)
-
-        ds_mx = mx_tiles("ds", N)
-        identity = sb.tile([P, P], F32, name="identity", align_bytes=64)
-        make_identity(nc, identity[:])
         nc.gpsimd.memset(windows[LAST][:], 0.0)
 
-        gate_bank = psum.tile([P, PLACES, P], F32, name="gate_bank", tag="second")
-        for j in range(PLACES):
-            nc.tensor.transpose(gate_bank[:, j, :], gate[:, j : j + 1].to_broadcast([P, P]), identity[:])
-        gate_row = sb.tile([P, R], F32, name="gate_row", align_bytes=64)
+        gates = sb.tile([P, P, PLACES], F32, name="gates", align_bytes=64)
         nc.scalar.activation(
-            out=gate_row[:].rearrange("p (u s e) -> p u s e", u=2, e=2),
-            in_=gate_bank[:].rearrange("p (u e) s -> p u s e", u=2),
-            func=ACT.Copy,
-            scale=-0.25,
+            out=gates[:], in_=gate[:].unsqueeze(1).to_broadcast([P, P, PLACES]), func=ACT.Copy, scale=-0.25
         )
+        gate_row = gates[:].rearrange("p n j -> p (n j)")
 
-        q_grouped = sb.tile([P, R, PLACES], BF16, name="q_grouped", align_bytes=64)
-        nc.scalar.copy(
-            out=q_grouped[:].rearrange("p (u s e) t -> p s u t e", u=2, e=2),
-            in_=q_raw[:].rearrange("p t (s u e) -> p s u t e", u=2, e=2),
-        )
+        q_dealt = sb.tile([P, R * PLACES], BF16, name="q_dealt", align_bytes=64)
+        deal(nc.scalar.copy, q_dealt, q_raw, 0, 0, P)
         q_mx = mx_tiles("q", R)
-        quantize(q_mx, E4M3, 0, R, flat(q_grouped, 0, R))
+        quantize(q_mx, E4M3, 0, R, q_dealt[:])
 
-        k_grouped = sb.tile([P, N, PLACES], BF16, name="k_grouped", align_bytes=64)
+        k_grouped = sb.tile([P, N * PLACES], BF16, name="k_grouped", align_bytes=64)
         for t in range(LAST):
-            nc.vector.tensor_copy(out=k_grouped[:, :, t], in_=k_pool[t][:].indirect(offsets[:]))
+            nc.vector.tensor_copy(out=place(k_grouped, slice(0, N), t), in_=k_pool[t][:].indirect(offsets[:]))
         k_mx = mx_tiles("k", N)
         for cols in halves:
-            nc.vector.tensor_copy(out=k_grouped[:, cols, LAST], in_=k_pool[LAST][:].indirect(entries(cols)))
+            nc.vector.tensor_copy(out=place(k_grouped, cols, LAST), in_=k_pool[LAST][:].indirect(entries(cols)))
             quantize(k_mx, E4M3, cols.start, cols.stop, flat(k_grouped, cols.start, cols.stop))
+
+        def batch_product(name, tag, lhs, lhs_fmt, rhs, moving):
+            bank = psum.tile([P, PLACES, P], F32, name=name, tag=tag)
+            for j in range(PLACES):
+                product(bank[:, j, :], lhs, lhs_fmt, j, rhs, E4M3, moving)
+            return bank[:].rearrange("p j n -> p n j")
+
+        def by_place(row):
+            return row.rearrange("p (n j) -> p n j", j=PLACES)
 
         squares = []
         for b in range(BATCHES):
-            score = psum.tile([P, R], F32, name="score", tag="first")
-            product(score[:], k_mx, E4M3, b, q_mx, E4M3)
+            score = batch_product("score", "first", q_mx, E4M3, k_mx, batch(b))
             tanh = sb.tile([P, R], F32, name="tanh%d" % b, align_bytes=64)
-            nc.scalar.activation(out=tanh[:], in_=score[:], func=ACT.Tanh, scale=0.5)
+            nc.scalar.activation(out=by_place(tanh[:]), in_=score, func=ACT.Tanh, scale=0.5)
             square = sb.tile([P, R], F32, name="square%d" % b, tag="square%d" % b, align_bytes=64)
             nc.scalar.activation(out=square[:], in_=tanh[:], func=ACT.Square)
             squares.append(square)
 
-        v_grouped = sb.tile([P, N, PLACES], BF16, name="v_grouped", align_bytes=64)
+        v_grouped = sb.tile([P, N * PLACES], BF16, name="v_grouped", align_bytes=64)
         v_first = sb.tile([P, 2, N], BF16, name="v_first", align_bytes=64)
         slopes = []
         for t in range(LAST):
-            dst = v_first[:, t, :] if t < 2 else v_grouped[:, :, t]
+            dst = v_first[:, t, :] if t < 2 else place(v_grouped, slice(0, N), t)
             nc.vector.tensor_copy(out=dst, in_=v_pool[t][:].indirect(offsets[:]))
             if t == 1:
-                nc.scalar.copy(out=v_grouped[:, :, 0:2], in_=v_first[:].rearrange("p t n -> p n t"))
+                nc.scalar.copy(
+                    out=v_grouped[:].rearrange("p (n t) -> p n t", t=PLACES)[:, :, 0:2],
+                    in_=v_first[:].rearrange("p t n -> p n t"),
+                )
             if t < 2:
                 batches = SLOPES_BEHIND[t]
                 some = sb.tile([P, len(batches), R], F32, name="slopes%d" % t, tag="slopes%d" % t, align_bytes=64)
@@ -155,7 +166,7 @@ def tile_attend_gat_pl_sig_k_kernel(tc, qT, kT, vT, doT, rw, qm, offs, out_0, ou
                         out=some[:, i, :],
                         in0=squares[b][:],
                         scalar=1.0,
-                        in1=gate_row[:],
+                        in1=gate_row,
                         op0=ALU.subtract,
                         op1=ALU.mult,
                     )
@@ -165,138 +176,124 @@ def tile_attend_gat_pl_sig_k_kernel(tc, qT, kT, vT, doT, rw, qm, offs, out_0, ou
             out=shifted[:], in0=squares[BATCHES - 1][:], scalar1=1.0, scalar2=-1.0, op0=ALU.mult, op1=ALU.add
         )
         last_slope = sb.tile([P, R], F32, name="last_slope", align_bytes=64)
-        nc.gpsimd.tensor_tensor(out=last_slope[:], in0=shifted[:], in1=gate_row[:], op=ALU.mult)
+        nc.gpsimd.tensor_tensor(out=last_slope[:], in0=shifted[:], in1=gate_row, op=ALU.mult)
         slopes.append(last_slope[:])
         for cols in halves:
-            nc.vector.tensor_copy(out=v_grouped[:, cols, LAST], in_=v_pool[LAST][:].indirect(entries(cols)))
+            nc.vector.tensor_copy(out=place(v_grouped, cols, LAST), in_=v_pool[LAST][:].indirect(entries(cols)))
         v_mx = [mx_tiles("v0", HALF)]
         quantize(v_mx[0], E4M3, 0, HALF, flat(v_grouped, 0, HALF))
 
-        do_grouped = sb.tile([P, R, PLACES], BF16, name="do_grouped", tag="do_grouped", align_bytes=64)
-        do_mx = mx_tiles("do", R)
-
-        def place_pair(copy, w, c0, c1):
-            u, s0 = divmod(c0 // 2, P)
-            s1 = s0 + (c1 - c0) // 2
-            copy(
-                out=do_grouped[:, c0:c1, 2 * w : 2 * w + 2].rearrange("p (s e) t -> p s e t", e=2),
-                in_=do_raw[w][:].rearrange("p t (s u e) -> p u s e t", u=2, e=2)[:, u, s0:s1, :, :],
-            )
-
-        place_pair(nc.scalar.copy, 0, 0, HALF)
-        place_pair(nc.scalar.copy, 0, HALF, R - DO_GPSIMD)
-        place_pair(gpsimd_round, 0, R - DO_GPSIMD, R)
-        place_pair(nc.vector.tensor_copy, 1, 0, HALF)
-        place_pair(nc.vector.tensor_copy, 1, HALF, HALF + DO_VECTOR)
-        place_pair(nc.scalar.copy, 1, HALF + DO_VECTOR, R)
-        for cols in halves:
-            quantize(do_mx, E5M2, cols.start, cols.stop, flat(do_grouped, cols.start, cols.stop))
-
-        v_mx.append(mx_tiles("v1", HALF))
+        do_dealt = sb.tile([P, R * PLACES], BF16, name="do_dealt", align_bytes=64)
+        do_mx = [mx_tiles("do%d" % j, P) for j in range(PLACES)]
+        deal(nc.scalar.copy, do_dealt, do_raw[0], 0, 0, P - DO_GPSIMD)
+        deal(gpsimd_round, do_dealt, do_raw[0], 0, P - DO_GPSIMD, P)
+        deal(nc.vector.tensor_copy, do_dealt, do_raw[1], 2, 0, DO_VECTOR)
+        deal(nc.scalar.copy, do_dealt, do_raw[1], 2, DO_VECTOR, P)
+        for j in range(PLACES):
+            quantize(do_mx[j], E5M2, 0, P, flat(do_dealt, P * j, P * (j + 1)))
+        v_mx.append(mx_tiles("v1", HALF, "v1_codes"))
         quantize(v_mx[1], E4M3, 0, HALF, flat(v_grouped, HALF, N))
-        warm = psum.tile([P, R], F32, name="warm", tag="first")
-        product(warm[:], v_mx[1], E4M3, 0, q_mx, E4M3)
-        dp_first = psum.tile([P, HALF], F32, name="dp_first", tag="first")
-        product(dp_first[:], v_mx[0], E4M3, 0, do_mx, E5M2, first)
+
         dps = []
         for b in range(BATCHES):
-            dp = psum.tile([P, R], F32, name="dp", tag="second")
-            cols = whole if b else second
-            product(dp[:, cols], v_mx[b // 2], E4M3, b % 2, do_mx, E5M2, cols)
-            dps.append(dp)
+            bank = psum.tile([P, PLACES, P], F32, name="dp", tag="second")
+            for j in range(PLACES):
+                product(bank[:, j, :], do_mx[j], E5M2, 0, v_mx[b // 2], E4M3, batch(b % 2))
+            dps.append(bank[:].rearrange("p j n -> p n j"))
 
-        qm_dealt = sb.tile([P, PLACES, P, PLACES], BF16, name="qm_dealt", tag="do_grouped", align_bytes=64)
-        for copy, s0, s1 in ((nc.scalar.copy, 0, P // 2), (gpsimd_round, P // 2, P)):
-            copy(
-                out=qm_dealt[:, :, s0:s1, :].rearrange("p j s t -> p s j t"),
-                in_=qm_raw[:].rearrange("p t (s j) -> p s j t", j=PLACES)[:, s0:s1, :, :],
-            )
+        qm_dealt = sb.tile([P, D * PLACES], BF16, name="qm_dealt", align_bytes=64)
+        deal(nc.vector.tensor_copy, qm_dealt, qm_raw[0], 0, 0, QM_VECTOR)
+        deal(nc.scalar.copy, qm_dealt, qm_raw[0], 0, QM_VECTOR, P)
+        deal(nc.scalar.copy, qm_dealt, qm_raw[1], 2, 0, P - QM_GPSIMD)
+        deal(gpsimd_round, qm_dealt, qm_raw[1], 2, P - QM_GPSIMD, P)
 
-        ds_grouped = [
-            sb.tile([P, HALF, PLACES], BF16, name="ds_grouped%d" % h, tag="ds_grouped%d" % h, align_bytes=64)
-            for h in range(2)
-        ]
+        ds_grouped = [sb.tile([P, R], BF16, name="ds_grouped%d" % b, align_bytes=64)[:] for b in range(2)]
+        ds_grouped = ds_grouped + [flat(qm_dealt, 0, P), flat(qm_dealt, P, 2 * P)]
+        ds_mx = mx_tiles("ds", N)
 
-        def form_ds(b, cols, dp, turned):
-            ds = sb.tile([P, cols.stop - cols.start], BF16, name="ds%d_%d" % (b, cols.start), align_bytes=64)
-            nc.vector.tensor_tensor(out=ds[:], in0=dp, in1=slopes[b][:, cols], op=ALU.mult)
-            words = ds[:].bitcast(F32)
-            for u in range(cols.start // HALF, cols.stop // HALF):
-                w0 = u * P - cols.start // 2
-                nc.tensor.transpose(turned[:, u, :], words[:, w0 : w0 + P], identity[:])
+        def form_ds(b):
+            nc.vector.tensor_tensor(out=by_place(ds_grouped[b]), in0=dps[b], in1=by_place(slopes[b]), op=ALU.mult)
 
-        def empty_turned(b, turned):
-            h, n0 = divmod(b * P, HALF)
-            nc.scalar.copy(
-                out=flat(ds_grouped[h], n0, n0 + P).bitcast(F32).rearrange("p (n u) -> p n u", u=2),
-                in_=turned[:].rearrange("p u n -> p n u"),
-            )
+        def quantize_ds(b):
+            quantize(ds_mx, E5M2, b * P, (b + 1) * P, ds_grouped[b])
 
-        for b in range(LAST):
-            turned = psum.tile([P, 2, P], F32, name="turned", tag="first")
-            for cols in halves if b < 2 else (whole,):
-                form_ds(b, cols, dp_first[:] if (b, cols) == (0, first) else dps[b][:, cols], turned)
-            empty_turned(b, turned)
-        qm_first = mx_tiles("qm_first", P, "slopes1")
-        quantize(qm_first, E4M3, 0, P, qm_dealt[:, 0, :, :].rearrange("p s t -> p (s t)"))
-        turned = psum.tile([P, 2, P], F32, name="turned", tag="first")
-        for cols in halves:
-            form_ds(LAST, cols, dps[LAST][:, cols], turned)
-        empty_turned(LAST, turned)
-        quantize(ds_mx, E5M2, 0, HALF, flat(ds_grouped[0], 0, HALF))
+        qm_mx = [mx_tiles("qm%d" % j, P) for j in range(PLACES)]
 
-        banks = [psum.tile([P, N], F32, name="acc", tag="second") for j in range(PLACES)]
+        def quantize_qm(j):
+            quantize(qm_mx[j], E4M3, 0, P, flat(qm_dealt, j * P, (j + 1) * P))
 
-        def empty(copy, src, name):
-            dk = sb.tile(list(src.shape), F32, name=name, align_bytes=64)
-            copy(out=dk[:], in_=src)
-            return dk
+        banks = {}
 
-        def scalar_scatter(j, cols, src):
-            nc.scalar.activation(out=windows[j][:].indirect(entries(cols)), in_=src, func=ACT.Copy)
+        def gradient(j, h, ring):
+            banks[j, h] = psum.tile([P, HALF], F32, name="acc", tag=ring)
+            if j:
+                product(banks[j, h][:], qm_mx[j], E4M3, 0, ds_mx, E5M2, halves[h])
+            else:
+                for i in range(2):
+                    product(banks[j, h][:, batch(i)], qm_mx[j], E4M3, 0, ds_mx, E5M2, batch(2 * h + i))
 
-        def vector_scatter(j, cols, src):
-            nc.vector.tensor_copy(out=windows[j][:].indirect(entries(cols)), in_=src)
+        dk = {}
+
+        def empty(copy, j, h):
+            dk[j, h] = sb.tile([P, HALF], F32, name="dk%d%d" % (j, h), tag="dk%d%d" % (j, h), align_bytes=64)
+            copy(out=dk[j, h][:], in_=banks[j, h][:])
+
+        def scalar_scatter(j, h):
+            nc.scalar.activation(out=windows[j][:].indirect(entries(halves[h])), in_=dk[j, h][:], func=ACT.Copy)
+
+        def vector_scatter(j, h):
+            nc.vector.tensor_copy(out=windows[j][:].indirect(entries(halves[h])), in_=dk[j, h][:])
 
         def store_plane(j):
             nc.sync.dma_start(out=planes_of(out_0)[:, j, :], in_=windows[j][:])
 
-        product(banks[0][:, first], qm_first, E4M3, 0, ds_mx, E5M2, first)
-        scalar_scatter(0, first, empty(nc.scalar.copy, banks[0][:, first], "dk_00")[:])
-        qm_rest = mx_tiles("qm_rest", D - P, "ds_grouped0")
-        quantize(qm_rest, E4M3, 0, 2 * P, qm_dealt[:, 1:LAST, :, :].rearrange("p j s t -> p (j s t)"))
-        quantize(qm_rest, E4M3, 2 * P, LAST * P, qm_dealt[:, LAST, :, :].rearrange("p s t -> p (s t)"))
-        product(banks[1][:, first], qm_rest, E4M3, 0, ds_mx, E5M2, first)
-        product(banks[1][:, second], qm_rest, E4M3, 1, ds_mx, E5M2, first)
-        product(banks[2][:, first], qm_rest, E4M3, 2, ds_mx, E5M2, first)
-        for n0 in (0, P):
-            quantize(ds_mx, E5M2, HALF + n0, HALF + n0 + P, flat(ds_grouped[1], n0, n0 + P))
-        product(banks[0][:, second], qm_first, E4M3, 0, ds_mx, E5M2, second)
-        product(banks[2][:, second], qm_rest, E4M3, 0, ds_mx, E5M2, second)
-        product(banks[LAST][:, first], qm_rest, E4M3, 1, ds_mx, E5M2, second)
-        product(banks[LAST][:, second], qm_rest, E4M3, 2, ds_mx, E5M2, second)
-
-        dk_10_20 = empty(nc.vector.tensor_copy, banks[1][:], "dk_10_20")
-        dk_01 = empty(nc.vector.tensor_copy, banks[0][:, second], "dk_01")
-        dk_30_11 = empty(nc.vector.tensor_copy, banks[2][:], "dk_30_11")
-        dk_21 = empty(nc.vector.tensor_copy, banks[LAST][:, first], "dk_21")
-        scalar_scatter(1, first, dk_10_20[:, first])
-        vector_scatter(0, second, dk_01[:])
+        form_ds(0)
+        form_ds(1)
+        quantize_ds(0)
+        quantize_qm(0)
+        quantize_ds(1)
+        gradient(0, 0, "first")
+        empty(nc.scalar.copy, 0, 0)
+        scalar_scatter(0, 0)
+        quantize_qm(1)
+        form_ds(2)
+        form_ds(3)
+        quantize_ds(2)
+        quantize_qm(2)
+        quantize_ds(3)
+        quantize_qm(LAST)
+        for j, h in ((1, 0), (0, 1), (2, 0)):
+            gradient(j, h, "first")
+        for j, h in ((1, 1), (LAST, 0), (2, 1), (LAST, 1)):
+            gradient(j, h, "second")
+        for j, h in ((1, 0), (0, 1), (2, 0)):
+            empty(nc.vector.tensor_copy, j, h)
+        scalar_scatter(1, 0)
+        vector_scatter(0, 1)
         store_plane(0)
-        vector_scatter(1, second, dk_30_11[:, second])
+        scalar_scatter(2, 0)
+        empty(nc.vector.tensor_copy, 1, 1)
+        empty(nc.vector.tensor_copy, LAST, 0)
+        vector_scatter(1, 1)
         store_plane(1)
-        dk_31 = empty(nc.vector.tensor_copy, banks[LAST][:, second], "dk_31")
-        scalar_scatter(2, first, dk_10_20[:, second])
-        scalar_scatter(LAST, first, dk_30_11[:, first])
-        scalar_scatter(2, second, dk_21[:])
+        scalar_scatter(LAST, 0)
+        empty(nc.vector.tensor_copy, 2, 1)
+        empty(nc.vector.tensor_copy, LAST, 1)
+        vector_scatter(2, 1)
         store_plane(2)
-        scalar_scatter(LAST, second, dk_31[:])
+        scalar_scatter(LAST, 1)
         store_plane(LAST)
 
-        pairs = sb.tile([P, T * PLACES], BF16, name="pairs", align_bytes=64)
+        STRIP = P * PLACES
+        pairs = [
+            sb.tile([P, GPSIMD_STRIPS * STRIP], BF16, name="pairs_low", align_bytes=64),
+            sb.tile([P, (STRIPS - GPSIMD_STRIPS) * STRIP], BF16, name="pairs_high", tag="dk21", align_bytes=64),
+        ]
 
         def strip_range(s0, s1):
-            return pairs[:, s0 * P * PLACES : s1 * P * PLACES]
+            if s0 < GPSIMD_STRIPS:
+                return pairs[0][:, s0 * STRIP : s1 * STRIP]
+            return pairs[1][:, (s0 - GPSIMD_STRIPS) * STRIP : (s1 - GPSIMD_STRIPS) * STRIP]
 
         def round_plane(copy, j, s0, s1):
             u, e = divmod(j, 2)
@@ -305,19 +302,18 @@ def tile_attend_gat_pl_sig_k_kernel(tc, qT, kT, vT, doT, rw, qm, offs, out_0, ou
                 in_=windows[j][:, s0 * P : s1 * P].rearrange("p (s n) -> p s n", n=P),
             )
 
-        shared = GPSIMD_STRIPS - 1
-        round_plane(gpsimd_round, 0, 0, shared)
-        gpsimd_round(
-            out=strip_range(shared, shared + 1)[:, 0 : 2 * P].rearrange("p (n e) -> p n e", e=2),
-            in_=windows[0][:, shared * P : (shared + 1) * P].unsqueeze(2).to_broadcast([P, P, 2]),
-        )
-        round_plane(nc.vector.tensor_copy, 0, GPSIMD_STRIPS, STRIPS)
-        round_plane(nc.vector.tensor_copy, 1, GPSIMD_STRIPS, STRIPS)
-        round_plane(nc.vector.tensor_copy, 1, 0, GPSIMD_STRIPS)
-        round_plane(nc.vector.tensor_copy, 2, 0, STRIPS // 2)
-        round_plane(nc.vector.tensor_copy, 2, STRIPS // 2, STRIPS)
-        for s0, s1 in LAST_RUNS:
-            round_plane(nc.vector.tensor_copy, LAST, s0, s1)
+        split = GPSIMD_STRIPS + SCALAR_STRIPS
+        for j in range(2):
+            round_plane(gpsimd_round, j, 0, GPSIMD_STRIPS)
+        for j in range(2):
+            round_plane(nc.scalar.copy, j, GPSIMD_STRIPS, split)
+        for s0, s1 in ((0, 4), (4, GPSIMD_STRIPS)):
+            for j in (2, LAST):
+                round_plane(nc.vector.tensor_copy, j, s0, s1)
+        for j in range(2):
+            round_plane(nc.vector.tensor_copy, j, split, STRIPS)
+        for j in (2, LAST):
+            round_plane(nc.vector.tensor_copy, j, GPSIMD_STRIPS, STRIPS)
 
         band = T // SCALE_BANDS
         out_codes = sb.tile([P, T], U32, name="out_codes", align_bytes=64)
@@ -329,8 +325,7 @@ def tile_attend_gat_pl_sig_k_kernel(tc, qT, kT, vT, doT, rw, qm, offs, out_0, ou
 
         def weave(c):
             s0, s1 = PIECES[c]
-            copy = nc.vector.tensor_copy if c == VECTOR_PIECE else nc.scalar.copy
-            copy(
+            nc.scalar.copy(
                 out=out_grouped[c][:].bitcast(F32).rearrange("p (s n u) -> p s n u", n=P, u=2),
                 in_=strip_range(s0, s1).bitcast(F32).rearrange("p (s u n) -> p s n u", u=2, n=P),
             )

@@ -110,11 +110,14 @@ def tile_attend_gat_pl_sig_k_kernel(tc, qT, kT, vT, doT, rw, qm, offs, out_0, ou
             nc.vector.memset(window[:], 0.0)
         nc.gpsimd.memset(windows[LAST][:], 0.0)
 
-        gates = sb.tile([P, P, PLACES], F32, name="gates", align_bytes=64)
+        gates = sb.tile([P, P // 2, PLACES, 2], F32, name="gates", align_bytes=64)
         nc.scalar.activation(
-            out=gates[:], in_=gate[:].unsqueeze(1).to_broadcast([P, P, PLACES]), func=ACT.Copy, scale=-0.25
+            out=gates[:],
+            in_=gate[:].unsqueeze(1).unsqueeze(3).to_broadcast([P, P // 2, PLACES, 2]),
+            func=ACT.Copy,
+            scale=-0.25,
         )
-        gate_row = gates[:].rearrange("p n j -> p (n j)")
+        gate_row = gates[:].rearrange("p c j i -> p (c j i)")
 
         q_dealt = sb.tile([P, R * PLACES], BF16, name="q_dealt", align_bytes=64)
         deal(nc.scalar.copy, q_dealt, q_raw, 0, 0, P)
@@ -133,10 +136,10 @@ def tile_attend_gat_pl_sig_k_kernel(tc, qT, kT, vT, doT, rw, qm, offs, out_0, ou
             bank = psum.tile([P, PLACES, P], F32, name=name, tag=tag)
             for j in range(PLACES):
                 product(bank[:, j, :], lhs, lhs_fmt, j, rhs, E4M3, moving)
-            return bank[:].rearrange("p j n -> p n j")
+            return bank[:].rearrange("p j (c i) -> p c j i", i=2)
 
         def by_place(row):
-            return row.rearrange("p (n j) -> p n j", j=PLACES)
+            return row.rearrange("p (c j i) -> p c j i", j=PLACES, i=2)
 
         squares = []
         for b in range(BATCHES):
@@ -199,7 +202,7 @@ def tile_attend_gat_pl_sig_k_kernel(tc, qT, kT, vT, doT, rw, qm, offs, out_0, ou
             bank = psum.tile([P, PLACES, P], F32, name="dp", tag="second")
             for j in range(PLACES):
                 product(bank[:, j, :], do_mx[j], E5M2, 0, v_mx[b // 2], E4M3, batch(b % 2))
-            dps.append(bank[:].rearrange("p j n -> p n j"))
+            dps.append(bank[:].rearrange("p j (c i) -> p c j i", i=2))
 
         qm_dealt = sb.tile([P, D * PLACES], BF16, name="qm_dealt", align_bytes=64)
         deal(nc.vector.tensor_copy, qm_dealt, qm_raw[0], 0, 0, QM_VECTOR)
@@ -212,7 +215,8 @@ def tile_attend_gat_pl_sig_k_kernel(tc, qT, kT, vT, doT, rw, qm, offs, out_0, ou
         ds_mx = mx_tiles("ds", N)
 
         def form_ds(b):
-            nc.vector.tensor_tensor(out=by_place(ds_grouped[b]), in0=dps[b], in1=by_place(slopes[b]), op=ALU.mult)
+            out = ds_grouped[b].rearrange("p (c i j) -> p c j i", i=2, j=PLACES)
+            nc.vector.tensor_tensor(out=out, in0=dps[b], in1=by_place(slopes[b]), op=ALU.mult)
 
         def quantize_ds(b):
             quantize(ds_mx, E5M2, b * P, (b + 1) * P, ds_grouped[b])

@@ -24,11 +24,9 @@ E5M2 = mybir.dt.float8_e5m2_x4
 ALU = mybir.AluOpType
 ACT = mybir.ActivationFunctionType
 
-SLOPES_BEHIND = ((0,), (1, 2))
-DO_GPSIMD = 48
-DO_VECTOR = 80
-QM_VECTOR = 32
-QM_GPSIMD = 68
+SLOPES_BEHIND = ((0,), (1, 2), (3,), ())
+DO_VECTOR = (104, 84)
+QM_VECTOR = (64, 40)
 GPSIMD_STRIPS = 10
 SCALAR_STRIPS = 2
 PIECES = ((0, 2), (2, 4), (4, 6), (6, 8), (8, 10), (10, 12), (12, 14), (14, 15), (15, STRIPS))
@@ -151,51 +149,38 @@ def tile_attend_gat_pl_sig_k_kernel(tc, qT, kT, vT, doT, rw, qm, offs, out_0, ou
             squares.append(square)
 
         v_grouped = sb.tile([P, N * PLACES], BF16, name="v_grouped", align_bytes=64)
-        v_first = sb.tile([P, 2, N], BF16, name="v_first", align_bytes=64)
+        v_second = sb.tile([P, 2, HALF], BF16, name="v_second", align_bytes=64)
         slopes = []
-        for t in range(LAST):
-            dst = v_first[:, t, :] if t < 2 else place(v_grouped, slice(0, N), t)
-            nc.vector.tensor_copy(out=dst, in_=v_pool[t][:].indirect(offsets[:]))
-            if t == 1:
-                nc.scalar.copy(
-                    out=v_grouped[:].rearrange("p (n t) -> p n t", t=PLACES)[:, :, 0:2],
-                    in_=v_first[:].rearrange("p t n -> p n t"),
-                )
+        for t in range(LAST + 1):
             if t < 2:
-                batches = SLOPES_BEHIND[t]
-                some = sb.tile([P, len(batches), R], F32, name="slopes%d" % t, tag="slopes%d" % t, align_bytes=64)
-                for i, b in enumerate(batches):
-                    nc.vector.scalar_tensor_tensor(
-                        out=some[:, i, :],
-                        in0=squares[b][:],
-                        scalar=1.0,
-                        in1=gate_row,
-                        op0=ALU.subtract,
-                        op1=ALU.mult,
-                    )
-                    slopes.append(some[:, i, :])
-        shifted = sb.tile([P, R], F32, name="shifted", tag="square%d" % SLOPES_BEHIND[-1][-1], align_bytes=64)
-        nc.gpsimd.tensor_scalar(
-            out=shifted[:], in0=squares[BATCHES - 1][:], scalar1=1.0, scalar2=-1.0, op0=ALU.mult, op1=ALU.add
+                nc.vector.tensor_copy(out=place(v_grouped, slice(0, N), t), in_=v_pool[t][:].indirect(offsets[:]))
+            else:
+                nc.vector.tensor_copy(out=place(v_grouped, first, t), in_=v_pool[t][:].indirect(entries(first)))
+                nc.scalar.activation(
+                    out=v_second[:, t - 2, :], in_=v_pool[t][:].indirect(entries(second)), func=ACT.Copy
+                )
+            for b in SLOPES_BEHIND[t]:
+                slope = sb.tile([P, R], F32, name="slope%d" % b, align_bytes=64)
+                nc.vector.scalar_tensor_tensor(
+                    out=slope[:], in0=squares[b][:], scalar=1.0, in1=gate_row, op0=ALU.subtract, op1=ALU.mult
+                )
+                slopes.append(slope[:])
+        nc.scalar.copy(
+            out=v_grouped[:].rearrange("p (n t) -> p n t", t=PLACES)[:, second, 2:PLACES],
+            in_=v_second[:].rearrange("p t n -> p n t"),
         )
-        last_slope = sb.tile([P, R], F32, name="last_slope", align_bytes=64)
-        nc.gpsimd.tensor_tensor(out=last_slope[:], in0=shifted[:], in1=gate_row, op=ALU.mult)
-        slopes.append(last_slope[:])
-        for cols in halves:
-            nc.vector.tensor_copy(out=place(v_grouped, cols, LAST), in_=v_pool[LAST][:].indirect(entries(cols)))
-        v_mx = [mx_tiles("v0", HALF)]
+        v_mx = [mx_tiles("v%d" % h, HALF) for h in range(2)]
         quantize(v_mx[0], E4M3, 0, HALF, flat(v_grouped, 0, HALF))
 
         do_dealt = sb.tile([P, R * PLACES], BF16, name="do_dealt", align_bytes=64)
         do_mx = [mx_tiles("do%d" % j, P) for j in range(PLACES)]
-        deal(nc.scalar.copy, do_dealt, do_raw[0], 0, 0, P - DO_GPSIMD)
-        deal(gpsimd_round, do_dealt, do_raw[0], 0, P - DO_GPSIMD, P)
-        deal(nc.vector.tensor_copy, do_dealt, do_raw[1], 2, 0, DO_VECTOR)
-        deal(nc.scalar.copy, do_dealt, do_raw[1], 2, DO_VECTOR, P)
+        deal(nc.vector.tensor_copy, do_dealt, do_raw[0], 0, 0, DO_VECTOR[0])
+        deal(nc.scalar.copy, do_dealt, do_raw[0], 0, DO_VECTOR[0], P)
+        quantize(v_mx[1], E4M3, 0, HALF, flat(v_grouped, HALF, N))
+        deal(nc.vector.tensor_copy, do_dealt, do_raw[1], 2, 0, DO_VECTOR[1])
+        deal(nc.scalar.copy, do_dealt, do_raw[1], 2, DO_VECTOR[1], P)
         for j in range(PLACES):
             quantize(do_mx[j], E5M2, 0, P, flat(do_dealt, P * j, P * (j + 1)))
-        v_mx.append(mx_tiles("v1", HALF, "v1_codes"))
-        quantize(v_mx[1], E4M3, 0, HALF, flat(v_grouped, HALF, N))
 
         dps = []
         for b in range(BATCHES):
@@ -205,10 +190,9 @@ def tile_attend_gat_pl_sig_k_kernel(tc, qT, kT, vT, doT, rw, qm, offs, out_0, ou
             dps.append(bank[:].rearrange("p j (c i) -> p c j i", i=2))
 
         qm_dealt = sb.tile([P, D * PLACES], BF16, name="qm_dealt", align_bytes=64)
-        deal(nc.vector.tensor_copy, qm_dealt, qm_raw[0], 0, 0, QM_VECTOR)
-        deal(nc.scalar.copy, qm_dealt, qm_raw[0], 0, QM_VECTOR, P)
-        deal(nc.scalar.copy, qm_dealt, qm_raw[1], 2, 0, P - QM_GPSIMD)
-        deal(gpsimd_round, qm_dealt, qm_raw[1], 2, P - QM_GPSIMD, P)
+        deal(nc.vector.tensor_copy, qm_dealt, qm_raw[0], 0, 0, QM_VECTOR[0])
+        deal(nc.scalar.copy, qm_dealt, qm_raw[0], 0, QM_VECTOR[0], P)
+        deal(nc.scalar.copy, qm_dealt, qm_raw[1], 2, QM_VECTOR[1], P)
 
         ds_grouped = [sb.tile([P, R], BF16, name="ds_grouped%d" % b, align_bytes=64)[:] for b in range(2)]
         ds_grouped = ds_grouped + [flat(qm_dealt, 0, P), flat(qm_dealt, P, 2 * P)]
@@ -253,6 +237,7 @@ def tile_attend_gat_pl_sig_k_kernel(tc, qT, kT, vT, doT, rw, qm, offs, out_0, ou
 
         form_ds(0)
         form_ds(1)
+        deal(nc.vector.tensor_copy, qm_dealt, qm_raw[1], 2, 0, QM_VECTOR[1])
         quantize_ds(0)
         quantize_qm(0)
         quantize_ds(1)

@@ -85,6 +85,13 @@ def tile_attend_gat_pl_sig_k_kernel(tc, qT, kT, vT, doT, rw, qm, offs, out_0, ou
                 in_=raw[:].rearrange("p t (s j) -> p s j t", j=PLACES)[:, s0:s1, :, :],
             )
 
+        def deal_pair(copy, dealt, raw, t0, s0, s1):
+            c0, c1 = s0 // 2, s1 // 2
+            copy(
+                out=dealt[:].rearrange("p (j c i t) -> p c j i t", j=PLACES, i=2, t=PLACES)[:, c0:c1, :, :, t0 : t0 + 2],
+                in_=raw[:].rearrange("p t (c i j) -> p c j i t", i=2, j=PLACES)[:, c0:c1, :, :, :],
+            )
+
         halves = first, second = slice(0, HALF), slice(HALF, N)
 
         def entries(cols):
@@ -174,11 +181,11 @@ def tile_attend_gat_pl_sig_k_kernel(tc, qT, kT, vT, doT, rw, qm, offs, out_0, ou
 
         do_dealt = sb.tile([P, R * PLACES], BF16, name="do_dealt", align_bytes=64)
         do_mx = [mx_tiles("do%d" % j, P) for j in range(PLACES)]
-        deal(nc.vector.tensor_copy, do_dealt, do_raw[0], 0, 0, DO_VECTOR[0])
-        deal(nc.scalar.copy, do_dealt, do_raw[0], 0, DO_VECTOR[0], P)
+        deal_pair(nc.vector.tensor_copy, do_dealt, do_raw[0], 0, 0, DO_VECTOR[0])
+        deal_pair(nc.scalar.copy, do_dealt, do_raw[0], 0, DO_VECTOR[0], P)
         quantize(v_mx[1], E4M3, 0, HALF, flat(v_grouped, HALF, N))
-        deal(nc.vector.tensor_copy, do_dealt, do_raw[1], 2, 0, DO_VECTOR[1])
-        deal(nc.scalar.copy, do_dealt, do_raw[1], 2, DO_VECTOR[1], P)
+        deal_pair(nc.vector.tensor_copy, do_dealt, do_raw[1], 2, 0, DO_VECTOR[1])
+        deal_pair(nc.scalar.copy, do_dealt, do_raw[1], 2, DO_VECTOR[1], P)
         for j in range(PLACES):
             quantize(do_mx[j], E5M2, 0, P, flat(do_dealt, P * j, P * (j + 1)))
 
@@ -190,9 +197,9 @@ def tile_attend_gat_pl_sig_k_kernel(tc, qT, kT, vT, doT, rw, qm, offs, out_0, ou
             dps.append(bank[:].rearrange("p j (c i) -> p c j i", i=2))
 
         qm_dealt = sb.tile([P, D * PLACES], BF16, name="qm_dealt", align_bytes=64)
-        deal(nc.vector.tensor_copy, qm_dealt, qm_raw[0], 0, 0, QM_VECTOR[0])
-        deal(nc.scalar.copy, qm_dealt, qm_raw[0], 0, QM_VECTOR[0], P)
-        deal(nc.scalar.copy, qm_dealt, qm_raw[1], 2, QM_VECTOR[1], P)
+        deal_pair(nc.vector.tensor_copy, qm_dealt, qm_raw[0], 0, 0, QM_VECTOR[0])
+        deal_pair(nc.scalar.copy, qm_dealt, qm_raw[0], 0, QM_VECTOR[0], P)
+        deal_pair(nc.scalar.copy, qm_dealt, qm_raw[1], 2, QM_VECTOR[1], P)
 
         ds_grouped = [sb.tile([P, R], BF16, name="ds_grouped%d" % b, align_bytes=64)[:] for b in range(2)]
         ds_grouped = ds_grouped + [flat(qm_dealt, 0, P), flat(qm_dealt, P, 2 * P)]
@@ -237,7 +244,7 @@ def tile_attend_gat_pl_sig_k_kernel(tc, qT, kT, vT, doT, rw, qm, offs, out_0, ou
 
         form_ds(0)
         form_ds(1)
-        deal(nc.vector.tensor_copy, qm_dealt, qm_raw[1], 2, 0, QM_VECTOR[1])
+        deal_pair(nc.vector.tensor_copy, qm_dealt, qm_raw[1], 2, 0, QM_VECTOR[1])
         quantize_ds(0)
         quantize_qm(0)
         quantize_ds(1)

@@ -26,9 +26,11 @@ ACT = mybir.ActivationFunctionType
 
 SLOPES_BEHIND = ((0,), (1, 2), (3,), ())
 DO_VECTOR = (104, 84)
-QM_VECTOR = (64, 40)
-GPSIMD_STRIPS = 10
-SCALAR_STRIPS = 2
+QM_VECTOR = 32
+QM_GPSIMD = 56
+GPSIMD_STRIPS = 8
+LAST_RUNS = ((0, 2), (2, 8), (8, STRIPS))
+VECTOR_PIECE = 3
 PIECES = ((0, 2), (2, 4), (4, 6), (6, 8), (8, 10), (10, 12), (12, 14), (14, 15), (15, STRIPS))
 STORE_ENDS = (4, 8, 12, 14, STRIPS)
 SCALE_BANDS = 4
@@ -130,11 +132,26 @@ def tile_attend_gat_pl_sig_k_kernel(tc, qT, kT, vT, doT, rw, qm, offs, out_0, ou
         quantize(q_mx, E4M3, 0, R, q_dealt[:])
 
         k_grouped = sb.tile([P, N * PLACES], BF16, name="k_grouped", align_bytes=64)
-        for t in range(LAST):
-            nc.vector.tensor_copy(out=place(k_grouped, slice(0, N), t), in_=k_pool[t][:].indirect(offsets[:]))
+
+        def gather(grouped, rows, pool, t):
+            if t < 2:
+                nc.vector.tensor_copy(out=place(grouped, slice(0, N), t), in_=pool[t][:].indirect(offsets[:]))
+            else:
+                nc.vector.tensor_copy(out=place(grouped, first, t), in_=pool[t][:].indirect(entries(first)))
+                nc.scalar.activation(out=rows[:, t - 2, :], in_=pool[t][:].indirect(entries(second)), func=ACT.Copy)
+
+        def place_rows(grouped, rows):
+            nc.scalar.copy(
+                out=grouped[:].rearrange("p (n t) -> p n t", t=PLACES)[:, second, 2:PLACES],
+                in_=rows[:].rearrange("p t n -> p n t"),
+            )
+
+        k_rows = sb.tile([P, 2, HALF], BF16, name="k_rows", align_bytes=64)
+        for t in range(PLACES):
+            gather(k_grouped, k_rows, k_pool, t)
+        place_rows(k_grouped, k_rows)
         k_mx = mx_tiles("k", N)
         for cols in halves:
-            nc.vector.tensor_copy(out=place(k_grouped, cols, LAST), in_=k_pool[LAST][:].indirect(entries(cols)))
             quantize(k_mx, E4M3, cols.start, cols.stop, flat(k_grouped, cols.start, cols.stop))
 
         def batch_product(name, tag, lhs, lhs_fmt, rhs, moving):
@@ -159,23 +176,14 @@ def tile_attend_gat_pl_sig_k_kernel(tc, qT, kT, vT, doT, rw, qm, offs, out_0, ou
         v_second = sb.tile([P, 2, HALF], BF16, name="v_second", align_bytes=64)
         slopes = []
         for t in range(LAST + 1):
-            if t < 2:
-                nc.vector.tensor_copy(out=place(v_grouped, slice(0, N), t), in_=v_pool[t][:].indirect(offsets[:]))
-            else:
-                nc.vector.tensor_copy(out=place(v_grouped, first, t), in_=v_pool[t][:].indirect(entries(first)))
-                nc.scalar.activation(
-                    out=v_second[:, t - 2, :], in_=v_pool[t][:].indirect(entries(second)), func=ACT.Copy
-                )
+            gather(v_grouped, v_second, v_pool, t)
             for b in SLOPES_BEHIND[t]:
                 slope = sb.tile([P, R], F32, name="slope%d" % b, align_bytes=64)
                 nc.vector.scalar_tensor_tensor(
                     out=slope[:], in0=squares[b][:], scalar=1.0, in1=gate_row, op0=ALU.subtract, op1=ALU.mult
                 )
                 slopes.append(slope[:])
-        nc.scalar.copy(
-            out=v_grouped[:].rearrange("p (n t) -> p n t", t=PLACES)[:, second, 2:PLACES],
-            in_=v_second[:].rearrange("p t n -> p n t"),
-        )
+        place_rows(v_grouped, v_second)
         v_mx = [mx_tiles("v%d" % h, HALF) for h in range(2)]
         quantize(v_mx[0], E4M3, 0, HALF, flat(v_grouped, 0, HALF))
 
@@ -197,9 +205,10 @@ def tile_attend_gat_pl_sig_k_kernel(tc, qT, kT, vT, doT, rw, qm, offs, out_0, ou
             dps.append(bank[:].rearrange("p j (c i) -> p c j i", i=2))
 
         qm_dealt = sb.tile([P, D * PLACES], BF16, name="qm_dealt", align_bytes=64)
-        deal_pair(nc.vector.tensor_copy, qm_dealt, qm_raw[0], 0, 0, QM_VECTOR[0])
-        deal_pair(nc.scalar.copy, qm_dealt, qm_raw[0], 0, QM_VECTOR[0], P)
-        deal_pair(nc.scalar.copy, qm_dealt, qm_raw[1], 2, QM_VECTOR[1], P)
+        deal_pair(nc.vector.tensor_copy, qm_dealt, qm_raw[0], 0, 0, QM_VECTOR)
+        deal_pair(nc.scalar.copy, qm_dealt, qm_raw[0], 0, QM_VECTOR, P)
+        deal_pair(nc.scalar.copy, qm_dealt, qm_raw[1], 2, 0, P - QM_GPSIMD)
+        deal(gpsimd_round, qm_dealt, qm_raw[1], 2, P - QM_GPSIMD, P)
 
         ds_grouped = [sb.tile([P, R], BF16, name="ds_grouped%d" % b, align_bytes=64)[:] for b in range(2)]
         ds_grouped = ds_grouped + [flat(qm_dealt, 0, P), flat(qm_dealt, P, 2 * P)]
@@ -244,27 +253,28 @@ def tile_attend_gat_pl_sig_k_kernel(tc, qT, kT, vT, doT, rw, qm, offs, out_0, ou
 
         form_ds(0)
         form_ds(1)
-        deal_pair(nc.vector.tensor_copy, qm_dealt, qm_raw[1], 2, 0, QM_VECTOR[1])
         quantize_ds(0)
         quantize_qm(0)
         quantize_ds(1)
         gradient(0, 0, "first")
-        empty(nc.scalar.copy, 0, 0)
-        scalar_scatter(0, 0)
         quantize_qm(1)
+        gradient(1, 0, "first")
+        empty(nc.scalar.copy, 0, 0)
+        empty(nc.scalar.copy, 1, 0)
+        scalar_scatter(0, 0)
+        scalar_scatter(1, 0)
         form_ds(2)
         form_ds(3)
         quantize_ds(2)
         quantize_qm(2)
         quantize_ds(3)
         quantize_qm(LAST)
-        for j, h in ((1, 0), (0, 1), (2, 0)):
+        for j, h in ((2, 0), (0, 1)):
             gradient(j, h, "first")
         for j, h in ((1, 1), (LAST, 0), (2, 1), (LAST, 1)):
             gradient(j, h, "second")
-        for j, h in ((1, 0), (0, 1), (2, 0)):
-            empty(nc.vector.tensor_copy, j, h)
-        scalar_scatter(1, 0)
+        empty(nc.vector.tensor_copy, 2, 0)
+        empty(nc.vector.tensor_copy, 0, 1)
         vector_scatter(0, 1)
         store_plane(0)
         scalar_scatter(2, 0)
@@ -275,21 +285,15 @@ def tile_attend_gat_pl_sig_k_kernel(tc, qT, kT, vT, doT, rw, qm, offs, out_0, ou
         scalar_scatter(LAST, 0)
         empty(nc.vector.tensor_copy, 2, 1)
         empty(nc.vector.tensor_copy, LAST, 1)
-        vector_scatter(2, 1)
+        scalar_scatter(2, 1)
         store_plane(2)
         scalar_scatter(LAST, 1)
         store_plane(LAST)
 
-        STRIP = P * PLACES
-        pairs = [
-            sb.tile([P, GPSIMD_STRIPS * STRIP], BF16, name="pairs_low", align_bytes=64),
-            sb.tile([P, (STRIPS - GPSIMD_STRIPS) * STRIP], BF16, name="pairs_high", tag="dk21", align_bytes=64),
-        ]
+        pairs = sb.tile([P, T * PLACES], BF16, name="pairs", align_bytes=64)
 
         def strip_range(s0, s1):
-            if s0 < GPSIMD_STRIPS:
-                return pairs[0][:, s0 * STRIP : s1 * STRIP]
-            return pairs[1][:, (s0 - GPSIMD_STRIPS) * STRIP : (s1 - GPSIMD_STRIPS) * STRIP]
+            return pairs[:, s0 * P * PLACES : s1 * P * PLACES]
 
         def round_plane(copy, j, s0, s1):
             u, e = divmod(j, 2)
@@ -298,18 +302,19 @@ def tile_attend_gat_pl_sig_k_kernel(tc, qT, kT, vT, doT, rw, qm, offs, out_0, ou
                 in_=windows[j][:, s0 * P : s1 * P].rearrange("p (s n) -> p s n", n=P),
             )
 
-        split = GPSIMD_STRIPS + SCALAR_STRIPS
-        for j in range(2):
-            round_plane(gpsimd_round, j, 0, GPSIMD_STRIPS)
-        for j in range(2):
-            round_plane(nc.scalar.copy, j, GPSIMD_STRIPS, split)
-        for s0, s1 in ((0, 4), (4, GPSIMD_STRIPS)):
-            for j in (2, LAST):
-                round_plane(nc.vector.tensor_copy, j, s0, s1)
-        for j in range(2):
-            round_plane(nc.vector.tensor_copy, j, split, STRIPS)
-        for j in (2, LAST):
-            round_plane(nc.vector.tensor_copy, j, GPSIMD_STRIPS, STRIPS)
+        shared = GPSIMD_STRIPS - 1
+        round_plane(gpsimd_round, 0, 0, shared)
+        gpsimd_round(
+            out=strip_range(shared, shared + 1)[:, 0 : 2 * P].rearrange("p (n e) -> p n e", e=2),
+            in_=windows[0][:, shared * P : (shared + 1) * P].unsqueeze(2).to_broadcast([P, P, 2]),
+        )
+        round_plane(nc.vector.tensor_copy, 0, GPSIMD_STRIPS, STRIPS)
+        round_plane(nc.vector.tensor_copy, 1, GPSIMD_STRIPS, STRIPS)
+        round_plane(nc.vector.tensor_copy, 1, 0, GPSIMD_STRIPS)
+        round_plane(nc.vector.tensor_copy, 2, 0, STRIPS // 2)
+        round_plane(nc.vector.tensor_copy, 2, STRIPS // 2, STRIPS)
+        for s0, s1 in LAST_RUNS:
+            round_plane(nc.vector.tensor_copy, LAST, s0, s1)
 
         band = T // SCALE_BANDS
         out_codes = sb.tile([P, T], U32, name="out_codes", align_bytes=64)
@@ -321,7 +326,8 @@ def tile_attend_gat_pl_sig_k_kernel(tc, qT, kT, vT, doT, rw, qm, offs, out_0, ou
 
         def weave(c):
             s0, s1 = PIECES[c]
-            nc.scalar.copy(
+            copy = nc.vector.tensor_copy if c == VECTOR_PIECE else nc.scalar.copy
+            copy(
                 out=out_grouped[c][:].bitcast(F32).rearrange("p (s n u) -> p s n u", n=P, u=2),
                 in_=strip_range(s0, s1).bitcast(F32).rearrange("p (s u n) -> p s n u", u=2, n=P),
             )

@@ -25,9 +25,8 @@ ALU = mybir.AluOpType
 ACT = mybir.ActivationFunctionType
 
 SLOPES_BEHIND = ((0,), (1, 2), (3,), ())
-DO_VECTOR = (104, 84)
-QM_VECTOR = 32
-QM_GPSIMD = 56
+DO_VECTOR = 32
+QM_VECTOR = 64
 GPSIMD_STRIPS = 8
 LAST_RUNS = ((0, 2), (2, 8), (8, STRIPS))
 VECTOR_PIECE = 3
@@ -87,11 +86,11 @@ def tile_attend_gat_pl_sig_k_kernel(tc, qT, kT, vT, doT, rw, qm, offs, out_0, ou
                 in_=raw[:].rearrange("p t (s j) -> p s j t", j=PLACES)[:, s0:s1, :, :],
             )
 
-        def deal_pair(copy, dealt, raw, t0, s0, s1):
+        def deal_pair(copy, dealt, raw, t0, s0, s1, tiles=slice(0, PLACES)):
             c0, c1 = s0 // 2, s1 // 2
             copy(
-                out=dealt[:].rearrange("p (j c i t) -> p c j i t", j=PLACES, i=2, t=PLACES)[:, c0:c1, :, :, t0 : t0 + 2],
-                in_=raw[:].rearrange("p t (c i j) -> p c j i t", i=2, j=PLACES)[:, c0:c1, :, :, :],
+                out=dealt[:].rearrange("p (j c i t) -> p c j i t", j=PLACES, i=2, t=PLACES)[:, c0:c1, tiles, :, t0 : t0 + 2],
+                in_=raw[:].rearrange("p t (c i j) -> p c j i t", i=2, j=PLACES)[:, c0:c1, tiles, :, :],
             )
 
         halves = first, second = slice(0, HALF), slice(HALF, N)
@@ -184,18 +183,20 @@ def tile_attend_gat_pl_sig_k_kernel(tc, qT, kT, vT, doT, rw, qm, offs, out_0, ou
                 )
                 slopes.append(slope[:])
         place_rows(v_grouped, v_second)
-        v_mx = [mx_tiles("v%d" % h, HALF) for h in range(2)]
+        v_mx = [mx_tiles("v0", HALF)]
         quantize(v_mx[0], E4M3, 0, HALF, flat(v_grouped, 0, HALF))
 
         do_dealt = sb.tile([P, R * PLACES], BF16, name="do_dealt", align_bytes=64)
         do_mx = [mx_tiles("do%d" % j, P) for j in range(PLACES)]
-        deal_pair(nc.vector.tensor_copy, do_dealt, do_raw[0], 0, 0, DO_VECTOR[0])
-        deal_pair(nc.scalar.copy, do_dealt, do_raw[0], 0, DO_VECTOR[0], P)
-        quantize(v_mx[1], E4M3, 0, HALF, flat(v_grouped, HALF, N))
-        deal_pair(nc.vector.tensor_copy, do_dealt, do_raw[1], 2, 0, DO_VECTOR[1])
-        deal_pair(nc.scalar.copy, do_dealt, do_raw[1], 2, DO_VECTOR[1], P)
+        deal_pair(nc.vector.tensor_copy, do_dealt, do_raw[0], 0, 0, P)
+        low, high = slice(0, 2), slice(2, PLACES)
+        deal_pair(nc.vector.tensor_copy, do_dealt, do_raw[1], 2, 0, P, low)
+        deal_pair(nc.vector.tensor_copy, do_dealt, do_raw[1], 2, 0, DO_VECTOR, high)
+        deal_pair(nc.scalar.copy, do_dealt, do_raw[1], 2, DO_VECTOR, P, high)
         for j in range(PLACES):
             quantize(do_mx[j], E5M2, 0, P, flat(do_dealt, P * j, P * (j + 1)))
+        v_mx.append(mx_tiles("v1", HALF, "do_raw1"))
+        quantize(v_mx[1], E4M3, 0, HALF, flat(v_grouped, HALF, N))
 
         dps = []
         for b in range(BATCHES):
@@ -205,10 +206,11 @@ def tile_attend_gat_pl_sig_k_kernel(tc, qT, kT, vT, doT, rw, qm, offs, out_0, ou
             dps.append(bank[:].rearrange("p j (c i) -> p c j i", i=2))
 
         qm_dealt = sb.tile([P, D * PLACES], BF16, name="qm_dealt", align_bytes=64)
-        deal_pair(nc.vector.tensor_copy, qm_dealt, qm_raw[0], 0, 0, QM_VECTOR)
-        deal_pair(nc.scalar.copy, qm_dealt, qm_raw[0], 0, QM_VECTOR, P)
-        deal_pair(nc.scalar.copy, qm_dealt, qm_raw[1], 2, 0, P - QM_GPSIMD)
-        deal(gpsimd_round, qm_dealt, qm_raw[1], 2, P - QM_GPSIMD, P)
+        deal_pair(nc.scalar.copy, qm_dealt, qm_raw[0], 0, 0, P, low)
+        deal_pair(nc.vector.tensor_copy, qm_dealt, qm_raw[0], 0, 0, QM_VECTOR, high)
+        deal_pair(nc.scalar.copy, qm_dealt, qm_raw[0], 0, QM_VECTOR, P, high)
+        deal_pair(nc.scalar.copy, qm_dealt, qm_raw[1], 2, 0, P, low)
+        deal_pair(nc.scalar.copy, qm_dealt, qm_raw[1], 2, 0, P, high)
 
         ds_grouped = [sb.tile([P, R], BF16, name="ds_grouped%d" % b, align_bytes=64)[:] for b in range(2)]
         ds_grouped = ds_grouped + [flat(qm_dealt, 0, P), flat(qm_dealt, P, 2 * P)]

@@ -28,7 +28,8 @@ SLOPES_BEHIND = ((0,), (1, 2), (3,), ())
 DO_VECTOR = 32
 QM_VECTOR = 64
 GPSIMD_STRIPS = 8
-LAST_RUNS = ((0, 2), (2, 8), (8, STRIPS))
+SCALAR_STRIPS = 2
+LAST_RUNS = ((0, 2), (2, 8), (8, STRIPS - SCALAR_STRIPS))
 VECTOR_PIECE = 3
 PIECES = ((0, 2), (2, 4), (4, 6), (6, 8), (8, 10), (10, 12), (12, 14), (14, 15), (15, STRIPS))
 STORE_ENDS = (4, 8, 12, 14, STRIPS)
@@ -292,10 +293,14 @@ def tile_attend_gat_pl_sig_k_kernel(tc, qT, kT, vT, doT, rw, qm, offs, out_0, ou
         scalar_scatter(LAST, 1)
         store_plane(LAST)
 
-        pairs = sb.tile([P, T * PLACES], BF16, name="pairs", align_bytes=64)
+        split = STRIPS - SCALAR_STRIPS
+        pairs = sb.tile([P, split * P * PLACES], BF16, name="pairs", align_bytes=64)
+        last_pairs = sb.tile([P, SCALAR_STRIPS * P * PLACES], BF16, name="last_pairs", tag="dk21", align_bytes=64)
 
         def strip_range(s0, s1):
-            return pairs[:, s0 * P * PLACES : s1 * P * PLACES]
+            if s0 < split:
+                return pairs[:, s0 * P * PLACES : s1 * P * PLACES]
+            return last_pairs[:, (s0 - split) * P * PLACES : (s1 - split) * P * PLACES]
 
         def round_plane(copy, j, s0, s1):
             u, e = divmod(j, 2)
@@ -310,13 +315,16 @@ def tile_attend_gat_pl_sig_k_kernel(tc, qT, kT, vT, doT, rw, qm, offs, out_0, ou
             out=strip_range(shared, shared + 1)[:, 0 : 2 * P].rearrange("p (n e) -> p n e", e=2),
             in_=windows[0][:, shared * P : (shared + 1) * P].unsqueeze(2).to_broadcast([P, P, 2]),
         )
-        round_plane(nc.vector.tensor_copy, 0, GPSIMD_STRIPS, STRIPS)
-        round_plane(nc.vector.tensor_copy, 1, GPSIMD_STRIPS, STRIPS)
+        round_plane(nc.vector.tensor_copy, 0, GPSIMD_STRIPS, split)
+        round_plane(nc.vector.tensor_copy, 1, GPSIMD_STRIPS, split)
         round_plane(nc.vector.tensor_copy, 1, 0, GPSIMD_STRIPS)
-        round_plane(nc.vector.tensor_copy, 2, 0, STRIPS // 2)
-        round_plane(nc.vector.tensor_copy, 2, STRIPS // 2, STRIPS)
+        for j in range(2):
+            round_plane(nc.scalar.copy, j, split, STRIPS)
+        round_plane(nc.vector.tensor_copy, 2, 0, split)
         for s0, s1 in LAST_RUNS:
             round_plane(nc.vector.tensor_copy, LAST, s0, s1)
+        for j in (2, LAST):
+            round_plane(nc.vector.tensor_copy, j, split, STRIPS)
 
         band = T // SCALE_BANDS
         out_codes = sb.tile([P, T], U32, name="out_codes", align_bytes=64)

@@ -25,8 +25,8 @@ ALU = mybir.AluOpType
 ACT = mybir.ActivationFunctionType
 
 SLOPES_BEHIND = ((0,), (1, 2), (3,), ())
-DO_VECTOR = 32
-QM_VECTOR = 64
+DO_VECTOR = (88, 56)
+QM_VECTOR = 88
 GPSIMD_STRIPS = 8
 SCALAR_STRIPS = 2
 LAST_RUNS = ((0, 2), (2, 8), (8, STRIPS - SCALAR_STRIPS))
@@ -191,9 +191,9 @@ def tile_attend_gat_pl_sig_k_kernel(tc, qT, kT, vT, doT, rw, qm, offs, out_0, ou
         do_mx = [mx_tiles("do%d" % j, P) for j in range(PLACES)]
         deal_pair(nc.vector.tensor_copy, do_dealt, do_raw[0], 0, 0, P)
         low, high = slice(0, 2), slice(2, PLACES)
-        deal_pair(nc.vector.tensor_copy, do_dealt, do_raw[1], 2, 0, P, low)
-        deal_pair(nc.vector.tensor_copy, do_dealt, do_raw[1], 2, 0, DO_VECTOR, high)
-        deal_pair(nc.scalar.copy, do_dealt, do_raw[1], 2, DO_VECTOR, P, high)
+        for tiles, share in zip((low, high), DO_VECTOR):
+            deal_pair(nc.vector.tensor_copy, do_dealt, do_raw[1], 2, 0, share, tiles)
+            deal_pair(nc.scalar.copy, do_dealt, do_raw[1], 2, share, P, tiles)
         for j in range(PLACES):
             quantize(do_mx[j], E5M2, 0, P, flat(do_dealt, P * j, P * (j + 1)))
         v_mx.append(mx_tiles("v1", HALF, "do_raw1"))
@@ -202,7 +202,7 @@ def tile_attend_gat_pl_sig_k_kernel(tc, qT, kT, vT, doT, rw, qm, offs, out_0, ou
         dps = []
         for b in range(BATCHES):
             bank = psum.tile([P, PLACES, P], F32, name="dp", tag="second")
-            for j in range(PLACES):
+            for j in reversed(range(PLACES)) if b else range(PLACES):
                 product(bank[:, j, :], do_mx[j], E5M2, 0, v_mx[b // 2], E4M3, batch(b % 2))
             dps.append(bank[:].rearrange("p j (c i) -> p c j i", i=2))
 
@@ -231,19 +231,19 @@ def tile_attend_gat_pl_sig_k_kernel(tc, qT, kT, vT, doT, rw, qm, offs, out_0, ou
 
         banks = {}
 
-        def gradient(j, h, ring):
-            banks[j, h] = psum.tile([P, HALF], F32, name="acc", tag=ring)
-            if j:
-                product(banks[j, h][:], qm_mx[j], E4M3, 0, ds_mx, E5M2, halves[h])
-            else:
-                for i in range(2):
-                    product(banks[j, h][:, batch(i)], qm_mx[j], E4M3, 0, ds_mx, E5M2, batch(2 * h + i))
+        def gradient(j, tokens, ring):
+            bank = psum.tile([P, tokens.stop - tokens.start], F32, name="acc", tag=ring)
+            product(bank[:], qm_mx[j], E4M3, 0, ds_mx, E5M2, tokens)
+            banks[j, tokens.start] = bank[:]
 
         dk = {}
+        for j in range(PLACES):
+            for h in range(2):
+                dk[j, h] = sb.tile([P, HALF], F32, name="dk%d%d" % (j, h), tag="dk%d%d" % (j, h), align_bytes=64)
 
-        def empty(copy, j, h):
-            dk[j, h] = sb.tile([P, HALF], F32, name="dk%d%d" % (j, h), tag="dk%d%d" % (j, h), align_bytes=64)
-            copy(out=dk[j, h][:], in_=banks[j, h][:])
+        def empty(copy, j, tokens):
+            h, n0 = divmod(tokens.start, HALF)
+            copy(out=dk[j, h][:, n0 : n0 + tokens.stop - tokens.start], in_=banks[j, tokens.start])
 
         def scalar_scatter(j, h):
             nc.scalar.activation(out=windows[j][:].indirect(entries(halves[h])), in_=dk[j, h][:], func=ACT.Copy)
@@ -259,11 +259,12 @@ def tile_attend_gat_pl_sig_k_kernel(tc, qT, kT, vT, doT, rw, qm, offs, out_0, ou
         quantize_ds(0)
         quantize_qm(0)
         quantize_ds(1)
-        gradient(0, 0, "first")
         quantize_qm(1)
-        gradient(1, 0, "first")
-        empty(nc.scalar.copy, 0, 0)
-        empty(nc.scalar.copy, 1, 0)
+        for b in range(2):
+            gradient(0, batch(b), "first")
+            empty(nc.scalar.copy, 0, batch(b))
+        gradient(1, first, "first")
+        empty(nc.scalar.copy, 1, first)
         scalar_scatter(0, 0)
         scalar_scatter(1, 0)
         form_ds(2)
@@ -272,22 +273,26 @@ def tile_attend_gat_pl_sig_k_kernel(tc, qT, kT, vT, doT, rw, qm, offs, out_0, ou
         quantize_qm(2)
         quantize_ds(3)
         quantize_qm(LAST)
-        for j, h in ((2, 0), (0, 1)):
-            gradient(j, h, "first")
-        for j, h in ((1, 1), (LAST, 0), (2, 1), (LAST, 1)):
-            gradient(j, h, "second")
-        empty(nc.vector.tensor_copy, 2, 0)
-        empty(nc.vector.tensor_copy, 0, 1)
+        gradient(2, first, "first")
+        for b in (2, LAST):
+            gradient(0, batch(b), "second")
+        gradient(1, second, "second")
+        gradient(LAST, first, "second")
+        gradient(2, second, "first")
+        gradient(LAST, second, "first")
+        empty(nc.vector.tensor_copy, 0, batch(2))
+        empty(nc.vector.tensor_copy, 2, first)
+        empty(nc.vector.tensor_copy, 0, batch(LAST))
         vector_scatter(0, 1)
         store_plane(0)
         scalar_scatter(2, 0)
-        empty(nc.vector.tensor_copy, 1, 1)
-        empty(nc.vector.tensor_copy, LAST, 0)
+        empty(nc.vector.tensor_copy, 1, second)
+        empty(nc.vector.tensor_copy, LAST, first)
         vector_scatter(1, 1)
         store_plane(1)
         scalar_scatter(LAST, 0)
-        empty(nc.vector.tensor_copy, 2, 1)
-        empty(nc.vector.tensor_copy, LAST, 1)
+        empty(nc.vector.tensor_copy, 2, second)
+        empty(nc.vector.tensor_copy, LAST, second)
         scalar_scatter(2, 1)
         store_plane(2)
         scalar_scatter(LAST, 1)

@@ -24,7 +24,7 @@ E5M2 = mybir.dt.float8_e5m2_x4
 ALU = mybir.AluOpType
 ACT = mybir.ActivationFunctionType
 
-SLOPES_BEHIND = ((0,), (1, 2), (3,), ())
+SLOPES_BEHIND = ((0,), (1, 2), (), ())
 DO_VECTOR = (88, 56)
 QM_VECTOR = 88
 GPSIMD_STRIPS = 8
@@ -34,6 +34,7 @@ VECTOR_PIECE = 3
 PIECES = ((0, 2), (2, 4), (4, 6), (6, 8), (8, 10), (10, 12), (12, 14), (14, 15), (15, STRIPS))
 STORE_ENDS = (4, 8, 12, 14, STRIPS)
 SCALE_BANDS = 4
+RUN = 4
 
 
 def tile_attend_gat_pl_sig_k_kernel(tc, qT, kT, vT, doT, rw, qm, offs, out_0, out_1, out_2):
@@ -117,10 +118,10 @@ def tile_attend_gat_pl_sig_k_kernel(tc, qT, kT, vT, doT, rw, qm, offs, out_0, ou
             nc.vector.memset(window[:], 0.0)
         nc.gpsimd.memset(windows[LAST][:], 0.0)
 
-        gates = sb.tile([P, P // 2, PLACES, 2], F32, name="gates", align_bytes=64)
+        gates = sb.tile([P, P // RUN, PLACES, RUN], F32, name="gates", align_bytes=64)
         nc.scalar.activation(
             out=gates[:],
-            in_=gate[:].unsqueeze(1).unsqueeze(3).to_broadcast([P, P // 2, PLACES, 2]),
+            in_=gate[:].unsqueeze(1).unsqueeze(3).to_broadcast([P, P // RUN, PLACES, RUN]),
             func=ACT.Copy,
             scale=-0.25,
         )
@@ -158,10 +159,10 @@ def tile_attend_gat_pl_sig_k_kernel(tc, qT, kT, vT, doT, rw, qm, offs, out_0, ou
             bank = psum.tile([P, PLACES, P], F32, name=name, tag=tag)
             for j in range(PLACES):
                 product(bank[:, j, :], lhs, lhs_fmt, j, rhs, E4M3, moving)
-            return bank[:].rearrange("p j (c i) -> p c j i", i=2)
+            return bank[:].rearrange("p j (c i) -> p c j i", i=RUN)
 
         def by_place(row):
-            return row.rearrange("p (c j i) -> p c j i", j=PLACES, i=2)
+            return row.rearrange("p (c j i) -> p c j i", j=PLACES, i=RUN)
 
         squares = []
         for b in range(BATCHES):
@@ -184,6 +185,13 @@ def tile_attend_gat_pl_sig_k_kernel(tc, qT, kT, vT, doT, rw, qm, offs, out_0, ou
                 )
                 slopes.append(slope[:])
         place_rows(v_grouped, v_second)
+        shifted = sb.tile([P, R], F32, name="shifted", tag="square2", align_bytes=64)
+        nc.gpsimd.tensor_scalar(
+            out=shifted[:], in0=squares[LAST][:], scalar1=1.0, scalar2=-1.0, op0=ALU.mult, op1=ALU.add
+        )
+        last_slope = sb.tile([P, R], F32, name="last_slope", align_bytes=64)
+        nc.gpsimd.tensor_tensor(out=last_slope[:], in0=shifted[:], in1=gate_row, op=ALU.mult)
+        slopes.append(last_slope[:])
         v_mx = [mx_tiles("v0", HALF)]
         quantize(v_mx[0], E4M3, 0, HALF, flat(v_grouped, 0, HALF))
 
@@ -204,7 +212,7 @@ def tile_attend_gat_pl_sig_k_kernel(tc, qT, kT, vT, doT, rw, qm, offs, out_0, ou
             bank = psum.tile([P, PLACES, P], F32, name="dp", tag="second")
             for j in reversed(range(PLACES)) if b else range(PLACES):
                 product(bank[:, j, :], do_mx[j], E5M2, 0, v_mx[b // 2], E4M3, batch(b % 2))
-            dps.append(bank[:].rearrange("p j (c i) -> p c j i", i=2))
+            dps.append(bank[:].rearrange("p j (c i) -> p c j i", i=RUN))
 
         qm_dealt = sb.tile([P, D * PLACES], BF16, name="qm_dealt", align_bytes=64)
         deal_pair(nc.scalar.copy, qm_dealt, qm_raw[0], 0, 0, P, low)
@@ -218,7 +226,7 @@ def tile_attend_gat_pl_sig_k_kernel(tc, qT, kT, vT, doT, rw, qm, offs, out_0, ou
         ds_mx = mx_tiles("ds", N)
 
         def form_ds(b):
-            out = ds_grouped[b].rearrange("p (c i j) -> p c j i", i=2, j=PLACES)
+            out = ds_grouped[b].rearrange("p (c i j) -> p c j i", i=RUN, j=PLACES)
             nc.vector.tensor_tensor(out=out, in0=dps[b], in1=by_place(slopes[b]), op=ALU.mult)
 
         def quantize_ds(b):

@@ -25,7 +25,7 @@ ALU = mybir.AluOpType
 ACT = mybir.ActivationFunctionType
 
 SLOPES_BEHIND = ((0,), (1, 2), (), ())
-DO_VECTOR = (88, 56)
+DO_VECTOR = (88, 72)
 QM_VECTOR = 88
 GPSIMD_STRIPS = 8
 SCALAR_STRIPS = 2
@@ -34,7 +34,7 @@ VECTOR_PIECE = 3
 PIECES = ((0, 2), (2, 4), (4, 6), (6, 8), (8, 10), (10, 12), (12, 14), (14, 15), (15, STRIPS))
 STORE_ENDS = (4, 8, 12, 14, STRIPS)
 SCALE_BANDS = 4
-RUN = 4
+RUN = 8
 
 
 def tile_attend_gat_pl_sig_k_kernel(tc, qT, kT, vT, doT, rw, qm, offs, out_0, out_1, out_2):
@@ -334,10 +334,10 @@ def tile_attend_gat_pl_sig_k_kernel(tc, qT, kT, vT, doT, rw, qm, offs, out_0, ou
         for j in range(2):
             round_plane(nc.scalar.copy, j, split, STRIPS)
         round_plane(nc.vector.tensor_copy, 2, 0, split)
+        round_plane(nc.vector.tensor_copy, 2, split, STRIPS)
         for s0, s1 in LAST_RUNS:
             round_plane(nc.vector.tensor_copy, LAST, s0, s1)
-        for j in (2, LAST):
-            round_plane(nc.vector.tensor_copy, j, split, STRIPS)
+        round_plane(nc.vector.tensor_copy, LAST, split, STRIPS)
 
         band = T // SCALE_BANDS
         out_codes = sb.tile([P, T], U32, name="out_codes", align_bytes=64)

@@ -24,7 +24,7 @@ E5M2 = mybir.dt.float8_e5m2_x4
 ALU = mybir.AluOpType
 ACT = mybir.ActivationFunctionType
 
-SLOPES_BEHIND = ((0,), (1, 2), (), ())
+Q_VECTOR = 64
 DO_VECTOR = (88, 72)
 QM_VECTOR = 88
 GPSIMD_STRIPS = 8
@@ -81,11 +81,10 @@ def tile_attend_gat_pl_sig_k_kernel(tc, qT, kT, vT, doT, rw, qm, offs, out_0, ou
         def place(grouped, cols, t):
             return grouped[:].rearrange("p (n t) -> p n t", t=PLACES)[:, cols, t]
 
-        def deal(copy, dealt, raw, t0, s0, s1):
-            planes = raw.shape[1]
+        def deal(copy, dealt, raw, s0, s1, tiles):
             copy(
-                out=dealt[:].rearrange("p (j s t) -> p s j t", j=PLACES, t=PLACES)[:, s0:s1, :, t0 : t0 + planes],
-                in_=raw[:].rearrange("p t (s j) -> p s j t", j=PLACES)[:, s0:s1, :, :],
+                out=dealt[:].rearrange("p (j s t) -> p s j t", j=PLACES, t=PLACES)[:, s0:s1, tiles, :],
+                in_=raw[:].rearrange("p t (s j) -> p s j t", j=PLACES)[:, s0:s1, tiles, :],
             )
 
         def deal_pair(copy, dealt, raw, t0, s0, s1, tiles=slice(0, PLACES)):
@@ -103,43 +102,36 @@ def tile_attend_gat_pl_sig_k_kernel(tc, qT, kT, vT, doT, rw, qm, offs, out_0, ou
         def batch(b):
             return slice(b * P, (b + 1) * P)
 
-        q_raw = load("q_raw", planes_of(qT[0]))
+        k_pool = [load("k_pool0", planes_of(kT)[:, 0:2, :])]
         offsets = sb.tile([P, N // LIST_ROWS], U16, name="offsets")
         nc.sync.dma_start(offsets[:], offs)
         gate = sb.tile([P, PLACES], F32, name="gate")
         nc.scalar.dma_start(out=gate[:], in_=rw[0].rearrange("(s j) o -> s (j o)", j=PLACES))
-        k_pool = [load("k_pool%d" % t, planes_of(kT)[:, t, :]) for t in range(PLACES)]
-        v_pool = [load("v_pool%d" % t, planes_of(vT)[:, t, :]) for t in range(PLACES)]
+        k_pool.append(load("k_pool2", planes_of(kT)[:, 2:PLACES, :]))
+        q_raw = load("q_raw", planes_of(qT[0]))
+        v_pair = load("v_pool0", planes_of(vT)[:, 0:2, :])
+        v_pool = [load("v_pool%d" % t, planes_of(vT)[:, t, :]) for t in (2, LAST)]
         do_raw = [load("do_raw%d" % w, planes_of(doT[0])[:, 2 * w : 2 * w + 2, :]) for w in range(2)]
         qm_raw = [load("qm_raw%d" % w, planes_of(qm[0])[:, 2 * w : 2 * w + 2, :]) for w in range(2)]
+        k_planes = [k_pool[t // 2][:, t % 2, :] for t in range(PLACES)]
+        v_planes = [v_pair[:, 0, :], v_pair[:, 1, :], v_pool[0][:], v_pool[1][:]]
 
         windows = [sb.tile([P, T], F32, name="window%d" % j, align_bytes=64) for j in range(PLACES)]
         for window in windows[:LAST]:
             nc.vector.memset(window[:], 0.0)
         nc.gpsimd.memset(windows[LAST][:], 0.0)
 
-        gates = sb.tile([P, P // RUN, PLACES, RUN], F32, name="gates", align_bytes=64)
-        nc.scalar.activation(
-            out=gates[:],
-            in_=gate[:].unsqueeze(1).unsqueeze(3).to_broadcast([P, P // RUN, PLACES, RUN]),
-            func=ACT.Copy,
-            scale=-0.25,
-        )
-        gate_row = gates[:].rearrange("p c j i -> p (c j i)")
+        quarter = sb.tile([P, PLACES], F32, name="quarter")
+        minus_quarter = sb.tile([P, PLACES], F32, name="minus_quarter")
+        nc.scalar.activation(out=quarter[:], in_=gate[:], func=ACT.Copy, scale=0.25)
+        nc.scalar.activation(out=minus_quarter[:], in_=gate[:], func=ACT.Copy, scale=-0.25)
 
-        q_dealt = sb.tile([P, R * PLACES], BF16, name="q_dealt", align_bytes=64)
-        deal(nc.scalar.copy, q_dealt, q_raw, 0, 0, P)
-        q_mx = mx_tiles("q", R)
-        quantize(q_mx, E4M3, 0, R, q_dealt[:])
-
-        k_grouped = sb.tile([P, N * PLACES], BF16, name="k_grouped", align_bytes=64)
-
-        def gather(grouped, rows, pool, t):
+        def gather(grouped, rows, planes, t):
             if t < 2:
-                nc.vector.tensor_copy(out=place(grouped, slice(0, N), t), in_=pool[t][:].indirect(offsets[:]))
+                nc.vector.tensor_copy(out=place(grouped, slice(0, N), t), in_=planes[t].indirect(offsets[:]))
             else:
-                nc.vector.tensor_copy(out=place(grouped, first, t), in_=pool[t][:].indirect(entries(first)))
-                nc.scalar.activation(out=rows[:, t - 2, :], in_=pool[t][:].indirect(entries(second)), func=ACT.Copy)
+                nc.vector.tensor_copy(out=place(grouped, first, t), in_=planes[t].indirect(entries(first)))
+                nc.scalar.activation(out=rows[:, t - 2, :], in_=planes[t].indirect(entries(second)), func=ACT.Copy)
 
         def place_rows(grouped, rows):
             nc.scalar.copy(
@@ -147,58 +139,52 @@ def tile_attend_gat_pl_sig_k_kernel(tc, qT, kT, vT, doT, rw, qm, offs, out_0, ou
                 in_=rows[:].rearrange("p t n -> p n t"),
             )
 
-        k_rows = sb.tile([P, 2, HALF], BF16, name="k_rows", align_bytes=64)
+        low, high = slice(0, 2), slice(2, PLACES)
+        k_grouped = sb.tile([P, N * PLACES], BF16, name="k_grouped", align_bytes=64)
+        k_rows = sb.tile([P, 2, HALF], F32, name="k_rows", align_bytes=64)
         for t in range(PLACES):
-            gather(k_grouped, k_rows, k_pool, t)
+            gather(k_grouped, k_rows, k_planes, t)
         place_rows(k_grouped, k_rows)
         k_mx = mx_tiles("k", N)
         for cols in halves:
             quantize(k_mx, E4M3, cols.start, cols.stop, flat(k_grouped, cols.start, cols.stop))
 
-        def batch_product(name, tag, lhs, lhs_fmt, rhs, moving):
-            bank = psum.tile([P, PLACES, P], F32, name=name, tag=tag)
-            for j in range(PLACES):
-                product(bank[:, j, :], lhs, lhs_fmt, j, rhs, E4M3, moving)
-            return bank[:].rearrange("p j (c i) -> p c j i", i=RUN)
+        q_dealt = sb.tile([P, R * PLACES], BF16, name="q_dealt", align_bytes=64)
+        deal(nc.vector.tensor_copy, q_dealt, q_raw, 0, P, low)
+        deal(nc.vector.tensor_copy, q_dealt, q_raw, 0, Q_VECTOR, high)
+        deal(nc.scalar.copy, q_dealt, q_raw, Q_VECTOR, P, high)
+        q_mx = mx_tiles("q", R)
+        for tiles in (low, high):
+            quantize(q_mx, E4M3, tiles.start * P, tiles.stop * P, flat(q_dealt, tiles.start * P, tiles.stop * P))
 
-        def by_place(row):
-            return row.rearrange("p (c j i) -> p c j i", j=PLACES, i=RUN)
-
-        squares = []
-        for b in range(BATCHES):
-            score = batch_product("score", "first", q_mx, E4M3, k_mx, batch(b))
-            tanh = sb.tile([P, R], F32, name="tanh%d" % b, align_bytes=64)
-            nc.scalar.activation(out=by_place(tanh[:]), in_=score, func=ACT.Tanh, scale=0.5)
-            square = sb.tile([P, R], F32, name="square%d" % b, tag="square%d" % b, align_bytes=64)
+        slope = sb.tile([P, PLACES, N], F32, name="slope", align_bytes=64)
+        for j in range(PLACES):
+            score = psum.tile([P, N], F32, name="score", tag="first")
+            product(score[:], q_mx, E4M3, j, k_mx, E4M3, slice(0, N))
+            tanh = sb.tile([P, N], F32, name="tanh%d" % j, align_bytes=64)
+            nc.scalar.activation(out=tanh[:], in_=score[:], func=ACT.Tanh, scale=0.5)
+            square = sb.tile([P, N], F32, name="square%d" % j, align_bytes=64)
             nc.scalar.activation(out=square[:], in_=tanh[:], func=ACT.Square)
-            squares.append(square)
+            nc.gpsimd.tensor_scalar(
+                out=slope[:, j, :],
+                in0=square[:],
+                scalar1=minus_quarter[:, j : j + 1],
+                scalar2=quarter[:, j : j + 1],
+                op0=ALU.mult,
+                op1=ALU.add,
+            )
 
         v_grouped = sb.tile([P, N * PLACES], BF16, name="v_grouped", align_bytes=64)
         v_second = sb.tile([P, 2, HALF], BF16, name="v_second", align_bytes=64)
-        slopes = []
-        for t in range(LAST + 1):
-            gather(v_grouped, v_second, v_pool, t)
-            for b in SLOPES_BEHIND[t]:
-                slope = sb.tile([P, R], F32, name="slope%d" % b, align_bytes=64)
-                nc.vector.scalar_tensor_tensor(
-                    out=slope[:], in0=squares[b][:], scalar=1.0, in1=gate_row, op0=ALU.subtract, op1=ALU.mult
-                )
-                slopes.append(slope[:])
+        for t in range(PLACES):
+            gather(v_grouped, v_second, v_planes, t)
         place_rows(v_grouped, v_second)
-        shifted = sb.tile([P, R], F32, name="shifted", tag="square2", align_bytes=64)
-        nc.gpsimd.tensor_scalar(
-            out=shifted[:], in0=squares[LAST][:], scalar1=1.0, scalar2=-1.0, op0=ALU.mult, op1=ALU.add
-        )
-        last_slope = sb.tile([P, R], F32, name="last_slope", align_bytes=64)
-        nc.gpsimd.tensor_tensor(out=last_slope[:], in0=shifted[:], in1=gate_row, op=ALU.mult)
-        slopes.append(last_slope[:])
         v_mx = [mx_tiles("v0", HALF)]
         quantize(v_mx[0], E4M3, 0, HALF, flat(v_grouped, 0, HALF))
 
         do_dealt = sb.tile([P, R * PLACES], BF16, name="do_dealt", align_bytes=64)
         do_mx = [mx_tiles("do%d" % j, P) for j in range(PLACES)]
         deal_pair(nc.vector.tensor_copy, do_dealt, do_raw[0], 0, 0, P)
-        low, high = slice(0, 2), slice(2, PLACES)
         for tiles, share in zip((low, high), DO_VECTOR):
             deal_pair(nc.vector.tensor_copy, do_dealt, do_raw[1], 2, 0, share, tiles)
             deal_pair(nc.scalar.copy, do_dealt, do_raw[1], 2, share, P, tiles)
@@ -227,7 +213,7 @@ def tile_attend_gat_pl_sig_k_kernel(tc, qT, kT, vT, doT, rw, qm, offs, out_0, ou
 
         def form_ds(b):
             out = ds_grouped[b].rearrange("p (c i j) -> p c j i", i=RUN, j=PLACES)
-            nc.vector.tensor_tensor(out=out, in0=dps[b], in1=by_place(slopes[b]), op=ALU.mult)
+            nc.vector.tensor_tensor(out=out, in0=dps[b], in1=slope[:, :, batch(b)].rearrange("p j (c i) -> p c j i", i=RUN), op=ALU.mult)
 
         def quantize_ds(b):
             quantize(ds_mx, E5M2, b * P, (b + 1) * P, ds_grouped[b])

@@ -28,9 +28,8 @@ Q_VECTOR = 64
 DO_VECTOR = (88, 72)
 QM_VECTOR = 88
 GPSIMD_STRIPS = 8
-SCALAR_STRIPS = 2
-LAST_RUNS = ((0, 2), (2, 8), (8, STRIPS - SCALAR_STRIPS))
-VECTOR_PIECE = 3
+SCALAR_STRIPS = 4
+HELD_STRIPS = 2
 PIECES = ((0, 2), (2, 4), (4, 6), (6, 8), (8, 10), (10, 12), (12, 14), (14, 15), (15, STRIPS))
 STORE_ENDS = (4, 8, 12, 14, STRIPS)
 SCALE_BANDS = 4
@@ -287,19 +286,11 @@ def tile_attend_gat_pl_sig_k_kernel(tc, qT, kT, vT, doT, rw, qm, offs, out_0, ou
         scalar_scatter(LAST, 0)
         empty(nc.vector.tensor_copy, 2, second)
         empty(nc.vector.tensor_copy, LAST, second)
-        scalar_scatter(2, 1)
+        vector_scatter(2, 1)
         store_plane(2)
-        scalar_scatter(LAST, 1)
-        store_plane(LAST)
 
-        split = STRIPS - SCALAR_STRIPS
+        split = STRIPS - HELD_STRIPS
         pairs = sb.tile([P, split * P * PLACES], BF16, name="pairs", align_bytes=64)
-        last_pairs = sb.tile([P, SCALAR_STRIPS * P * PLACES], BF16, name="last_pairs", tag="dk21", align_bytes=64)
-
-        def strip_range(s0, s1):
-            if s0 < split:
-                return pairs[:, s0 * P * PLACES : s1 * P * PLACES]
-            return last_pairs[:, (s0 - split) * P * PLACES : (s1 - split) * P * PLACES]
 
         def round_plane(copy, j, s0, s1):
             u, e = divmod(j, 2)
@@ -308,22 +299,27 @@ def tile_attend_gat_pl_sig_k_kernel(tc, qT, kT, vT, doT, rw, qm, offs, out_0, ou
                 in_=windows[j][:, s0 * P : s1 * P].rearrange("p (s n) -> p s n", n=P),
             )
 
-        shared = GPSIMD_STRIPS - 1
-        round_plane(gpsimd_round, 0, 0, shared)
-        gpsimd_round(
-            out=strip_range(shared, shared + 1)[:, 0 : 2 * P].rearrange("p (n e) -> p n e", e=2),
-            in_=windows[0][:, shared * P : (shared + 1) * P].unsqueeze(2).to_broadcast([P, P, 2]),
-        )
-        round_plane(nc.vector.tensor_copy, 0, GPSIMD_STRIPS, split)
-        round_plane(nc.vector.tensor_copy, 1, GPSIMD_STRIPS, split)
-        round_plane(nc.vector.tensor_copy, 1, 0, GPSIMD_STRIPS)
+        def strip_range(s0, s1):
+            if s0 < split:
+                return pairs[:, s0 * P * PLACES : s1 * P * PLACES]
+            return last_pairs[:, (s0 - split) * P * PLACES : (s1 - split) * P * PLACES]
+
+        scalar_from = STRIPS - SCALAR_STRIPS
         for j in range(2):
+            round_plane(gpsimd_round, j, 0, GPSIMD_STRIPS)
+            round_plane(nc.scalar.copy, j, scalar_from, split)
+        scalar_scatter(LAST, 1)
+        store_plane(LAST)
+        last_pairs = sb.tile([P, HELD_STRIPS * P * PLACES], BF16, name="last_pairs", tag="dk31", align_bytes=64)
+        for j in range(2):
+            round_plane(nc.vector.tensor_copy, j, GPSIMD_STRIPS, scalar_from)
             round_plane(nc.scalar.copy, j, split, STRIPS)
-        round_plane(nc.vector.tensor_copy, 2, 0, split)
-        round_plane(nc.vector.tensor_copy, 2, split, STRIPS)
-        for s0, s1 in LAST_RUNS:
-            round_plane(nc.vector.tensor_copy, LAST, s0, s1)
-        round_plane(nc.vector.tensor_copy, LAST, split, STRIPS)
+        round_plane(nc.vector.tensor_copy, 2, 0, 8)
+        round_plane(nc.vector.tensor_copy, LAST, 0, 2)
+        round_plane(nc.vector.tensor_copy, LAST, 2, 8)
+        for j in (2, LAST):
+            round_plane(nc.vector.tensor_copy, j, 8, split)
+            round_plane(nc.vector.tensor_copy, j, split, STRIPS)
 
         band = T // SCALE_BANDS
         out_codes = sb.tile([P, T], U32, name="out_codes", align_bytes=64)
@@ -335,8 +331,7 @@ def tile_attend_gat_pl_sig_k_kernel(tc, qT, kT, vT, doT, rw, qm, offs, out_0, ou
 
         def weave(c):
             s0, s1 = PIECES[c]
-            copy = nc.vector.tensor_copy if c == VECTOR_PIECE else nc.scalar.copy
-            copy(
+            nc.scalar.copy(
                 out=out_grouped[c][:].bitcast(F32).rearrange("p (s n u) -> p s n u", n=P, u=2),
                 in_=strip_range(s0, s1).bitcast(F32).rearrange("p (s u n) -> p s n u", u=2, n=P),
             )

from contextlib import ExitStack

import concourse.mybir as mybir

N, T, D, R = 512, 2048, 512, 512
P = 128
PLACES = 4
LAST = PLACES - 1
BATCHES = N // P
HALF = N // 2
LIST_ROWS = 16
STRIPS = T // P
QUADRANT = 32
FLOPS = 3 * 2 * R * D * N

F32 = mybir.dt.float32
BF16 = mybir.dt.bfloat16
I32 = mybir.dt.int32
U32 = mybir.dt.uint32
U16 = mybir.dt.uint16
U8 = mybir.dt.uint8
E4M3 = mybir.dt.float8_e4m3fn_x4
E5M2 = mybir.dt.float8_e5m2_x4
ALU = mybir.AluOpType
ACT = mybir.ActivationFunctionType

Q_VECTOR = 64
DO_VECTOR = (88, 72)
QM_VECTOR = 88
GPSIMD_STRIPS = 8
SCALAR_STRIPS = 4
HELD_STRIPS = 2
PIECES = ((0, 2), (2, 4), (4, 6), (6, 8), (8, 10), (10, 12), (12, 14), (14, 15), (15, STRIPS))
STORE_ENDS = (4, 8, 12, 14, STRIPS)
SCALE_BANDS = 4
RUN = 8


def tile_attend_gat_pl_sig_k_kernel(tc, qT, kT, vT, doT, rw, qm, offs, out_0, out_1, out_2):
    nc = tc.nc

    with ExitStack() as ctx:
        sb = ctx.enter_context(tc.tile_pool(name="sb", bufs=1))
        psum = ctx.enter_context(tc.psum_pool(name="psum", bufs=BATCHES))

        def planes_of(x):
            return x.rearrange("(p t) c -> p t c", t=PLACES)

        def load(name, src):
            raw = sb.tile(list(src.shape), F32, name=name, tag=name, align_bytes=64)
            nc.sync.dma_start(out=raw[:], in_=src)
            return raw

        def mx_tiles(name, width, tag=None):
            codes = sb.tile([P, width], U32, name=name + "_codes", tag=tag or name + "_codes", align_bytes=64)
            scales = sb.tile([P, width], U8, name=name + "_scales", align_bytes=64)
            return codes, scales

        def quantize(mx, fmt, c0, c1, grouped):
            nc.vector.quantize_mx(out=mx[0][:, c0:c1].bitcast(fmt), scales=mx[1][:, c0:c1], in_=grouped)

        def gpsimd_round(out, in_):
            nc.gpsimd.tensor_scalar(out=out, in0=in_, scalar1=1.0, scalar2=0.0, op0=ALU.mult, op1=ALU.add)

        def product(out, lhs, lhs_fmt, j, rhs, rhs_fmt, moving):
            cols = slice(j * P, (j + 1) * P)
            nc.tensor.matmul_mx(
                out=out,
                lhsT=lhs[0][:, cols].bitcast(lhs_fmt),
                lhsT_scale=lhs[1][:, cols],
                rhs=rhs[0][:, moving].bitcast(rhs_fmt),
                rhs_scale=rhs[1][:, moving],
                start=True,
                stop=True,
            )

        def flat(grouped, c0, c1):
            return grouped[:, c0 * PLACES : c1 * PLACES]

        def place(grouped, cols, t):
            return grouped[:].rearrange("p (n t) -> p n t", t=PLACES)[:, cols, t]

        def deal(copy, dealt, raw, s0, s1, tiles):
            copy(
                out=dealt[:].rearrange("p (j s t) -> p s j t", j=PLACES, t=PLACES)[:, s0:s1, tiles, :],
                in_=raw[:].rearrange("p t (s j) -> p s j t", j=PLACES)[:, s0:s1, tiles, :],
            )

        def deal_pair(copy, dealt, raw, t0, s0, s1, tiles=slice(0, PLACES)):
            c0, c1 = s0 // 2, s1 // 2
            copy(
                out=dealt[:].rearrange("p (j c i t) -> p c j i t", j=PLACES, i=2, t=PLACES)[:, c0:c1, tiles, :, t0 : t0 + 2],
                in_=raw[:].rearrange("p t (c i j) -> p c j i t", i=2, j=PLACES)[:, c0:c1, tiles, :, :],
            )

        halves = first, second = slice(0, HALF), slice(HALF, N)

        def entries(cols):
            return offsets[:, cols.start // LIST_ROWS : cols.stop // LIST_ROWS]

        def batch(b):
            return slice(b * P, (b + 1) * P)

        k_pool = [load("k_pool0", planes_of(kT)[:, 0:2, :])]
        offsets = sb.tile([P, N // LIST_ROWS], U16, name="offsets")
        nc.sync.dma_start(offsets[:], offs)
        gate = sb.tile([P, PLACES], F32, name="gate")
        nc.scalar.dma_start(out=gate[:], in_=rw[0].rearrange("(s j) o -> s (j o)", j=PLACES))
        k_pool.append(load("k_pool2", planes_of(kT)[:, 2:PLACES, :]))
        q_raw = load("q_raw", planes_of(qT[0]))
        v_pair = load("v_pool0", planes_of(vT)[:, 0:2, :])
        v_pool = [load("v_pool%d" % t, planes_of(vT)[:, t, :]) for t in (2, LAST)]
        do_raw = [load("do_raw%d" % w, planes_of(doT[0])[:, 2 * w : 2 * w + 2, :]) for w in range(2)]
        qm_raw = [load("qm_raw%d" % w, planes_of(qm[0])[:, 2 * w : 2 * w + 2, :]) for w in range(2)]
        k_planes = [k_pool[t // 2][:, t % 2, :] for t in range(PLACES)]
        v_planes = [v_pair[:, 0, :], v_pair[:, 1, :], v_pool[0][:], v_pool[1][:]]

        windows = [sb.tile([P, T], F32, name="window%d" % j, align_bytes=64) for j in range(PLACES)]
        for window in windows[:LAST]:
            nc.vector.memset(window[:], 0.0)
        nc.gpsimd.memset(windows[LAST][:], 0.0)

        quarter = sb.tile([P, PLACES], F32, name="quarter")
        minus_quarter = sb.tile([P, PLACES], F32, name="minus_quarter")
        nc.scalar.activation(out=quarter[:], in_=gate[:], func=ACT.Copy, scale=0.25)
        nc.scalar.activation(out=minus_quarter[:], in_=gate[:], func=ACT.Copy, scale=-0.25)

        def gather(grouped, rows, planes, t):
            if t < 2:
                nc.vector.tensor_copy(out=place(grouped, slice(0, N), t), in_=planes[t].indirect(offsets[:]))
            else:
                nc.vector.tensor_copy(out=place(grouped, first, t), in_=planes[t].indirect(entries(first)))
                nc.scalar.activation(out=rows[:, t - 2, :], in_=planes[t].indirect(entries(second)), func=ACT.Copy)

        def place_rows(grouped, rows):
            nc.scalar.copy(
                out=grouped[:].rearrange("p (n t) -> p n t", t=PLACES)[:, second, 2:PLACES],
                in_=rows[:].rearrange("p t n -> p n t"),
            )

        low, high = slice(0, 2), slice(2, PLACES)
        k_grouped = sb.tile([P, N * PLACES], BF16, name="k_grouped", align_bytes=64)
        k_rows = sb.tile([P, 2, HALF], F32, name="k_rows", align_bytes=64)
        for t in range(PLACES):
            gather(k_grouped, k_rows, k_planes, t)
        place_rows(k_grouped, k_rows)
        k_mx = mx_tiles("k", N)
        for cols in halves:
            quantize(k_mx, E4M3, cols.start, cols.stop, flat(k_grouped, cols.start, cols.stop))

        q_dealt = sb.tile([P, R * PLACES], BF16, name="q_dealt", align_bytes=64)
        deal(nc.vector.tensor_copy, q_dealt, q_raw, 0, P, low)
        deal(nc.vector.tensor_copy, q_dealt, q_raw, 0, Q_VECTOR, high)
        deal(nc.scalar.copy, q_dealt, q_raw, Q_VECTOR, P, high)
        q_mx = mx_tiles("q", R)
        for tiles in (low, high):
            quantize(q_mx, E4M3, tiles.start * P, tiles.stop * P, flat(q_dealt, tiles.start * P, tiles.stop * P))

        slope = sb.tile([P, PLACES, N], F32, name="slope", align_bytes=64)
        for j in range(PLACES):
            score = psum.tile([P, N], F32, name="score", tag="first")
            product(score[:], q_mx, E4M3, j, k_mx, E4M3, slice(0, N))
            tanh = sb.tile([P, N], F32, name="tanh%d" % j, align_bytes=64)
            nc.scalar.activation(out=tanh[:], in_=score[:], func=ACT.Tanh, scale=0.5)
            square = sb.tile([P, N], F32, name="square%d" % j, align_bytes=64)
            nc.scalar.activation(out=square[:], in_=tanh[:], func=ACT.Square)
            nc.gpsimd.tensor_scalar(
                out=slope[:, j, :],
                in0=square[:],
                scalar1=minus_quarter[:, j : j + 1],
                scalar2=quarter[:, j : j + 1],
                op0=ALU.mult,
                op1=ALU.add,
            )

        v_grouped = sb.tile([P, N * PLACES], BF16, name="v_grouped", align_bytes=64)
        v_second = sb.tile([P, 2, HALF], BF16, name="v_second", align_bytes=64)
        for t in range(PLACES):
            gather(v_grouped, v_second, v_planes, t)
        place_rows(v_grouped, v_second)
        v_mx = [mx_tiles("v0", HALF)]
        quantize(v_mx[0], E4M3, 0, HALF, flat(v_grouped, 0, HALF))

        do_dealt = sb.tile([P, R * PLACES], BF16, name="do_dealt", align_bytes=64)
        do_mx = [mx_tiles("do%d" % j, P) for j in range(PLACES)]
        deal_pair(nc.vector.tensor_copy, do_dealt, do_raw[0], 0, 0, P)
        for tiles, share in zip((low, high), DO_VECTOR):
            deal_pair(nc.vector.tensor_copy, do_dealt, do_raw[1], 2, 0, share, tiles)
            deal_pair(nc.scalar.copy, do_dealt, do_raw[1], 2, share, P, tiles)
        for j in range(PLACES):
            quantize(do_mx[j], E5M2, 0, P, flat(do_dealt, P * j, P * (j + 1)))
        v_mx.append(mx_tiles("v1", HALF, "do_raw1"))
        quantize(v_mx[1], E4M3, 0, HALF, flat(v_grouped, HALF, N))

        dps = []
        for b in range(BATCHES):
            bank = psum.tile([P, PLACES, P], F32, name="dp", tag="second")
            for j in reversed(range(PLACES)) if b else range(PLACES):
                product(bank[:, j, :], do_mx[j], E5M2, 0, v_mx[b // 2], E4M3, batch(b % 2))
            dps.append(bank[:].rearrange("p j (c i) -> p c j i", i=RUN))

        qm_dealt = sb.tile([P, D * PLACES], BF16, name="qm_dealt", align_bytes=64)
        deal_pair(nc.scalar.copy, qm_dealt, qm_raw[0], 0, 0, P, low)
        deal_pair(nc.vector.tensor_copy, qm_dealt, qm_raw[0], 0, 0, QM_VECTOR, high)
        deal_pair(nc.scalar.copy, qm_dealt, qm_raw[0], 0, QM_VECTOR, P, high)
        deal_pair(nc.scalar.copy, qm_dealt, qm_raw[1], 2, 0, P, low)
        deal_pair(nc.scalar.copy, qm_dealt, qm_raw[1], 2, 0, P, high)

        ds_grouped = [sb.tile([P, R], BF16, name="ds_grouped%d" % b, align_bytes=64)[:] for b in range(2)]
        ds_grouped = ds_grouped + [flat(qm_dealt, 0, P), flat(qm_dealt, P, 2 * P)]
        ds_mx = mx_tiles("ds", N)

        def form_ds(b):
            out = ds_grouped[b].rearrange("p (c i j) -> p c j i", i=RUN, j=PLACES)
            nc.vector.tensor_tensor(out=out, in0=dps[b], in1=slope[:, :, batch(b)].rearrange("p j (c i) -> p c j i", i=RUN), op=ALU.mult)

        def quantize_ds(b):
            quantize(ds_mx, E5M2, b * P, (b + 1) * P, ds_grouped[b])

        qm_mx = [mx_tiles("qm%d" % j, P) for j in range(PLACES)]

        def quantize_qm(j):
            quantize(qm_mx[j], E4M3, 0, P, flat(qm_dealt, j * P, (j + 1) * P))

        banks = {}

        def gradient(j, tokens, ring):
            bank = psum.tile([P, tokens.stop - tokens.start], F32, name="acc", tag=ring)
            product(bank[:], qm_mx[j], E4M3, 0, ds_mx, E5M2, tokens)
            banks[j, tokens.start] = bank[:]

        dk = {}
        for j in range(PLACES):
            for h in range(2):
                dk[j, h] = sb.tile([P, HALF], F32, name="dk%d%d" % (j, h), tag="dk%d%d" % (j, h), align_bytes=64)

        def empty(copy, j, tokens):
            h, n0 = divmod(tokens.start, HALF)
            copy(out=dk[j, h][:, n0 : n0 + tokens.stop - tokens.start], in_=banks[j, tokens.start])

        def scalar_scatter(j, h):
            nc.scalar.activation(out=windows[j][:].indirect(entries(halves[h])), in_=dk[j, h][:], func=ACT.Copy)

        def vector_scatter(j, h):
            nc.vector.tensor_copy(out=windows[j][:].indirect(entries(halves[h])), in_=dk[j, h][:])

        def store_plane(j):
            nc.sync.dma_start(out=planes_of(out_0)[:, j, :], in_=windows[j][:])

        form_ds(0)
        form_ds(1)
        quantize_ds(0)
        quantize_qm(0)
        quantize_ds(1)
        quantize_qm(1)
        for b in range(2):
            gradient(0, batch(b), "first")
            empty(nc.scalar.copy, 0, batch(b))
        gradient(1, first, "first")
        empty(nc.scalar.copy, 1, first)
        scalar_scatter(0, 0)
        scalar_scatter(1, 0)
        form_ds(2)
        form_ds(3)
        quantize_ds(2)
        quantize_qm(2)
        quantize_ds(3)
        quantize_qm(LAST)
        gradient(2, first, "first")
        for b in (2, LAST):
            gradient(0, batch(b), "second")
        gradient(1, second, "second")
        gradient(LAST, first, "second")
        gradient(2, second, "first")
        gradient(LAST, second, "first")
        empty(nc.vector.tensor_copy, 0, batch(2))
        empty(nc.vector.tensor_copy, 2, first)
        empty(nc.vector.tensor_copy, 0, batch(LAST))
        vector_scatter(0, 1)
        store_plane(0)
        scalar_scatter(2, 0)
        empty(nc.vector.tensor_copy, 1, second)
        empty(nc.vector.tensor_copy, LAST, first)
        vector_scatter(1, 1)
        store_plane(1)
        scalar_scatter(LAST, 0)
        empty(nc.vector.tensor_copy, 2, second)
        empty(nc.vector.tensor_copy, LAST, second)
        vector_scatter(2, 1)
        store_plane(2)

        split = STRIPS - HELD_STRIPS
        pairs = sb.tile([P, split * P * PLACES], BF16, name="pairs", align_bytes=64)

        def round_plane(copy, j, s0, s1):
            u, e = divmod(j, 2)
            copy(
                out=strip_range(s0, s1).rearrange("p (s u n e) -> p s u n e", u=2, n=P, e=2)[:, :, u, :, e],
                in_=windows[j][:, s0 * P : s1 * P].rearrange("p (s n) -> p s n", n=P),
            )

        def strip_range(s0, s1):
            if s0 < split:
                return pairs[:, s0 * P * PLACES : s1 * P * PLACES]
            return last_pairs[:, (s0 - split) * P * PLACES : (s1 - split) * P * PLACES]

        scalar_from = STRIPS - SCALAR_STRIPS
        for j in range(2):
            round_plane(gpsimd_round, j, 0, GPSIMD_STRIPS)
            round_plane(nc.scalar.copy, j, scalar_from, split)
        scalar_scatter(LAST, 1)
        store_plane(LAST)
        last_pairs = sb.tile([P, HELD_STRIPS * P * PLACES], BF16, name="last_pairs", tag="dk31", align_bytes=64)
        for j in range(2):
            round_plane(nc.vector.tensor_copy, j, GPSIMD_STRIPS, scalar_from)
            round_plane(nc.scalar.copy, j, split, STRIPS)
        round_plane(nc.vector.tensor_copy, 2, 0, 8)
        round_plane(nc.vector.tensor_copy, LAST, 0, 2)
        round_plane(nc.vector.tensor_copy, LAST, 2, 8)
        for j in (2, LAST):
            round_plane(nc.vector.tensor_copy, j, 8, split)
            round_plane(nc.vector.tensor_copy, j, split, STRIPS)

        band = T // SCALE_BANDS
        out_codes = sb.tile([P, T], U32, name="out_codes", align_bytes=64)
        out_scales = sb.tile([P, band], U8, name="out_scales", align_bytes=64)
        words_out = out_1[0].rearrange("p t l -> p (t l)").bitcast(I32)
        out_grouped = [
            sb.tile([P, (s1 - s0) * P * PLACES], BF16, name="out_grouped%d" % s0, align_bytes=64) for s0, s1 in PIECES
        ]

        def weave(c):
            s0, s1 = PIECES[c]
            nc.scalar.copy(
                out=out_grouped[c][:].bitcast(F32).rearrange("p (s n u) -> p s n u", n=P, u=2),
                in_=strip_range(s0, s1).bitcast(F32).rearrange("p (s u n) -> p s n u", u=2, n=P),
            )

        weave(0)
        stored = 0
        for c, (s0, s1) in enumerate(PIECES):
            if c + 1 < len(PIECES):
                weave(c + 1)
            a, b0 = divmod(s0 * P, band)
            nc.vector.quantize_mx(
                out=out_codes[:, s0 * P : s1 * P].bitcast(E4M3),
                scales=out_scales[PLACES * a : P, b0 : b0 + (s1 - s0) * P],
                in_=out_grouped[c][:],
            )
            if s1 in STORE_ENDS:
                nc.sync.dma_start(out=words_out[:, stored : s1 * P], in_=out_codes[:, stored : s1 * P].bitcast(I32))
                stored = s1 * P
        for q in range(P // QUADRANT):
            rows = out_2[0, PLACES * q : PLACES * (q + 1), :].bitcast(I32)
            nc.sync.dma_start(
                out=rows.rearrange("r (a c) -> a r c", a=SCALE_BANDS),
                in_=out_scales[QUADRANT * q : QUADRANT * q + PLACES * SCALE_BANDS, :].bitcast(I32),
            )
